import numpy as np, ml_dtypes
CORES = [23,119,17,113]
N = 4
BF = ml_dtypes.bfloat16
W, C, TS, HOP, SA, SX = 4096, 256, 4, 1, 2, 8
def rise(rng):
    return np.sort(rng.integers(0, W - 15, (N, 8, 16, C)), axis=2) + np.arange(16)[:, None]
def inner(rng):
    m = np.sort(rng.integers(0, W - 15, (N, 8, 14, C)), axis=2) + np.arange(14)[:, None] + 1
    return np.concatenate([np.zeros((N, 8, 1, C), np.int64), m, np.full((N, 8, 1, C), W - 1)], axis=2)
def split(rng):
    k = np.arange(16)[:, None]
    return np.where(k < rng.integers(0, 17, (N, 8, 1, C)), k, W - 16 + k)
def signs(rng):
    return 2 * rng.integers(0, 2, (N, 8, C)) - 1
def pack(x, r, a, s, w):
    return {"xt": np.ascontiguousarray(x).reshape(N, 128, W).astype(np.float32).astype(BF), "rl": np.ascontiguousarray(r).reshape(N, 128, C).astype(np.int32),
            "av": np.ascontiguousarray(a).reshape(N, 128, C).astype(np.float32).astype(BF), "sg": s.astype(np.int32), "wt": np.ascontiguousarray(w).reshape(N, 128, 1).astype(np.int32)}
def setup_inputs(rng):
    return pack(rng.integers(0, 256, (N, 8, 16, W)), rise(rng), rng.integers(0, 256, (N, 8, 16, C)), signs(rng), rng.integers(1, 256, (N, 8, 16)))
def setup_inputs_corners(rng):
    k = np.arange(16)[:, None]; z = int(rng.integers(0, N)); z1 = (z + HOP) % N
    x = rng.integers(0, 256, (N, 8, 16, W)); kind = rng.integers(0, 16, (N, 8, 1, W)); x = np.where(kind == 0, 0, np.where(kind == 1, 255, x)); x[np.arange(N) != z1, ..., ::64] = 0
    zero = 64 * (np.sort(rng.integers(0, W // 64 - 15, (N, 8, 16, C)), axis=2) + k)
    high = 64 * (2 * np.sort(rng.integers(0, W // 128 - 7, (N, 8, 16, C)), axis=2) + k) + 32
    typ = rng.integers(0, 8, (N, 8, 1, C)); typ[..., 8:16] = np.arange(8); typ[:, 2, :, C // 2:C - 1] = 8; typ[..., 5] = 7; typ[..., C - 1] = 7; typ[z] = 7
    r = np.choose(typ, [k, W - 16 + k, rng.integers(0, W - 15, (N, 8, 1, C)) + k, inner(rng), split(rng), rng.integers(0, W - 30, (N, 8, 1, C)) + 2 * k, rise(rng), zero, high])
    ka = rng.integers(0, 5, (N, 8, 1, C)); a = np.where(ka == 0, 0, np.where(ka == 1, 255, rng.integers(0, 256, (N, 8, 16, C))))
    a[z, :, :, 0] = rng.integers(1, 256, (8, 16))
    kw = rng.integers(0, 4, (N, 8, 1)); w = np.where(kw == 0, 1, np.where(kw == 1, 255, rng.integers(1, 256, (N, 8, 16))))
    w[:, 2, 0] = 1; w[:, 2, 1] = 16
    y = x[:, 2, :, 32::64]
    rem = (np.where(np.arange(W // 64) % 2 == 0, 4089, 4087) - np.sum(w[:, 2, 2:, None] * y[:, 2:], axis=1)) & 4095
    y[:, 0] = rem & 15; y[:, 1] = rem >> 4
    return pack(x, r, a, signs(rng), w)
def setup_inputs_ends(rng):
    k = np.arange(16)[:, None]; S = W >> 4
    w = 1 + 254 * rng.integers(0, 2, (N, 8, 16)); w[..., 0] = 1; w[..., 15] = 1; w[..., 7] = 255; w[:, 3] = 255; w[:, 5] = 1
    top = np.zeros((16, 1), np.int64); top[[0, 7, 15]] = 1
    kind = rng.integers(0, 6, (N, 8, 1, W)); x = rng.integers(0, 2, (N, 8, 16, W))
    x = np.where(kind == 0, 0, np.where(kind == 1, 1, np.where(kind == 2, top, x)))
    x[..., ::S] = top
    m = rng.random((N, 8, 16)) < 0.4; m[:, ::2] = False; m[..., 15] = True; m[:, 7, rng.integers(0, 4)] = True
    x[..., S - 1::S] = np.where(m[:, :, None, :], 1, x[..., S - 1::S]); x[:, :, 3, S - 1::S] = m
    ka = rng.integers(0, 4, (N, 8, 1, C)); ka[..., [0, 2, C - 2, C - 1]] = 0; ka[..., [1, C - 3]] = 1
    a = np.where(ka == 0, 0, np.where(ka == 1, 1, rng.integers(0, 2, (N, 8, 16, C))))
    typ = np.array([0, 0, 0, 0, 0, 0, 0, 1, 1, 2])[rng.integers(0, 10, (N, 8, 1, C))]; typ[..., [0, 1, 2, C - 3, C - 2, C - 1]] = 2
    return pack(255 * x, np.choose(typ, [split(rng), inner(rng), k * S]), 255 * a, signs(rng), w)
def setup_inputs_shared(rng):
    r = rise(rng); r = np.take_along_axis(r, rng.integers(0, 4, (N, 8, 1, C)), 3)
    x = rng.integers(0, 256, (N, 8, 16, W)); a = rng.integers(0, 256, (N, 8, 16, C)); s = signs(rng)
    r[:, 6] = r[:, 6, :, :1].copy(); s[:, 6] = s[:, 6, :1].copy()
    b = rng.integers(112, 144, (N, 16, 1)); far = rng.integers(0, 64, (N, 16, W)) + 192 * rng.integers(0, 2, (N, 16, W))
    for q in range(N): far[q][:, r[q, 6, :, 0]] = b[q] + rng.integers(-2, 3, (16, 16))
    x[:, 6] = far; a[:, 6] = b + rng.integers(-2, 3, (N, 16, C))
    return pack(x, r, a, s, rng.integers(1, 256, (N, 8, 16)))
def setup_inputs_spread(rng):
    x = np.minimum(np.exp2(9 * rng.random((N, 8, 1, W))) * rng.random((N, 8, 16, W)), 255).astype(np.int64)
    a = np.minimum(np.exp2(9 * rng.random((N, 8, 1, C))) * rng.random((N, 8, 16, C)), 255).astype(np.int64)
    r = np.sort((rng.random((N, 8, 16, C)) ** 3 * (W - 15)).astype(np.int64), axis=2) + np.arange(16)[:, None]
    return pack(x, r, a, signs(rng), np.clip(np.exp2(8 * rng.random((N, 8, 16))).astype(np.int64), 1, 255))
def setup_inputs_ties(rng):
    x = 100 + rng.integers(0, 3, (N, 8, 16, W)); a = 100 + rng.integers(0, 3, (N, 8, 16, C)) + rng.integers(-1, 2, (N, 8, 1, C))
    x[:, 6:] = 100 + SX * rng.integers(-1, 2, (N, 2, 16, W)); a[:, 6:] = 100 + SA * rng.integers(-1, 2, (N, 2, 16, C))
    return pack(x, rise(rng), a, signs(rng), rng.integers(1, 256, (N, 8, 16)))
def check_inputs(d):
    bad = []
    for k, lo, hi in (("xt", 0, 255), ("rl", 0, W - 1), ("av", 0, 255), ("sg", -1, 1), ("wt", 1, 255)):
        v = np.asarray(d[k]).astype(np.float64)
        if not np.all((v >= lo) & (v <= hi)): bad.append("range of " + k)
        elif not np.all(v == np.floor(v)): bad.append("whole numbers of " + k)
    if np.any(np.asarray(d["sg"]) == 0): bad.append("signs of sg")
    r = np.asarray(d["rl"]).astype(np.int64).reshape(N, 8, 16, C)
    if not np.all(r[:, :, 1:] > r[:, :, :-1]): bad.append("rl not rising")
    return bad
def pick(x, ix):
    return np.take_along_axis(x, ix.reshape(8, 1, 16 * C), 2).reshape(8, 16, 16, C)
def reference(xt, rl, av, sg, wt):
    x = xt.astype(np.float32).astype(np.int64).reshape(N, 8, 16, W); R = rl.astype(np.int64).reshape(N, 8, 16, C)
    A = av.astype(np.float32).astype(np.int64).reshape(N, 8, 16, C); sig = sg.astype(np.int64).reshape(N, 8, C)
    w = wt.astype(np.int64).reshape(N, 8, 16, 1, 1); cnt = np.zeros((N, C), np.int64); kk = np.arange(16)[None, :, None]
    for t in range(TS):
        for r in range(N):
            p = (r + HOP * t) % N; X = x[p]; L = R[r].copy(); a = A[r].copy(); s0 = sig[r].copy()
            u = np.sum(w[p] * pick(X, L), axis=1) & 4095
            h = ((u * np.roll(u, -1, axis=1) >> 5) + u + cnt[r]) & 255
            st = (np.concatenate([L[:, 1:], L[:, :1] + W], axis=1) - L) * h >> 8
            q = (L + st) & (W - 1)
            Xq = pick(X, q); E = np.where(st == 0, -1, np.sum(np.abs(Xq - a[:, :, None, :]), axis=1))
            k = np.argmax(E, axis=1); e = np.max(E, axis=1)
            qb = np.take_along_axis(q, k[:, None, :], 1)[:, 0]; xq = np.take_along_axis(Xq, k[:, None, None, :], 2)[:, :, 0]
            s = np.where(np.sum(xq > a, axis=1) >= 8, 1, -1)
            out = k == 15; first = out & (qb < L[:, 0])
            shift = out & (s != np.where(first, s0, -s0))
            place = np.where(out, np.where(first != shift, 0, 15), k + (s != s0 * (1 - 2 * (k & 1))))
            col = np.take_along_axis(L, place[:, None, :], 1)[:, 0]; xl = np.take_along_axis(X, col[:, None, :], 2)
            go = e > np.sum(np.abs(xl - a), axis=1)
            qn = qb[:, None, :]; new = np.where(kk == place[:, None, :], qn, L)
            new = np.where((shift & first)[:, None, :], np.concatenate([qn, L[:, :15]], axis=1), new)
            new = np.where((shift & ~first)[:, None, :], np.concatenate([L[:, 1:], qn], axis=1), new)
            R[r] = np.where(go[:, None, :], new, L); sig[r] = np.where(go & shift, -s0, s0); cnt[r] = np.sum(go, axis=0)
            A[r] = np.where(go[:, None, :], a + np.clip(xq - a, -SA, SA), a)
            back = xl + np.clip(a - xl, -SX, SX)
            for g in range(8):
                c = np.nonzero(go[g])[0]; cols, i = np.unique(col[g, c], return_index=True)
                x[p, g][:, cols] = back[g][:, c[i]]
    return {"yr": R.reshape(N, 128, C).astype(np.float32), "ya": A.reshape(N, 128, C).astype(np.float32).astype(BF),
            "ys": sig.astype(np.float32), "yx": x.reshape(N, 128, W).astype(np.float32).astype(BF)}

@@ -1,0 +1,603 @@
+from concourse.mybir import AluOpType, ActivationFunctionType
+
+N, W, C, TS = 4, 4096, 256, 4
+WX = W + 16
+AWW = 400
+CFG = {"REF_DVE": ((4, 4), (0, 2)), "MPRE": (1, 1), "PROBE_ACT": (4, 8), "CREP": "act", "WIN": 100.0, "QACT": (2, 2), "LACT": (2, 2),
+       "BIAS": 2000.0, "NPE": False, "WAW": True}
+ORDER = {_p.split(":")[0]: int(_p.split(":")[1]) for _p in (
+    "G.1024a:-28 mk.0a:2 sm.176a:-20 M3.0a:-12 sm.48a:-20 sm.160a:-10 Rf.144a:15 su.56a:-13 Dd.3072a:11 msk.144a:-25 Dd.1024a:38 "
+    "Dd.1792a:43 SR.144a:-13 K3.16a:-52 Dd.1280a:38 K.128a:20 K3.0a:55 AB.1536a:23 G.1792a:23 si.0a:4 vo.128a:-18 gr.0a:-10 sm.168a:-5 "
+    "Dd.512a:-45 Dd.2560a:10 Dl.0a:-15 sm.192a:-20 Dd.3840a:13 G.2560a:5 eq.128a:20 sm.0a:-40 su.16a:10 AB.2560a:-27 pr.0b:-10 "
+    "AW.144a:-20 msk.0a:-23 sm.64a:5 Dd.1536a:20 QU.128a:-10 Dd.3584a:20").split()}
+
+SCRATCH = {}
+for _n, _w, _d in (
+        ("X", WX, "bfloat16"), ("IOTA", WX, "float32"), ("G", W, "bfloat16"), ("Dd", W, "bfloat16"), ("AB", W, "bfloat16"),
+        ("L", 256, "int32"), ("L1", 256, "float32"), ("L2", 256, "float32"), ("L3", 288, "float32"), ("L4", 288, "float32"),
+        ("L5", 288, "float32"), ("L6", 288, "float32"), ("ng", 16, "float32"),
+        ("wti", 8, "int32"), ("wtf", 8, "float32"), ("sgi", 256, "int32"), ("sgb", 256, "bfloat16"),
+        ("COL", 144, "float32"), ("COLX", 256, "float32"), ("COLG", 128, "float32"), ("PAR", 144, "bfloat16"),
+        ("pi", 8, "int32"), ("pv", 16, "int32"), ("pf", 16, "float32"), ("ci", 128, "int32"), ("cj", 128, "int32"),
+        ("cb", 8, "bfloat16"), ("cu", 160, "uint16"),
+        ("I", 128, "bfloat16"), ("NI", 128, "bfloat16"), ("IA", 128, "bfloat16"), ("NIA", 128, "bfloat16"), ("IB", 128, "bfloat16"),
+        ("IC", 128, "bfloat16"), ("If", 128, "float32"), ("NIf", 128, "float32"), ("I4", 128, "float32"),
+        ("Z", 272, "bfloat16"), ("ONE", 128, "bfloat16"), ("BW", 144, "bfloat16"), ("NBW", 144, "bfloat16"), ("WU", 144, "bfloat16"),
+        ("WE", 144, "bfloat16"), ("SX", 128, "bfloat16"), ("BO", 128, "bfloat16"), ("DG", 256, "bfloat16"), ("TRI", 2048, "bfloat16"),
+        ("trs", 16, "float32"),
+        ("Rf", 288, "float32"), ("wr", 256, "bfloat16"), ("si", 256, "int32"), ("u", 288, "int32"), ("pr", 256, "int32"),
+        ("p16", 256, "int32"), ("tt", 256, "int32"), ("h", 256, "int32"), ("dh", 256, "float32"), ("z", 256, "int32"),
+        ("q", 256, "int32"), ("QU", 256, "uint16"), ("vo", 256, "bfloat16"), ("K", 256, "float32"), ("K1", 128, "float32"),
+        ("K2", 64, "float32"), ("K3", 32, "float32"), ("KV", 32, "int32"), ("OF", 64, "int32"), ("oh", 256, "float32"),
+        ("mk", 256, "float32"), ("M1", 128, "float32"), ("M2", 64, "float32"), ("M3", 32, "float32"),
+        ("sm", 256, "float32"), ("su", 96, "uint16"), ("Dq", 256, "bfloat16"), ("gt", 256, "bfloat16"), ("Dl", 256, "bfloat16"),
+        ("ABl", 256, "bfloat16"), ("cl", 256, "bfloat16"), ("tb", 256, "bfloat16"), ("cq", 256, "bfloat16"),
+        ("msk", 288, "float32"), ("md", 288, "float32"), ("crep", 256, "float32"), ("eq", 256, "bfloat16"),
+        ("F0", 288, "float32"), ("F1", 256, "float32"), ("F2", 256, "float32"), ("F3", 256, "float32"), ("F4", 256, "float32"),
+        ("F5", 256, "float32"), ("F6", 256, "float32"), ("F7", 256, "int32"), ("F8", 256, "float32"),
+        ("r2", 256, "bfloat16"), ("r3", 256, "bfloat16"), ("gr", 256, "bfloat16"), ("fb", 256, "bfloat16"), ("ys2", 256, "float32")):
+    SCRATCH[_n] = ("sbuf", [128, _w], _d)
+for _t in range(TS + 1):
+    SCRATCH["RU%d" % _t] = ("sbuf", [128, 288], "uint16")
+    SCRATCH["AW%d" % _t] = ("sbuf", [128, 2 * AWW], "bfloat16")
+for _t in range(TS):
+    SCRATCH["SR%d" % _t] = ("sbuf", [128, 288], "uint16")
+    SCRATCH["SA%d" % _t] = ("sbuf", [128, 288], "bfloat16")
+for _b in ("PS0", "PS1", "PE0", "PE1", "PR0", "PR1", "PV0", "PV1"):
+    SCRATCH[_b] = ("psum", [128, 512], "float32")
+
+SEMAPHORES = (["c_dve", "c_act", "c_pe", "c_pool", "sent", "d_x", "d_l", "d_a", "d_w", "d_s", "o_x", "o_r", "o_r2", "o_a", "o_s"]
+              + ["a%s%d_%d" % (k, t, b) for k in "ra" for t in range(TS) for b in range(2)])
+
+CYC, PCYC, GC, SC = 0.95, 0.5, 1.56, 3.8
+LAT_SAME, LAT_X, LAT_R = 60.0, 110.0, 3200.0
+OP = AluOpType
+AF = ActivationFunctionType
+
+
+def arrange(ops):
+    n = len(ops)
+    pri = [o["pri"] + 100.0 * ORDER.get(o.get("key"), 0) for o in ops]
+    left = [len(o["deps"]) for o in ops]
+    rdy = [0.0] * n
+    free = {"arr": 0.0, "dve": 0.0, "act": 0.0, "pe": 0.0, "pool": 0.0, "sp": 0.0}
+    ready = [k for k in range(n) if left[k] == 0]
+    order = []
+    while ready:
+        st = {k: max(rdy[k], free[ops[k]["eng"]]) for k in ready}
+        k0 = min(ready, key=lambda j: (st[j], -pri[j], j))
+        lim = st[k0] + min(CFG["WIN"], 0.6 * ops[k0]["cost"])
+        k = max([j for j in ready if ops[j]["eng"] == ops[k0]["eng"] and st[j] <= lim], key=lambda j: (pri[j], -j))
+        ready.remove(k)
+        o = ops[k]
+        if o["eng"] != "arr":
+            free[o["eng"]] = st[k] + o["cost"]
+        o["t0"] = st[k]
+        order.append(k)
+        for (s, e) in o["succ"]:
+            rdy[s] = max(rdy[s], st[k] + o["cost"] + e)
+            left[s] -= 1
+            if left[s] == 0:
+                ready.append(s)
+    return order
+
+
+def rank_program(g, core, T, topo):
+    rank = T.rank_of(core)
+    if rank is None:
+        return
+    nxt = T.cores[(rank + 1) % N]
+    rid, pid, _ = topo.addr(nxt)
+    engs = topo.engines(core, nxt)
+    nen = len(engs)
+    emask = topo.mask(core, nxt)
+    ops = []
+    hist = {}
+    Q = {"dve": g.vector, "act": g.scalar, "pe": g.tensor, "pool": g, "sp": g.sync}
+
+    def V(name, a=None, b=None, s=1):
+        w = SCRATCH[name][1][1]
+        a = 0 if a is None else a
+        b = w if b is None else b
+        ap = T[name][:, a:b] if s == 1 else T[name][:, a:b:s]
+        return (ap, [(name, a, b)], len(range(a, b, s)), SCRATCH[name][2], SCRATCH[name][0])
+
+    def IND(win, off):
+        return (win[0].indirect(off[0]), win[1] + off[1], 16 * off[2], win[3], "ind")
+
+    def add(eng, fn, reads, writes, cost, sem=None, cnt=0, lat=0.0, after=()):
+        k = len(ops)
+        deps = set(after)
+        soft = set()
+        for regs, isw in ((reads, False), (writes, True)):
+            for (nm, a, b) in regs:
+                ps = SCRATCH[nm][0] == "psum"
+                for (j, e2, a2, b2, w2) in hist.setdefault(nm, []):
+                    if ps and (e2 != eng or eng == "pe"):
+                        deps.add(j)
+                    elif (isw or w2) and a < b2 and a2 < b:
+                        if isw and e2 == eng and ops[j]["sem"] is None and sem is None and not CFG["WAW"]:
+                            soft.add(j)
+                        else:
+                            deps.add(j)
+        for regs, isw in ((reads, False), (writes, True)):
+            for (nm, a, b) in regs:
+                hist[nm].append((k, eng, a, b, isw))
+        deps.discard(k)
+        soft -= deps
+        deps |= soft
+        ops.append({"soft": soft, "w": writes[0] if writes else ("-", 0, 0), "eng": eng, "fn": fn, "deps": deps, "cost": cost, "sem": sem, "cnt": cnt, "lat": lat})
+        return k
+
+    def two(*vs):
+        return all(v[3] in ("bfloat16", "uint16") for v in vs)
+
+    def vcost(n, f):
+        if f in (GC, SC):
+            return 50.0 + n * f * CYC
+        return 10.0 + max(64.0, n * f) * CYC
+
+    def cp(o, i):
+        f = GC if i[4] == "ind" else (0.5 if two(o, i) else 1.0)
+        return add("dve", lambda: g.vector.tensor_copy(o[0], i[0]), i[1], o[1], vcost(o[2], f))
+
+    def tt(o, a, b, op):
+        if o[4] == "ind":
+            return add("dve", lambda: g.vector.tensor_tensor(o[0], a[0], b[0], op), a[1] + b[1] + o[1][1:], o[1][:1], vcost(o[2], SC))
+        f = GC if a[4] == "ind" else (1.0 if "psum" in (a[4], b[4]) else 2.0)
+        return add("dve", lambda: g.vector.tensor_tensor(o[0], a[0], b[0], op), a[1] + b[1], o[1], vcost(o[2], f))
+
+    def ts(o, a, s1, op0, s2=None, op1=None):
+        rd = list(a[1])
+        x1, x2 = s1, s2
+        if isinstance(s1, tuple):
+            rd += s1[1]
+            x1 = s1[0]
+        if isinstance(s2, tuple):
+            rd += s2[1]
+            x2 = s2[0]
+        f = GC if a[4] == "ind" else (0.5 if two(o, a) else 1.0)
+        if op1 is None:
+            return add("dve", lambda: g.vector.tensor_scalar(o[0], a[0], x1, None, op0), rd, o[1], vcost(o[2], f))
+        return add("dve", lambda: g.vector.tensor_scalar(o[0], a[0], x1, x2, op0, op1), rd, o[1], vcost(o[2], f))
+
+    def ms(o, val):
+        return add("dve", lambda: g.vector.memset(o[0], val), [], o[1], vcost(o[2], 1.0))
+
+    def act(o, i, fn, bias=None, scale=1.0):
+        f = GC if i[4] == "ind" else 1.0
+        if bias is None:
+            return add("act", lambda: g.scalar.activation(o[0], i[0], fn), i[1], o[1], 65.0 + o[2] * f * CYC)
+        return add("act", lambda: g.scalar.activation(o[0], i[0], fn, bias=bias[0], scale=scale), i[1] + bias[1], o[1], 65.0 + o[2] * f * CYC)
+
+    def mm(items):
+        rd, wr, cost = [], [], 0.0
+        for (o, l, r, st, sp) in items:
+            rd += l[1] + r[1]
+            wr += o[1]
+            cost += 4.0 + max(64, r[2]) * PCYC * (4 if r[3] == "float32" else 1)
+
+        def fn():
+            last = None
+            for (o, l, r, st, sp) in items:
+                last = g.tensor.matmul(o[0], l[0], r[0], st, sp)
+            return last
+        return add("pe", fn, rd, wr, cost)
+
+    def fold(o, wname, src, a, n, first, last):
+        its = []
+        for x in range(16):
+            l = V("TRI", 128 * x, 128 * x + 128) if wname == "TRI" else V(wname, 15 - x, 143 - x)
+            its.append((o, l, V(src, a + x, a + 16 * n, 16), first and x == 0, last and x == 15))
+        return mm(its)
+
+    def iota(o, pat, base, cm, after=()):
+        if o[3] == "int32":
+            return add("pool", lambda: g.iota(o[0], pat, base, cm), [], o[1], 130.0 + 2 * o[2] * CYC, after=after)
+        return add("pool", lambda: g.iota(o[0], pat, base, cm, allow_small_or_imprecise_dtypes=True), [], o[1], 130.0 + 2 * o[2] * CYC, after=after)
+
+    def dma(eng, pairs, reads, writes, sem, lat):
+        def fn():
+            for (o, i) in pairs:
+                Q[eng].dma_start(o, i).then_inc(T.sem[sem], 16)
+            return None
+        return add(eng, fn, reads, writes, 60.0 * len(pairs), sem, 16 * len(pairs), lat)
+
+    dma("sp", [(T.X[:, 0:W], T.xt[:])], [], [("X", 0, W)], "d_x", 6500.0)
+    pieces = [(gh, b, gl) for gh in range(4) for b in range(2) for gl in range(2)]
+    dma("act", [(T.L[32 * gh + 16 * b:32 * gh + 16 * b + 16, 128 * gl:128 * gl + 128],
+                 T.rl[32 * gh + 16 * gl:32 * gh + 16 * gl + 16, 128 * b:128 * b + 128]) for (gh, b, gl) in pieces],
+        [], [("L", 0, 256)], "d_l", 2500.0)
+    ms(V("sgi"), 0)
+    dma("sp", [(T.sgi[0:128:16, :], T.sg[:])], [], [("sgi", 0, 256)], "d_s", 2500.0)
+    dma("sp", [(T.wti[:, 0:1], T.wt[:])], [], [("wti", 0, 8)], "d_w", 2500.0)
+    dma("sp", [(T.AW0[:, AWW * b + 16:AWW * b + 144], T.av[:, 128 * b:128 * b + 128]) for b in range(2)], [],
+        [("AW0", 16, 144), ("AW0", AWW + 16, AWW + 144)], "d_a", 2500.0)
+
+    io = [iota(V("pi", 0, 1), [[0, 1]], 0, 1),
+          iota(V("COL"), [[1, 144]], 0, 0),
+          iota(V("ci", 0, 16), [[16, 8], [128, 2]], 0, 0),
+          iota(V("ci", 16, 34), [[0, 2], [2, 9]], 0, 0),
+          iota(V("ci", 40, 58), [[16, 2], [0, 9]], 0, 0),
+          iota(V("COLX"), [[0, 16], [1, 16]], 0, 0),
+          iota(V("ci", 64, 80), [[8, 16]], 0, 0),
+          iota(V("ci", 80, 96), [[16, 2], [32, 8]], 0, 0),
+          iota(V("COLG"), [[16, 8], [0, 16]], 0, 0),
+          iota(V("PAR"), [[0, 9], [1, 2], [0, 8]], 0, 0),
+          iota(V("ci", 112, 128), [[16, 8], [128, 2]], 0, 0)]
+    iota(V("IOTA"), [[1, WX]], 0, 0, after=io)
+    ms(V("X", W, WX), 0.0)
+    ms(V("ONE"), 1.0)
+    P = V("pi", 0, 1)
+    ts(V("pv", 0, 1), P, 15, OP.bitwise_and)
+    ts(V("pv", 1, 2), P, 112, OP.bitwise_and)
+    ts(V("pv", 2, 3), P, 7, OP.bitwise_and)
+    ts(V("pv", 3, 4), P, 3, OP.logical_shift_right, 1, OP.bitwise_and)
+    ts(V("pv", 4, 5), P, 1, OP.bitwise_and)
+    ts(V("pv", 5, 6), P, 1, OP.logical_shift_right, 7, OP.bitwise_and)
+    cp(V("pf", 0, 6), V("pv", 0, 6))
+    cp(V("pf", 6, 7), P)
+    xf, g16, y3, k0, pff = V("pf", 0, 1), V("pf", 1, 2), V("pf", 2, 3), V("pf", 3, 4), V("pf", 6, 7)
+    ts(V("pf", 7, 8), g16, 15.0, OP.add)
+    ts(V("pf", 8, 9), xf, float(W), OP.add)
+    ts(V("pf", 9, 10), xf, -1.0, OP.mult, -float(W), OP.add)
+    DUM, NDUM = V("pf", 8, 9), V("pf", 9, 10)
+    ts(V("pf", 10, 11), y3, 32.0, OP.mult)
+    ms(V("pf", 12, 13), 4088.0)
+    B4088 = V("pf", 12, 13)
+    ms(V("pf", 14, 15), -0.5)
+    ms(V("pf", 15, 16), -2.0)
+    ms(V("wtf", 4, 5), -8.0)
+    CMH, CM2, CM8 = V("pf", 14, 15), V("pf", 15, 16), V("wtf", 4, 5)
+    ts(V("cu", 0, 16), V("ci", 0, 16), xf, OP.add)
+    for j, one in ((0, 0.0), (1, 1.0)):
+        a = 24 * j
+        ts(V("cj", a, a + 18), V("ci", 16, 34), k0, OP.add, one, OP.add)
+        ts(V("cj", 48 + a, 66 + a), V("cj", a, a + 18), 15, OP.bitwise_and)
+        tt(V("cj", a, a + 18), V("cj", 48 + a, 66 + a), V("ci", 40, 58), OP.add)
+        ts(V("cu", 16 + 18 * j, 34 + 18 * j), V("cj", a, a + 18), V("pf", 10, 11), OP.add)
+    ts(V("cu", 52, 70), V("ci", 40, 58), 0.5, OP.mult, y3, OP.add)
+    ts(V("cu", 70, 86), V("ci", 112, 128), xf, OP.add)
+    ts(V("cu", 86, 102), V("ci", 80, 96), xf, OP.add)
+    ts(V("cu", 102, 118), V("ci", 64, 80), 0.125, OP.mult)
+    ts(V("cu", 118, 128), V("ci", 64, 74), 0.0, OP.mult, y3, OP.add)
+    ts(V("cu", 128, 136), V("ci", 64, 72), 0.125, OP.mult)
+    P1, P2, P2b, BN, P3, P4, P5 = (V("cu", 0, 16), V("cu", 16, 34), V("cu", 34, 52), V("cu", 52, 70), V("cu", 70, 86),
+                                   V("cu", 86, 102), V("cu", 102, 118))
+    BX, BX9, BY = V("cu", 118, 126), V("cu", 118, 127), V("cu", 128, 136)
+    ts(V("pf", 13, 14), xf, 16.0, OP.add)
+    ts(V("cb"), V("ci", 64, 72), 2.0, OP.mult, V("pf", 13, 14), OP.add)
+    C128 = V("COL", 0, 128)
+    ts(V("BW"), V("COL"), V("pf", 7, 8), OP.is_equal)
+    cp(V("wtf", 0, 1), V("wti", 0, 1))
+    ts(V("WU"), V("BW"), V("wtf", 0, 1), OP.mult, 16.0, OP.mult)
+    for nm, f in (("If", 1.0), ("NIf", -1.0), ("I4", 4096.0), ("I", 1.0), ("NI", -1.0), ("IA", 2048.0), ("NIA", -2048.0),
+                  ("IB", 8388608.0), ("IC", 256.0)):
+        ts(V(nm), C128, pff, OP.is_equal, f, OP.mult)
+    ts(V("WE"), V("BW"), -4096.0, OP.mult)
+    ts(V("NBW"), V("BW"), -1.0, OP.mult)
+    ts(V("SX"), V("COLX", 0, 128), xf, OP.is_equal, 16.0, OP.mult)
+    ts(V("trs"), V("COL", 0, 16), xf, OP.is_gt, 8192.0, OP.mult)
+    for x in range(16):
+        ts(V("TRI", 128 * x, 128 * x + 128), V("BW", 15 - x, 143 - x), V("trs", x, x + 1), OP.mult)
+    ts(V("BO"), V("COLG"), g16, OP.is_equal)
+    ts(V("DG"), V("COLX"), xf, OP.is_equal)
+    ts(V("PAR"), V("PAR"), 0.25, OP.mult)
+    for b in range(2):
+        ms(V("AW0", AWW * b, AWW * b + 16), 0.0)
+        for t in range(TS):
+            ms(V("SA%d" % t, 144 * b + 8, 144 * b + 16), 0.0)
+
+    cp(V("L1"), IND(V("L"), P1))
+    add("dve", lambda: g.vector.transpose(T.L2[:], T.L1[:]), [("L1", 0, 256)], [("L2", 0, 256)], vcost(256, 1.0))
+    cp(V("L3"), IND(V("L2"), P2))
+    tt(V("L4"), IND(V("L2"), P2b), V("L3"), OP.subtract)
+    ts(V("sgb"), V("sgi"), 0.0, OP.is_lt)
+    fold(V("PE0", 0, 16), "BW", "sgb", 0, 16, True, True)
+    cp(V("ng"), V("PE0", 0, 16))
+    tt(V("L5"), IND(V("ng"), BN), V("L4"), OP.mult)
+    tt(V("L6"), V("L5"), V("L3"), OP.add)
+    cp(V("RU0"), V("L6"))
+
+    XW = V("X")
+    nv = [0]
+    lead = []
+    steps = []
+    for t in range(TS):
+        RU, AW, SR, SA = "RU%d" % t, "AW%d" % t, "SR%d" % t, "SA%d" % t
+        sends = []
+        step0 = len(ops)
+        for hi, b in enumerate((1, 0)):
+            def H(nm, a=0, e=128, s=1, b=b):
+                w = SCRATCH[nm][1][1] // 2
+                return V(nm, w * b + a, w * b + e, s)
+
+            def S(j, b=b):
+                return V("sm", 128 * b + 8 * j, 128 * b + 8 * j + 8)
+            first = len(ops)
+            PS, PE, PR = "PS%d" % b, "PE%d" % b, "PR%d" % b
+            A, A2 = H(AW, 16, 144), H(AW, 16, 272)
+            PD = V(PR, 144, 272)
+            cp(H("Rf", 0, 144), H(RU, 0, 144))
+            act(H(AW, 144, 272), A, AF.Copy)
+            mm([(V(PR, 272, 400), V("If"), H("Rf", 8, 136), True, False), (V(PR, 272, 400), V("NIf"), H("Rf"), False, True)])
+            act(H("wr"), V(PR, 272, 400), AF.Sign)
+            mm([(PD, V("If"), H("Rf", 8, 136), True, False), (PD, V("NIf"), H("Rf"), False, False),
+                (PD, V("NIA"), H("wr"), False, False), (PD, V("IA"), V("ONE"), False, True),
+                (V(PR, 0, 136), V("I4"), H("Rf", 0, 136), True, True)])
+            rd = CFG["REF_DVE"][hi]
+            for a0, r in zip((0, 8), rd):
+                cuts = sorted(set([a0, a0 + 8 - r, a0 + 8] + ([a0 + 4] if r in (0, 8) else [])))
+                for a, e in zip(cuts[:-1], cuts[1:]):
+                    src = IND(XW, H(RU, 8 * a, 8 * e))
+                    if a >= a0 + 8 - r:
+                        cp(H("G", 128 * a, 128 * e), src)
+                    else:
+                        act(H("G", 128 * a, 128 * e), src, AF.Copy)
+            SN = V(PS, 0, 128)
+            npe = t > 0 and CFG["NPE"]
+            if t > 0 and not npe:
+                act(H("gr"), IND(H(AW, 0, 16), BX), AF.Copy)
+                mm([(V(PE, 256, 384), V("SX"), H("gr"), True, True)])
+            for a in (0, 8):
+                fold(V(PS, 8 * a, 8 * a + 64), "WU", "G", 2048 * b + 128 * a, 64, True, True)
+                if npe:
+                    fold(V(PE, 256 + 8 * a, 320 + 8 * a), "WU", "G", 2048 * b + 128 * a, 64, True, False)
+                    if a == 0:
+                        act(H("gr"), IND(H(AW, 0, 16), BX), AF.Copy)
+                    mm([(V(PE, 256 + 8 * a, 320 + 8 * a), V("SX"), H("gr", 0, 64), False, True)])
+                    SN = V(PE, 256, 384)
+            cp(H("si"), V(PS, 0, 128))
+            ts(H("u"), H("si"), 4, OP.logical_shift_right, 4095, OP.bitwise_and)
+            ts(H("u", 128, 136), H("si", 0, 8), 4, OP.logical_shift_right, 4095, OP.bitwise_and)
+            tt(H("pr"), H("u"), H("u", 8, 136), OP.mult)
+            ts(H("p16"), H("pr"), 1, OP.logical_shift_right, 4080, OP.bitwise_and)
+            tt(H("tt"), H("p16"), SN, OP.add)
+            if t > 0 and not npe:
+                tt(H("pr"), H("tt"), V(PE, 256, 384), OP.add)
+                ts(H("h"), H("pr"), 4080, OP.bitwise_and)
+            else:
+                ts(H("h"), H("tt"), 4080, OP.bitwise_and)
+            tt(H("dh"), H("h"), PD, OP.mult)
+            tt(H("z"), H("dh"), V(PR, 0, 128), OP.add)
+            ts(H("q"), H("z"), 12, OP.logical_shift_right, 4095, OP.bitwise_and)
+            cp(H("QU"), H("q"))
+            act(H("vo"), H("dh"), AF.Sign, B4088, -1.0)
+            tt(V(PS, 128, 256), H("q"), V(PR, 8, 136), OP.add)
+            mm([(V(PE, 0, 128), V("IB"), H("vo"), True, False), (V(PE, 0, 128), V("IB"), V("ONE"), False, False)])
+            pa = CFG["PROBE_ACT"][hi]
+            for a in range(0, 16, 4):
+                c0, c1 = 128 * a, 128 * a + 512
+                if a < pa:
+                    pv = "PV%d" % (nv[0] % 2)
+                    nv[0] += 1
+                    act(H("Dd", c0, c1), IND(XW, H("QU", 8 * a, 8 * a + 32)), AF.Copy)
+                    mm([(V(pv), V("I"), H("Dd", c0, c1), True, False), (V(pv, 0, 256), V("NI"), A2, False, False),
+                        (V(pv, 256, 512), V("NI"), A2, False, True)])
+                    act(H("AB", c0, c1), V(pv), AF.Abs)
+                else:
+                    for m in (a, a + 2):
+                        tt(H("Dd", 128 * m, 128 * m + 256), IND(XW, H("QU", 8 * m, 8 * m + 16)), A2, OP.subtract)
+                        if a == 12:
+                            act(H("AB", 128 * m, 128 * m + 256), H("Dd", 128 * m, 128 * m + 256), AF.Abs)
+                    if a < 12:
+                        act(H("AB", c0, c1), H("Dd", c0, c1), AF.Abs)
+                if a % 8 == 4:
+                    fold(V(PE, 8 * (a - 4), 8 * (a + 4)), "WE", "AB", 2048 * b + 128 * (a - 4), 64, False, a == 12)
+            tt(H("K"), H("Rf"), V(PE, 0, 128), OP.add)
+            tt(H("K1", 0, 64), H("K", 0, 64), H("K", 64, 128), OP.min)
+            tt(H("K2", 0, 32), H("K1", 0, 32), H("K1", 32, 64), OP.min)
+            tt(H("K3", 0, 16), H("K2", 0, 16), H("K2", 16, 32), OP.min)
+            tt(H("KV", 0, 8), H("K3", 0, 8), H("K3", 8, 16), OP.min)
+            tt(H("oh"), IND(H("KV", 0, 8), BX), H("K"), OP.is_equal)
+            tt(H("mk"), H("oh"), V(PS, 128, 256), OP.mult)
+            tt(H("M1", 0, 64), H("mk", 0, 64), H("mk", 64, 128), OP.max)
+            tt(H("M2", 0, 32), H("M1", 0, 32), H("M1", 32, 64), OP.max)
+            tt(H("M3", 0, 16), H("M2", 0, 16), H("M2", 16, 32), OP.max)
+            tt(H("KV", 8, 16), H("M3", 0, 8), H("M3", 8, 16), OP.max)
+            ts(H("OF", 16, 32), H("KV", 0, 16), 4095, OP.bitwise_and)
+            cp(H("su", 0, 8), H("OF", 24, 32))
+            ts(H("OF", 0, 16), H("KV", 0, 16), 12, OP.arith_shift_right)
+            negE, Rr, Rl, qs = H("OF", 0, 8), H("OF", 8, 16), H("OF", 16, 24), H("OF", 24, 32)
+            qa, la = CFG["QACT"][hi], CFG["LACT"][hi]
+            DQ, DL = H("Dq"), H("Dl")
+            if qa == 3:
+                DQ = V(PS, 128, 256)
+                act(H("Dq"), IND(XW, H("su", 0, 8)), AF.Copy)
+                mm([(DQ, V("I"), H("Dq"), True, False), (DQ, V("NI"), A, False, True)])
+                act(H("gt"), DQ, AF.Sign, CMH)
+            else:
+                tt(H("Dq"), IND(XW, H("su", 0, 8)), A, OP.subtract)
+                ts(H("gt"), H("Dq"), 0.0, OP.is_gt)
+            fold(V(PE, 128, 136), "BW", "gt", 128 * b, 8, True, True)
+            tt(S(0), H("K3", 0, 8), H("K3", 8, 16), OP.is_lt)
+            tt(S(1), Rl, Rr, OP.subtract)
+            ts(S(2), V(PE, 128, 136), -0.5 if qa == 3 else 7.5, OP.is_ge)
+            tt(S(3), S(2), S(0), OP.is_equal)
+            tt(S(4), S(3), S(1), OP.mult)
+            tt(S(5), S(4), Rr, OP.add)
+            cp(H("su", 8, 16), S(5))
+            if la == 3:
+                DL = V(PS, 264, 392)
+                act(H("Dl"), IND(XW, H("su", 8, 16)), AF.Copy)
+                mm([(DL, V("I"), H("Dl"), True, False), (DL, V("NI"), A, False, True)])
+            else:
+                tt(H("Dl"), IND(XW, H("su", 8, 16)), A, OP.subtract)
+            act(H("ABl"), DL, AF.Abs)
+            fold(V(PE, 136, 144), "NBW", "ABl", 128 * b, 8, True, True)
+            tt(S(6), qs, S(5), OP.subtract)
+            if qa >= 2:
+                act(H("cq"), DQ, AF.Relu, CM2, -1.0)
+                act(H("r2"), DQ, AF.Relu, CM2)
+                mm([(V(PS, 0, 128), V("I"), H("Dq"), True, False)] + ([(V(PS, 0, 128), V("I"), A, False, False)] if qa == 2 else [])
+                   + [(V(PS, 0, 128), V("I"), H("cq"), False, False), (V(PS, 0, 128), V("NI"), H("r2"), False, True)])
+                act(H(AW, 272, 400), V(PS, 0, 128), AF.Copy)
+            elif qa == 1:
+                ts(H("cq"), H("Dq"), -2.0, OP.max, 2.0, OP.min)
+                mm([(V(PS, 0, 128), V("I"), A, True, False), (V(PS, 0, 128), V("I"), H("cq"), False, True)])
+                act(H(AW, 272, 400), V(PS, 0, 128), AF.Copy)
+            else:
+                ts(H("cq"), H("Dq"), -2.0, OP.max, 2.0, OP.min)
+                tt(H(AW, 272, 400), A, H("cq"), OP.add)
+            go = H(SA, 0, 8)
+            tt(go, V(PE, 136, 144), negE, OP.is_gt)
+            ts(S(7), go, NDUM, OP.mult, DUM, OP.add)
+            tt(S(8), S(7), S(5), OP.max)
+            if CFG["MPRE"][hi]:
+                tt(H("msk", 0, 144), IND(S(5), BX9), H("Rf", 0, 144), OP.is_equal)
+                tt(S(10), go, S(6), OP.mult)
+                tt(H("md", 0, 144), IND(S(10), BX9), H("msk", 0, 144), OP.mult)
+            else:
+                tt(H("msk", 0, 144), IND(S(8), BX9), H("Rf", 0, 144), OP.is_equal)
+                tt(H("md", 0, 144), IND(S(6), BX9), H("msk", 0, 144), OP.mult)
+            mm([(V(PR, 272, 416), V("If"), H("Rf", 0, 144), True, False)]
+               + ([(V(PR, 272, 416), V("I"), V("PAR"), False, False)] if t == TS - 1 else []))
+            mm([(V(PR, 272, 416), V("If"), H("md", 0, 144), False, True)])
+            if t == TS - 1:
+                ts(H(SR, 0, 144), V(PR, 272, 416), 4.0, OP.mult)
+            else:
+                cp(H(SR, 0, 144), V(PR, 272, 416))
+            mm([(V(PS, 256, 264), V("I"), V("cb"), True, False), (V(PS, 256, 264), V("IC"), go, False, True)])
+            cp(H("su", 16, 24), V(PS, 256, 264))
+            act(H(SA, 16, 144), IND(H(AW, 0, AWW), H("su", 16, 24)), AF.Copy)
+
+            def send_r(t=t, b=b, SR=SR):
+                return g.remote_dma(T["RU%d" % (t + 1)][:, 144 * b:144 * b + 144], T[SR][:, 144 * b:144 * b + 144],
+                                    T.sem["ar%d_%d" % (t, b)], T.sem.sent, pid, rid, emask)
+
+            def send_a(t=t, b=b, SA=SA):
+                return g.remote_dma(T["AW%d" % (t + 1)][:, AWW * b:AWW * b + 144], T[SA][:, 144 * b:144 * b + 144],
+                                    T.sem["aa%d_%d" % (t, b)], T.sem.sent, pid, rid, emask)
+            k1 = add("pool", send_r, H(SR, 0, 144)[1], [], 800.0, "remote")
+            sends.append((k1, add("pool", send_a, H(SA, 0, 144)[1], [], 800.0, "remote", after=[k1])))
+            if CFG["CREP"] == "act":
+                act(H("crep"), IND(V("IOTA"), H("su", 8, 16)), AF.Copy)
+            else:
+                cp(H("crep"), IND(V("IOTA"), H("su", 8, 16)))
+            tt(H("eq"), IND(S(8), BY), H("crep"), OP.is_equal)
+            fold(V(PE, 144, 152), "TRI", "eq", 128 * b, 8, True, True)
+            if la >= 2:
+                act(H("cl"), DL, AF.Relu, CM8)
+                act(H("r3"), DL, AF.Relu, CM8, -1.0)
+                mm([(V(PS, 128, 256), V("I"), H("cl"), True, False), (V(PS, 128, 256), V("NI"), H("r3"), False, True)])
+                act(H("tb"), V(PS, 128, 256), AF.Copy)
+            elif la == 1:
+                ts(H("cl"), H("Dl"), -8.0, OP.max, 8.0, OP.min)
+                mm([(V(PS, 384, 512), V("I"), H("Dl"), True, False), (V(PS, 384, 512), V("NI"), H("cl"), False, True)])
+                act(H("tb"), V(PS, 384, 512), AF.Copy)
+            else:
+                ts(H("cl"), H("Dl"), -8.0, OP.max, 8.0, OP.min)
+                tt(H("tb"), H("Dl"), H("cl"), OP.subtract)
+            tt(S(9), S(8), V(PE, 144, 152), OP.max)
+            ts(H("su", 32, 48, 2), S(9), DUM, OP.min)
+            if hi == 0:
+                lead.append((first, len(ops)))
+        for b in (1, 0):
+            for y in range(7, -1, -1):
+                tt(IND(XW, V("su", 48 * b + 32 + 2 * y, 48 * b + 33 + 2 * y)), V("tb", 128 * b + 16 * y, 128 * b + 16 * y + 16),
+                   V(AW, AWW * b + 16 + 16 * y, AWW * b + 32 + 16 * y), OP.add)
+        steps.append((step0, len(ops)))
+        for b, k in zip((1, 0), sends):
+            add("arr", None, [], [("RU%d" % (t + 1), 144 * b, 144 * b + 144)], 0.0, "ar%d_%d" % (t, b), nen, LAT_R, after=[k[0]])
+            add("arr", None, [], [("AW%d" % (t + 1), AWW * b, AWW * b + 144)], 0.0, "aa%d_%d" % (t, b), nen, LAT_R, after=[k[1]])
+
+    dma("sp", [(T.yx[:], T.X[:, 0:W])], [("X", 0, W)], [], "o_x", 6000.0)
+    dma("act", [(T.ya[:, 128 * b:128 * b + 128], T["AW%d" % TS][:, AWW * b + 16:AWW * b + 144]) for b in range(2)],
+        [("AW%d" % TS, 0, 2 * AWW)], [], "o_a", 2500.0)
+    for b in (1, 0):
+        c = 128 * b
+        ts(V("F1", c, c + 128), V("RU%d" % TS, 144 * b, 144 * b + 128), 0.25, OP.mult)
+        for j in range(1, 5):
+            i, o = "F%d" % j, "F%d" % (j + 1)
+            tt(V(o, c, c + 128, 2), V(i, c, c + 64), V(i, c + 64, c + 128), OP.min)
+            tt(V(o, c + 1, c + 128, 2), V(i, c, c + 64), V(i, c + 64, c + 128), OP.max)
+    cp(V("F0", 0, 256), IND(V("F5"), P3))
+    add("dve", lambda: g.vector.transpose(T.F6[:], T.F0[:, 0:256]), [("F0", 0, 256)], [("F6", 0, 256)], vcost(256, 1.0))
+    ts(V("F8"), IND(V("F6"), P4), 12582912.0, OP.add, -12582912.0, OP.add)
+    for eng, sem, part in (("act", "o_r", pieces[:8]), ("sp", "o_r2", pieces[8:])):
+        dma(eng, [(T.yr[32 * gh + 16 * gl:32 * gh + 16 * gl + 16, 128 * b:128 * b + 128],
+                   T.F8[32 * gh + 16 * b:32 * gh + 16 * b + 16, 128 * gl:128 * gl + 128]) for (gh, b, gl) in part],
+            [("F8", 0, 256)], [], sem, 2500.0)
+    cp(V("KV", 0, 16), V("F5", 0, 256, 16))
+    tt(V("ng"), V("F5", 0, 256, 16), V("KV", 0, 16), OP.subtract)
+    tt(V("fb"), IND(V("ng"), P5), V("DG"), OP.mult)
+    mm([(V("PE0", 0, 256), V("BO"), V("fb"), True, True)])
+    ts(V("ys2"), V("PE0", 0, 256), -8.0, OP.mult, 1.0, OP.add)
+    dma("sp", [(T.ys[:], T.ys2[0:128:16, :])], [("ys2", 0, 256)], [], "o_s", 2500.0)
+
+    n = len(ops)
+    succ = [[] for _ in range(n)]
+    for k, o in enumerate(ops):
+        for j in o["deps"]:
+            succ[j].append(k)
+
+    def edge(j, k):
+        a, b = ops[j]["eng"], ops[k]["eng"]
+        if a == b and (a in ("pe", "pool") or j in ops[k]["soft"]):
+            return 0.0
+        return ops[j]["lat"] + (LAT_SAME if a == b else LAT_X)
+    pri = [0.0] * n
+    for k in range(n - 1, -1, -1):
+        pri[k] = ops[k]["cost"] + max([edge(k, s) + pri[s] for s in succ[k]] + [ops[k]["lat"]])
+    for (a, e) in lead:
+        for k in range(a, e):
+            pri[k] += CFG["BIAS"]
+    for (a, e) in steps:
+        names = {}
+        for k in range(a, e):
+            nm, c0 = ops[k]["w"][0], ops[k]["w"][1]
+            nm = "%s.%d" % (nm[:2] if nm[:2] in ("AW", "SR", "SA") else nm, c0)
+            names[nm] = names.get(nm, 0) + 1
+            ops[k]["key"] = nm + "abcdefghijklmnop"[names[nm] - 1]
+    for k, o in enumerate(ops):
+        o["pri"] = pri[k]
+        o["succ"] = [(s, edge(k, s)) for s in succ[k]]
+    order = arrange(ops)
+
+    pos = {k: i for i, k in enumerate(order)}
+    need = set()
+    seen = {}
+    waits = {}
+    for k in order:
+        e = ops[k]["eng"]
+        w = []
+        if e != "arr":
+            best = {}
+            for j in ops[k]["deps"]:
+                o = ops[j]
+                if o["sem"] == "remote" or (o["eng"] == e and e in ("pe", "pool")) or j in ops[k]["soft"]:
+                    continue
+                if o["sem"] is not None:
+                    if (e, j) not in seen:
+                        seen[(e, j)] = 1
+                        w.append(j)
+                elif pos[j] > seen.get((e, o["eng"]), -1) and pos[j] > best.get(o["eng"], (-1, 0))[0]:
+                    best[o["eng"]] = (pos[j], j)
+            for f, (p, j) in best.items():
+                seen[(e, f)] = p
+                need.add(j)
+                w.append(j)
+        waits[k] = w
+    count = {}
+    val = {}
+    for k in order:
+        if k in need:
+            count[ops[k]["eng"]] = count.get(ops[k]["eng"], 0) + 1
+            val[k] = count[ops[k]["eng"]]
+    for k in order:
+        o = ops[k]
+        if o["eng"] == "arr":
+            continue
+        for j in waits[k]:
+            if ops[j]["sem"] is not None:
+                Q[o["eng"]].wait_ge(T.sem[ops[j]["sem"]], ops[j]["cnt"])
+            else:
+                Q[o["eng"]].wait_ge(T.sem["c_" + ops[j]["eng"]], val[j])
+        ins = o["fn"]()
+        if k in need:
+            ins.then_inc(T.sem["c_" + o["eng"]], 1)
+    g.wait_ge(T.sem.sent, 4 * TS * nen)
+    for o in ops:
+        if o["sem"] is not None and o["sem"].startswith("o_"):
+            g.wait_ge(T.sem[o["sem"]], o["cnt"])
+    return ops, order

@@ -3,13 +3,11 @@ from concourse.mybir import AluOpType, ActivationFunctionType
 N, W, C, TS = 4, 4096, 256, 4
 WX = W + 16
 AWW = 400
-CFG = {"REF_DVE": ((4, 4), (0, 2)), "MPRE": (1, 1), "PROBE_ACT": (4, 8), "CREP": "act", "WIN": 100.0, "QACT": (2, 2), "LACT": (2, 2),
-       "BIAS": 2000.0, "NPE": False, "WAW": True}
+CFG = {"REF_DVE": ((4, 4), (0, 4)), "MPRE": (1, 1), "PROBE_ACT": (8, 4), "CREP": "dve", "WIN": 200.0, "QACT": (0, 0), "LACT": (2, 0),
+       "BIAS": 500.0, "NPE": False, "WAW": True}
 ORDER = {_p.split(":")[0]: int(_p.split(":")[1]) for _p in (
-    "G.1024a:-28 mk.0a:2 sm.176a:-20 M3.0a:-12 sm.48a:-20 sm.160a:-10 Rf.144a:15 su.56a:-13 Dd.3072a:11 msk.144a:-25 Dd.1024a:38 "
-    "Dd.1792a:43 SR.144a:-13 K3.16a:-52 Dd.1280a:38 K.128a:20 K3.0a:55 AB.1536a:23 G.1792a:23 si.0a:4 vo.128a:-18 gr.0a:-10 sm.168a:-5 "
-    "Dd.512a:-45 Dd.2560a:10 Dl.0a:-15 sm.192a:-20 Dd.3840a:13 G.2560a:5 eq.128a:20 sm.0a:-40 su.16a:10 AB.2560a:-27 pr.0b:-10 "
-    "AW.144a:-20 msk.0a:-23 sm.64a:5 Dd.1536a:20 QU.128a:-10 Dd.3584a:20").split()}
+    "SR.0a:-20 Dd.3840a:18 G.2560a:-15 Dd.1024a:5 Dd.1536a:8 Dd.3328a:10 si.128a:-20 Dd.0a:30 dh.0a:5 msk.0a:-15 G.3584a:-10 "
+    "u.128a:-3 md.144a:10 OF.32a:20 sm.184a:-20 Dd.512a:-5 OF.48a:-10 wr.128a:20 Dd.768a:-5").split()}
 
 SCRATCH = {}
 for _n, _w, _d in (
@@ -49,8 +47,9 @@ for _b in ("PS0", "PS1", "PE0", "PE1", "PR0", "PR1", "PV0", "PV1"):
 SEMAPHORES = (["c_dve", "c_act", "c_pe", "c_pool", "sent", "d_x", "d_l", "d_a", "d_w", "d_s", "o_x", "o_r", "o_r2", "o_a", "o_s"]
               + ["a%s%d_%d" % (k, t, b) for k in "ra" for t in range(TS) for b in range(2)])
 
-CYC, PCYC, GC, SC = 0.95, 0.5, 1.56, 3.8
-LAT_SAME, LAT_X, LAT_R = 60.0, 110.0, 3200.0
+CYC, PCYC, GC, SC = 0.87, 0.55, 1.56, 3.8
+LAT_SAME, LAT_X, LAT_R = 150.0, 250.0, 4000.0
+OVH, MINC, POV = 20.0, 64.0, 4.0
 OP = AluOpType
 AF = ActivationFunctionType
 
@@ -135,7 +134,7 @@ def rank_program(g, core, T, topo):
     def vcost(n, f):
         if f in (GC, SC):
             return 50.0 + n * f * CYC
-        return 10.0 + max(64.0, n * f) * CYC
+        return OVH + max(MINC, n * f) * CYC
 
     def cp(o, i):
         f = GC if i[4] == "ind" else (0.5 if two(o, i) else 1.0)
@@ -175,7 +174,7 @@ def rank_program(g, core, T, topo):
         for (o, l, r, st, sp) in items:
             rd += l[1] + r[1]
             wr += o[1]
-            cost += 4.0 + max(64, r[2]) * PCYC * (4 if r[3] == "float32" else 1)
+            cost += POV + max(64, r[2]) * PCYC * (4 if r[3] == "float32" else 1)
 
         def fn():
             last = None

@@ -3,11 +3,11 @@ from concourse.mybir import AluOpType, ActivationFunctionType
 N, W, C, TS = 4, 4096, 256, 4
 WX = W + 16
 AWW = 400
-CFG = {"REF_DVE": ((4, 4), (0, 4)), "MPRE": (1, 1), "PROBE_ACT": (8, 4), "CREP": "dve", "WIN": 200.0, "QACT": (0, 0), "LACT": (2, 0),
-       "BIAS": 500.0, "NPE": False, "WAW": True}
+CFG = {"REF_DVE": ((3, 4), (3, 3)), "MPRE": (1, 1), "PROBE_ACT": (8, 4), "CREP": "act", "WIN": 100.0, "QACT": (1, 1), "LACT": (2, 0),
+       "PRE": (1, 1), "EQPRE": (0, 1), "BIAS": 1000.0, "NPE": False, "WAW": True}
 ORDER = {_p.split(":")[0]: int(_p.split(":")[1]) for _p in (
-    "SR.0a:-20 Dd.3840a:18 G.2560a:-15 Dd.1024a:5 Dd.1536a:8 Dd.3328a:10 si.128a:-20 Dd.0a:30 dh.0a:5 msk.0a:-15 G.3584a:-10 "
-    "u.128a:-3 md.144a:10 OF.32a:20 sm.184a:-20 Dd.512a:-5 OF.48a:-10 wr.128a:20 Dd.768a:-5").split()}
+    "Dd.3072a:-30 Dd.1536a:-10 K1.1a:7 sm.152a:10 Rf.144a:20 AB.512a:-3 sm.176a:-20 gt.128a:-3 sm.48a:-20 AB.2048a:-25 eq.0a:20 "
+    "M1.0a:5").split()}
 
 SCRATCH = {}
 for _n, _w, _d in (
@@ -25,9 +25,9 @@ for _n, _w, _d in (
         ("trs", 16, "float32"),
         ("Rf", 288, "float32"), ("wr", 256, "bfloat16"), ("si", 256, "int32"), ("u", 288, "int32"), ("pr", 256, "int32"),
         ("p16", 256, "int32"), ("tt", 256, "int32"), ("h", 256, "int32"), ("dh", 256, "float32"), ("z", 256, "int32"),
-        ("q", 256, "int32"), ("QU", 256, "uint16"), ("vo", 256, "bfloat16"), ("K", 256, "float32"), ("K1", 128, "float32"),
-        ("K2", 64, "float32"), ("K3", 32, "float32"), ("KV", 32, "int32"), ("OF", 64, "int32"), ("oh", 256, "float32"),
-        ("mk", 256, "float32"), ("M1", 128, "float32"), ("M2", 64, "float32"), ("M3", 32, "float32"),
+        ("q", 256, "int32"), ("QU", 256, "uint16"), ("vo", 256, "bfloat16"), ("K", 256, "float32"), ("K1", 384, "float32"),
+        ("K2", 192, "float32"), ("K3", 96, "float32"), ("KV", 48, "int32"), ("OF", 64, "int32"), ("oh", 256, "int32"),
+        ("mk", 256, "float32"), ("M1", 256, "float32"), ("ID", 128, "bfloat16"), ("IE", 128, "bfloat16"),
         ("sm", 256, "float32"), ("su", 96, "uint16"), ("Dq", 256, "bfloat16"), ("gt", 256, "bfloat16"), ("Dl", 256, "bfloat16"),
         ("ABl", 256, "bfloat16"), ("cl", 256, "bfloat16"), ("tb", 256, "bfloat16"), ("cq", 256, "bfloat16"),
         ("msk", 288, "float32"), ("md", 288, "float32"), ("crep", 256, "float32"), ("eq", 256, "bfloat16"),
@@ -47,9 +47,10 @@ for _b in ("PS0", "PS1", "PE0", "PE1", "PR0", "PR1", "PV0", "PV1"):
 SEMAPHORES = (["c_dve", "c_act", "c_pe", "c_pool", "sent", "d_x", "d_l", "d_a", "d_w", "d_s", "o_x", "o_r", "o_r2", "o_a", "o_s"]
               + ["a%s%d_%d" % (k, t, b) for k in "ra" for t in range(TS) for b in range(2)])
 
-CYC, PCYC, GC, SC = 0.87, 0.55, 1.56, 3.8
-LAT_SAME, LAT_X, LAT_R = 150.0, 250.0, 4000.0
-OVH, MINC, POV = 20.0, 64.0, 4.0
+CYC, PCYC, GC, SC = 0.86, 0.5, 1.56, 3.8
+LAT_SAME, LAT_X, LAT_R = 180.0, 250.0, 4000.0
+OVH, MINC, POV = 10.0, 64.0, 8.0
+WOVEN = {"K1": 3, "F2": 2, "F3": 2, "F4": 2, "F5": 2}
 OP = AluOpType
 AF = ActivationFunctionType
 
@@ -114,6 +115,8 @@ def rank_program(g, core, T, topo):
                 for (j, e2, a2, b2, w2) in hist.setdefault(nm, []):
                     if ps and (e2 != eng or eng == "pe"):
                         deps.add(j)
+                    elif isw and w2 and nm in WOVEN and e2 == eng and j >= k - 4 and (a - a2) % WOVEN[nm] and abs(a - a2) < WOVEN[nm]:
+                        continue
                     elif (isw or w2) and a < b2 and a2 < b:
                         if isw and e2 == eng and ops[j]["sem"] is None and sem is None and not CFG["WAW"]:
                             soft.add(j)
@@ -271,9 +274,9 @@ def rank_program(g, core, T, topo):
     cp(V("wtf", 0, 1), V("wti", 0, 1))
     ts(V("WU"), V("BW"), V("wtf", 0, 1), OP.mult, 16.0, OP.mult)
     for nm, f in (("If", 1.0), ("NIf", -1.0), ("I4", 4096.0), ("I", 1.0), ("NI", -1.0), ("IA", 2048.0), ("NIA", -2048.0),
-                  ("IB", 8388608.0), ("IC", 256.0)):
+                  ("IB", 16777216.0), ("IC", 256.0), ("ID", 2040.0), ("IE", 16711680.0)):
         ts(V(nm), C128, pff, OP.is_equal, f, OP.mult)
-    ts(V("WE"), V("BW"), -4096.0, OP.mult)
+    ts(V("WE"), V("BW"), -8192.0, OP.mult)
     ts(V("NBW"), V("BW"), -1.0, OP.mult)
     ts(V("SX"), V("COLX", 0, 128), xf, OP.is_equal, 16.0, OP.mult)
     ts(V("trs"), V("COL", 0, 16), xf, OP.is_gt, 8192.0, OP.mult)
@@ -362,8 +365,9 @@ def rank_program(g, core, T, topo):
             ts(H("q"), H("z"), 12, OP.logical_shift_right, 4095, OP.bitwise_and)
             cp(H("QU"), H("q"))
             act(H("vo"), H("dh"), AF.Sign, B4088, -1.0)
-            tt(V(PS, 128, 256), H("q"), V(PR, 8, 136), OP.add)
-            mm([(V(PE, 0, 128), V("IB"), H("vo"), True, False), (V(PE, 0, 128), V("IB"), V("ONE"), False, False)])
+            ts(H("oh"), H("z"), 12, OP.logical_shift_right)
+            mm([(V(PE, 0, 128), V("IB"), H("vo"), True, False), (V(PE, 0, 128), V("IB"), V("ONE"), False, False),
+                (V(PE, 0, 128), V("IE"), V("ONE"), False, False)])
             pa = CFG["PROBE_ACT"][hi]
             for a in range(0, 16, 4):
                 c0, c1 = 128 * a, 128 * a + 512
@@ -383,21 +387,19 @@ def rank_program(g, core, T, topo):
                         act(H("AB", c0, c1), H("Dd", c0, c1), AF.Abs)
                 if a % 8 == 4:
                     fold(V(PE, 8 * (a - 4), 8 * (a + 4)), "WE", "AB", 2048 * b + 128 * (a - 4), 64, False, a == 12)
+            tt(H("mk"), H("oh"), V(PE, 0, 128), OP.add)
             tt(H("K"), H("Rf"), V(PE, 0, 128), OP.add)
-            tt(H("K1", 0, 64), H("K", 0, 64), H("K", 64, 128), OP.min)
-            tt(H("K2", 0, 32), H("K1", 0, 32), H("K1", 32, 64), OP.min)
-            tt(H("K3", 0, 16), H("K2", 0, 16), H("K2", 16, 32), OP.min)
-            tt(H("KV", 0, 8), H("K3", 0, 8), H("K3", 8, 16), OP.min)
-            tt(H("oh"), IND(H("KV", 0, 8), BX), H("K"), OP.is_equal)
-            tt(H("mk"), H("oh"), V(PS, 128, 256), OP.mult)
-            tt(H("M1", 0, 64), H("mk", 0, 64), H("mk", 64, 128), OP.max)
-            tt(H("M2", 0, 32), H("M1", 0, 32), H("M1", 32, 64), OP.max)
-            tt(H("M3", 0, 16), H("M2", 0, 16), H("M2", 16, 32), OP.max)
-            tt(H("KV", 8, 16), H("M3", 0, 8), H("M3", 8, 16), OP.max)
-            ts(H("OF", 16, 32), H("KV", 0, 16), 4095, OP.bitwise_and)
-            cp(H("su", 0, 8), H("OF", 24, 32))
-            ts(H("OF", 0, 16), H("KV", 0, 16), 12, OP.arith_shift_right)
-            negE, Rr, Rl, qs = H("OF", 0, 8), H("OF", 8, 16), H("OF", 16, 24), H("OF", 24, 32)
+            tt(H("K1", 0, 192, 3), H("mk", 0, 64), H("mk", 64, 128), OP.min)
+            tt(H("M1"), H("K"), PD, OP.add)
+            tt(H("K1", 1, 192, 3), H("K", 0, 64), H("K", 64, 128), OP.min)
+            tt(H("K1", 2, 192, 3), H("M1", 0, 64), H("M1", 64, 128), OP.min)
+            tt(H("K2", 0, 96), H("K1", 0, 96), H("K1", 96, 192), OP.min)
+            tt(H("K3", 0, 48), H("K2", 0, 48), H("K2", 48, 96), OP.min)
+            tt(H("KV", 0, 24), H("K3", 0, 24), H("K3", 24, 48), OP.min)
+            ts(H("OF", 0, 24), H("KV", 0, 24), 4095, OP.bitwise_and)
+            cp(H("su", 0, 8), H("OF", 0, 24, 3))
+            ts(H("OF", 24, 32), H("KV", 0, 24, 3), 13, OP.arith_shift_right)
+            negE, Rr, Rl, qs = H("OF", 24, 32), H("OF", 2, 24, 3), H("OF", 1, 24, 3), H("OF", 0, 24, 3)
             qa, la = CFG["QACT"][hi], CFG["LACT"][hi]
             DQ, DL = H("Dq"), H("Dl")
             if qa == 3:
@@ -409,12 +411,20 @@ def rank_program(g, core, T, topo):
                 tt(H("Dq"), IND(XW, H("su", 0, 8)), A, OP.subtract)
                 ts(H("gt"), H("Dq"), 0.0, OP.is_gt)
             fold(V(PE, 128, 136), "BW", "gt", 128 * b, 8, True, True)
-            tt(S(0), H("K3", 0, 8), H("K3", 8, 16), OP.is_lt)
+            tt(S(0), H("K3", 0, 24, 3), H("K3", 24, 48, 3), OP.is_lt)
             tt(S(1), Rl, Rr, OP.subtract)
             ts(S(2), V(PE, 128, 136), -0.5 if qa == 3 else 7.5, OP.is_ge)
-            tt(S(3), S(2), S(0), OP.is_equal)
-            tt(S(4), S(3), S(1), OP.mult)
-            tt(S(5), S(4), Rr, OP.add)
+            if CFG["PRE"][hi]:
+                tt(S(11), S(0), S(1), OP.mult)
+                ts(S(12), S(0), 2.0, OP.mult, -1.0, OP.add)
+                tt(S(13), Rl, S(11), OP.subtract)
+                tt(S(3), S(12), S(1), OP.mult)
+                tt(S(4), S(2), S(3), OP.mult)
+                tt(S(5), S(4), S(13), OP.add)
+            else:
+                tt(S(3), S(2), S(0), OP.is_equal)
+                tt(S(4), S(3), S(1), OP.mult)
+                tt(S(5), S(4), Rr, OP.add)
             cp(H("su", 8, 16), S(5))
             if la == 3:
                 DL = V(PS, 264, 392)
@@ -423,7 +433,8 @@ def rank_program(g, core, T, topo):
             else:
                 tt(H("Dl"), IND(XW, H("su", 8, 16)), A, OP.subtract)
             act(H("ABl"), DL, AF.Abs)
-            fold(V(PE, 136, 144), "NBW", "ABl", 128 * b, 8, True, True)
+            mm([(V(PE, 136, 144), V("ID"), V("ONE", 0, 8), True, False)])
+            fold(V(PE, 136, 144), "NBW", "ABl", 128 * b, 8, False, True)
             tt(S(6), qs, S(5), OP.subtract)
             if qa >= 2:
                 act(H("cq"), DQ, AF.Relu, CM2, -1.0)
@@ -473,7 +484,11 @@ def rank_program(g, core, T, topo):
                 act(H("crep"), IND(V("IOTA"), H("su", 8, 16)), AF.Copy)
             else:
                 cp(H("crep"), IND(V("IOTA"), H("su", 8, 16)))
-            tt(H("eq"), IND(S(8), BY), H("crep"), OP.is_equal)
+            if CFG["EQPRE"][hi]:
+                tt(H("mk"), IND(S(5), BY), H("crep"), OP.is_equal)
+                tt(H("eq"), IND(H(SA, 0, 16), BY), H("mk"), OP.mult)
+            else:
+                tt(H("eq"), IND(S(8), BY), H("crep"), OP.is_equal)
             fold(V(PE, 144, 152), "TRI", "eq", 128 * b, 8, True, True)
             if la >= 2:
                 act(H("cl"), DL, AF.Relu, CM8)

@@ -1,13 +1,13 @@
 from concourse.mybir import AluOpType, ActivationFunctionType
 
 N, W, C, TS = 4, 4096, 256, 4
-WX = W + 16
+WX = W + 32
 AWW = 400
-CFG = {"REF_DVE": ((3, 4), (3, 3)), "MPRE": (1, 1), "PROBE_ACT": (8, 4), "CREP": "act", "WIN": 100.0, "QACT": (1, 1), "LACT": (2, 0),
-       "PRE": (1, 1), "EQPRE": (0, 1), "BIAS": 1000.0, "NPE": False, "WAW": True}
+CFG = {"REF_DVE": ((3, 4), (4, 2)), "MPRE": (1, 2), "PROBE_ACT": (8, 8), "CREP": "act", "WIN": 100.0, "QACT": (0, 0), "LACT": (1, 0),
+       "PRE": (1, 1), "SPLIT": (1, 0), "BIAS": 2000.0, "TAIL": 1000.0, "PAIR": (1, 1), "NPAR": (1, 1), "NPE": False, "WAW": True}
 ORDER = {_p.split(":")[0]: int(_p.split(":")[1]) for _p in (
-    "Dd.3072a:-30 Dd.1536a:-10 K1.1a:7 sm.152a:10 Rf.144a:20 AB.512a:-3 sm.176a:-20 gt.128a:-3 sm.48a:-20 AB.2048a:-25 eq.0a:20 "
-    "M1.0a:5").split()}
+    "u.272a:-20 u.128a:10 mk.128b:-23 si.0a:10 G.2048a:-2 z.184a:-15 Dd.3072a:-5 gt.128b:-15 Dd.3328a:-20 gr.128a:20 u.208a:-20 "
+    "PE1.144a:-10 su.16a:10 sm.8a:-20 Rf.144a:15 SR.144a:-5 K1.2a:-10 sm.16a:-10 sm.0a:-5").split()}
 
 SCRATCH = {}
 for _n, _w, _d in (
@@ -20,7 +20,7 @@ for _n, _w, _d in (
         ("cb", 8, "bfloat16"), ("cu", 160, "uint16"),
         ("I", 128, "bfloat16"), ("NI", 128, "bfloat16"), ("IA", 128, "bfloat16"), ("NIA", 128, "bfloat16"), ("IB", 128, "bfloat16"),
         ("IC", 128, "bfloat16"), ("If", 128, "float32"), ("NIf", 128, "float32"), ("I4", 128, "float32"),
-        ("Z", 272, "bfloat16"), ("ONE", 128, "bfloat16"), ("BW", 144, "bfloat16"), ("NBW", 144, "bfloat16"), ("WU", 144, "bfloat16"),
+        ("BW8", 144, "bfloat16"), ("dm2", 8, "float32"), ("I8", 128, "bfloat16"), ("NI8", 128, "bfloat16"), ("ONE", 128, "bfloat16"), ("BW", 144, "bfloat16"), ("NBW", 144, "bfloat16"), ("WU", 144, "bfloat16"),
         ("WE", 144, "bfloat16"), ("SX", 128, "bfloat16"), ("BO", 128, "bfloat16"), ("DG", 256, "bfloat16"), ("TRI", 2048, "bfloat16"),
         ("trs", 16, "float32"),
         ("Rf", 288, "float32"), ("wr", 256, "bfloat16"), ("si", 256, "int32"), ("u", 288, "int32"), ("pr", 256, "int32"),
@@ -32,7 +32,7 @@ for _n, _w, _d in (
         ("ABl", 256, "bfloat16"), ("cl", 256, "bfloat16"), ("tb", 256, "bfloat16"), ("cq", 256, "bfloat16"),
         ("msk", 288, "float32"), ("md", 288, "float32"), ("crep", 256, "float32"), ("eq", 256, "bfloat16"),
         ("F0", 288, "float32"), ("F1", 256, "float32"), ("F2", 256, "float32"), ("F3", 256, "float32"), ("F4", 256, "float32"),
-        ("F5", 256, "float32"), ("F6", 256, "float32"), ("F7", 256, "int32"), ("F8", 256, "float32"),
+        ("F5", 256, "float32"), ("F6", 256, "float32"), ("cr2", 128, "float32"), ("F8", 256, "float32"),
         ("r2", 256, "bfloat16"), ("r3", 256, "bfloat16"), ("gr", 256, "bfloat16"), ("fb", 256, "bfloat16"), ("ys2", 256, "float32")):
     SCRATCH[_n] = ("sbuf", [128, _w], _d)
 for _t in range(TS + 1):
@@ -50,7 +50,7 @@ SEMAPHORES = (["c_dve", "c_act", "c_pe", "c_pool", "sent", "d_x", "d_l", "d_a", 
 CYC, PCYC, GC, SC = 0.86, 0.5, 1.56, 3.8
 LAT_SAME, LAT_X, LAT_R = 180.0, 250.0, 4000.0
 OVH, MINC, POV = 10.0, 64.0, 8.0
-WOVEN = {"K1": 3, "F2": 2, "F3": 2, "F4": 2, "F5": 2}
+WOVEN = {"K1": 3, "su": 2, "F2": 2, "F3": 2, "F4": 2, "F5": 2}
 OP = AluOpType
 AF = ActivationFunctionType
 
@@ -274,10 +274,14 @@ def rank_program(g, core, T, topo):
     cp(V("wtf", 0, 1), V("wti", 0, 1))
     ts(V("WU"), V("BW"), V("wtf", 0, 1), OP.mult, 16.0, OP.mult)
     for nm, f in (("If", 1.0), ("NIf", -1.0), ("I4", 4096.0), ("I", 1.0), ("NI", -1.0), ("IA", 2048.0), ("NIA", -2048.0),
-                  ("IB", 16777216.0), ("IC", 256.0), ("ID", 2040.0), ("IE", 16711680.0)):
+                  ("IB", 16777216.0), ("IC", 256.0), ("ID", 2040.0), ("IE", 16711680.0), ("I8", 8192.0), ("NI8", -8192.0)):
         ts(V(nm), C128, pff, OP.is_equal, f, OP.mult)
     ts(V("WE"), V("BW"), -8192.0, OP.mult)
     ts(V("NBW"), V("BW"), -1.0, OP.mult)
+    ts(V("BW8"), V("BW"), 8192.0, OP.mult)
+    ts(V("cu", 136, 140), V("ci", 64, 68), 0.25, OP.mult)
+    BE = V("cu", 136, 140)
+    ts(V("dm2", 0, 1), DUM, 16.0, OP.add)
     ts(V("SX"), V("COLX", 0, 128), xf, OP.is_equal, 16.0, OP.mult)
     ts(V("trs"), V("COL", 0, 16), xf, OP.is_gt, 8192.0, OP.mult)
     for x in range(16):
@@ -292,14 +296,16 @@ def rank_program(g, core, T, topo):
 
     cp(V("L1"), IND(V("L"), P1))
     add("dve", lambda: g.vector.transpose(T.L2[:], T.L1[:]), [("L1", 0, 256)], [("L2", 0, 256)], vcost(256, 1.0))
-    cp(V("L3"), IND(V("L2"), P2))
-    tt(V("L4"), IND(V("L2"), P2b), V("L3"), OP.subtract)
     ts(V("sgb"), V("sgi"), 0.0, OP.is_lt)
     fold(V("PE0", 0, 16), "BW", "sgb", 0, 16, True, True)
     cp(V("ng"), V("PE0", 0, 16))
-    tt(V("L5"), IND(V("ng"), BN), V("L4"), OP.mult)
-    tt(V("L6"), V("L5"), V("L3"), OP.add)
-    cp(V("RU0"), V("L6"))
+    cp(V("msk"), IND(V("ng"), BN))
+    ts(V("md"), V("msk"), -1.0, OP.mult, 1.0, OP.add)
+    tt(V("L4"), IND(V("L2"), P2b), V("msk"), OP.mult)
+    tt(V("L5"), IND(V("L2"), P2), V("md"), OP.mult)
+    for c in (144, 0):
+        tt(V("L6", c, c + 144), V("L5", c, c + 144), V("L4", c, c + 144), OP.add)
+        cp(V("RU0", c, c + 144), V("L6", c, c + 144))
 
     XW = V("X")
     nv = [0]
@@ -310,7 +316,8 @@ def rank_program(g, core, T, topo):
         sends = []
         step0 = len(ops)
         for hi, b in enumerate((1, 0)):
-            def H(nm, a=0, e=128, s=1, b=b):
+            def H(nm, a=0, e=128, s=1, other=None, b=b):
+                nm = other or nm
                 w = SCRATCH[nm][1][1] // 2
                 return V(nm, w * b + a, w * b + e, s)
 
@@ -336,34 +343,38 @@ def rank_program(g, core, T, topo):
                         cp(H("G", 128 * a, 128 * e), src)
                     else:
                         act(H("G", 128 * a, 128 * e), src, AF.Copy)
-            SN = V(PS, 0, 128)
-            npe = t > 0 and CFG["NPE"]
-            if t > 0 and not npe:
+            if t > 0:
                 act(H("gr"), IND(H(AW, 0, 16), BX), AF.Copy)
                 mm([(V(PE, 256, 384), V("SX"), H("gr"), True, True)])
-            for a in (0, 8):
-                fold(V(PS, 8 * a, 8 * a + 64), "WU", "G", 2048 * b + 128 * a, 64, True, True)
-                if npe:
-                    fold(V(PE, 256 + 8 * a, 320 + 8 * a), "WU", "G", 2048 * b + 128 * a, 64, True, False)
-                    if a == 0:
-                        act(H("gr"), IND(H(AW, 0, 16), BX), AF.Copy)
-                    mm([(V(PE, 256 + 8 * a, 320 + 8 * a), V("SX"), H("gr", 0, 64), False, True)])
-                    SN = V(PE, 256, 384)
-            cp(H("si"), V(PS, 0, 128))
-            ts(H("u"), H("si"), 4, OP.logical_shift_right, 4095, OP.bitwise_and)
-            ts(H("u", 128, 136), H("si", 0, 8), 4, OP.logical_shift_right, 4095, OP.bitwise_and)
-            tt(H("pr"), H("u"), H("u", 8, 136), OP.mult)
-            ts(H("p16"), H("pr"), 1, OP.logical_shift_right, 4080, OP.bitwise_and)
-            tt(H("tt"), H("p16"), SN, OP.add)
-            if t > 0 and not npe:
-                tt(H("pr"), H("tt"), V(PE, 256, 384), OP.add)
-                ts(H("h"), H("pr"), 4080, OP.bitwise_and)
+            fold(V(PS, 0, 64), "WU", "G", 2048 * b, 64, True, True)
+            if CFG["SPLIT"][hi]:
+                fold(V("PV1", 0, 72), "WU", "G", 2048 * b + 896, 72, True, True)
+                parts = ((0, 64, 0, 56, PS, 0), (64, 128, 56, 128, "PV1", -56))
             else:
-                ts(H("h"), H("tt"), 4080, OP.bitwise_and)
-            tt(H("dh"), H("h"), PD, OP.mult)
-            tt(H("z"), H("dh"), V(PR, 0, 128), OP.add)
-            ts(H("q"), H("z"), 12, OP.logical_shift_right, 4095, OP.bitwise_and)
-            cp(H("QU"), H("q"))
+                fold(V(PS, 64, 128), "WU", "G", 2048 * b + 1024, 64, True, True)
+                parts = ((0, 128, 0, 128, PS, 0),)
+            for (s0, s1, a, e, bank, sh) in parts:
+                cp(H("si", s0, s1), V(bank, s0 + sh, s1 + sh))
+                ts(H("u", s0, s1), H("si", s0, s1), 4, OP.logical_shift_right, 4095, OP.bitwise_and)
+                if s0 == 0:
+                    ts(H("u", 128, 136), H("si", 0, 8), 4, OP.logical_shift_right, 4095, OP.bitwise_and)
+                tt(H("pr", a, e), H("u", a, e), H("u", a + 8, e + 8), OP.mult)
+                ts(H("p16", a, e), H("pr", a, e), 1, OP.logical_shift_right, 4080, OP.bitwise_and)
+                npar = t > 0 and CFG["NPAR"][hi]
+                SN = V(bank, a + sh, e + sh)
+                if npar:
+                    tt(H("z", a, e), H("si", a, e), V(PE, 256 + a, 256 + e), OP.add)
+                    SN = H("z", a, e)
+                tt(H("tt", a, e), H("p16", a, e), SN, OP.add)
+                if t > 0 and not npar:
+                    tt(H("pr", a, e), H("tt", a, e), V(PE, 256 + a, 256 + e), OP.add)
+                    ts(H("h", a, e), H("pr", a, e), 4080, OP.bitwise_and)
+                else:
+                    ts(H("h", a, e), H("tt", a, e), 4080, OP.bitwise_and)
+                tt(H("dh", a, e), H("h", a, e), V(PR, 144 + a, 144 + e), OP.mult)
+                tt(H("z", a, e), H("dh", a, e), V(PR, a, e), OP.add)
+                ts(H("q", a, e), H("z", a, e), 12, OP.logical_shift_right, 4095, OP.bitwise_and)
+                cp(H("QU", a, e), H("q", a, e))
             act(H("vo"), H("dh"), AF.Sign, B4088, -1.0)
             ts(H("oh"), H("z"), 12, OP.logical_shift_right)
             mm([(V(PE, 0, 128), V("IB"), H("vo"), True, False), (V(PE, 0, 128), V("IB"), V("ONE"), False, False),
@@ -387,6 +398,7 @@ def rank_program(g, core, T, topo):
                         act(H("AB", c0, c1), H("Dd", c0, c1), AF.Abs)
                 if a % 8 == 4:
                     fold(V(PE, 8 * (a - 4), 8 * (a + 4)), "WE", "AB", 2048 * b + 128 * (a - 4), 64, False, a == 12)
+            tail = len(ops)
             tt(H("mk"), H("oh"), V(PE, 0, 128), OP.add)
             tt(H("K"), H("Rf"), V(PE, 0, 128), OP.add)
             tt(H("K1", 0, 192, 3), H("mk", 0, 64), H("mk", 64, 128), OP.min)
@@ -408,8 +420,8 @@ def rank_program(g, core, T, topo):
                 mm([(DQ, V("I"), H("Dq"), True, False), (DQ, V("NI"), A, False, True)])
                 act(H("gt"), DQ, AF.Sign, CMH)
             else:
+                tt(H("gt"), IND(XW, H("su", 0, 8)), A, OP.is_gt)
                 tt(H("Dq"), IND(XW, H("su", 0, 8)), A, OP.subtract)
-                ts(H("gt"), H("Dq"), 0.0, OP.is_gt)
             fold(V(PE, 128, 136), "BW", "gt", 128 * b, 8, True, True)
             tt(S(0), H("K3", 0, 24, 3), H("K3", 24, 48, 3), OP.is_lt)
             tt(S(1), Rl, Rr, OP.subtract)
@@ -451,15 +463,13 @@ def rank_program(g, core, T, topo):
                 tt(H(AW, 272, 400), A, H("cq"), OP.add)
             go = H(SA, 0, 8)
             tt(go, V(PE, 136, 144), negE, OP.is_gt)
-            ts(S(7), go, NDUM, OP.mult, DUM, OP.add)
-            tt(S(8), S(7), S(5), OP.max)
-            if CFG["MPRE"][hi]:
-                tt(H("msk", 0, 144), IND(S(5), BX9), H("Rf", 0, 144), OP.is_equal)
+            tt(H("msk", 0, 144), IND(S(5), BX9), H("Rf", 0, 144), OP.is_equal)
+            if CFG["MPRE"][hi] == 2:
+                tt(H("L3", 0, 144), IND(S(6), BX9), H("msk", 0, 144), OP.mult)
+                tt(H("md", 0, 144), IND(H(SA, 0, 16), BX9), H("L3", 0, 144), OP.mult)
+            else:
                 tt(S(10), go, S(6), OP.mult)
                 tt(H("md", 0, 144), IND(S(10), BX9), H("msk", 0, 144), OP.mult)
-            else:
-                tt(H("msk", 0, 144), IND(S(8), BX9), H("Rf", 0, 144), OP.is_equal)
-                tt(H("md", 0, 144), IND(S(6), BX9), H("msk", 0, 144), OP.mult)
             mm([(V(PR, 272, 416), V("If"), H("Rf", 0, 144), True, False)]
                + ([(V(PR, 272, 416), V("I"), V("PAR"), False, False)] if t == TS - 1 else []))
             mm([(V(PR, 272, 416), V("If"), H("md", 0, 144), False, True)])
@@ -484,12 +494,17 @@ def rank_program(g, core, T, topo):
                 act(H("crep"), IND(V("IOTA"), H("su", 8, 16)), AF.Copy)
             else:
                 cp(H("crep"), IND(V("IOTA"), H("su", 8, 16)))
-            if CFG["EQPRE"][hi]:
-                tt(H("mk"), IND(S(5), BY), H("crep"), OP.is_equal)
-                tt(H("eq"), IND(H(SA, 0, 16), BY), H("mk"), OP.mult)
-            else:
-                tt(H("eq"), IND(S(8), BY), H("crep"), OP.is_equal)
-            fold(V(PE, 144, 152), "TRI", "eq", 128 * b, 8, True, True)
+            tt(H("mk"), IND(S(5), BY), H("crep"), OP.is_equal)
+            mm([(V(PE, 144, 152), V("If"), S(5), True, False), (V(PE, 144, 152), V("I8"), V("ONE", 0, 8), False, False),
+                (V(PE, 144, 152), V("NI8"), go, False, False)])
+            if CFG["PAIR"][hi]:
+                cp(H("su", 24, 28), V("sm", 128 * b + 41, 128 * b + 48, 2))
+                act(H("cr2", 0, 64), IND(V("IOTA"), H("su", 24, 28)), AF.Copy)
+                tt(H("M1", 0, 64), IND(S(5), BE), H("cr2", 0, 64), OP.is_equal)
+                tt(H("gt", 0, 64), IND(H(SA, 0, 16), BE), H("M1", 0, 64), OP.mult)
+                fold(V(PE, 145, 152, 2), "BW8", "gt", 128 * b, 4, False, False)
+            tt(H("eq"), IND(H(SA, 0, 16), BY), H("mk"), OP.mult)
+            fold(V(PE, 144, 152), "TRI", "eq", 128 * b, 8, False, True)
             if la >= 2:
                 act(H("cl"), DL, AF.Relu, CM8)
                 act(H("r3"), DL, AF.Relu, CM8, -1.0)
@@ -502,11 +517,20 @@ def rank_program(g, core, T, topo):
             else:
                 ts(H("cl"), H("Dl"), -8.0, OP.max, 8.0, OP.min)
                 tt(H("tb"), H("Dl"), H("cl"), OP.subtract)
-            tt(S(9), S(8), V(PE, 144, 152), OP.max)
-            ts(H("su", 32, 48, 2), S(9), DUM, OP.min)
+            if CFG["PAIR"][hi]:
+                ts(H("su", 32, 40, 2), V(PE, 144, 152, 2), DUM, OP.min)
+                ts(H("su", 33, 40, 2), V(PE, 145, 152, 2), V("dm2", 0, 1), OP.min)
+            else:
+                ts(H("su", 32, 48, 2), V(PE, 144, 152), DUM, OP.min)
             if hi == 0:
-                lead.append((first, len(ops)))
+                lead.append((first, len(ops), CFG["BIAS"]))
+                lead.append((tail, len(ops), CFG["TAIL"]))
         for b in (1, 0):
+            if CFG["PAIR"][1 - b]:
+                for y in range(6, -1, -2):
+                    tt(IND(XW, V("su", 48 * b + 32 + y, 48 * b + 34 + y)), V("tb", 128 * b + 16 * y, 128 * b + 16 * y + 32),
+                       V(AW, AWW * b + 16 + 16 * y, AWW * b + 48 + 16 * y), OP.add)
+                continue
             for y in range(7, -1, -1):
                 tt(IND(XW, V("su", 48 * b + 32 + 2 * y, 48 * b + 33 + 2 * y)), V("tb", 128 * b + 16 * y, 128 * b + 16 * y + 16),
                    V(AW, AWW * b + 16 + 16 * y, AWW * b + 32 + 16 * y), OP.add)
@@ -553,9 +577,9 @@ def rank_program(g, core, T, topo):
     pri = [0.0] * n
     for k in range(n - 1, -1, -1):
         pri[k] = ops[k]["cost"] + max([edge(k, s) + pri[s] for s in succ[k]] + [ops[k]["lat"]])
-    for (a, e) in lead:
+    for (a, e, f) in lead:
         for k in range(a, e):
-            pri[k] += CFG["BIAS"]
+            pri[k] += f
     for (a, e) in steps:
         names = {}
         for k in range(a, e):

@@ -3,83 +3,108 @@ from concourse.mybir import AluOpType, ActivationFunctionType
 N, W, C, TS = 4, 4096, 256, 4
 WX = W + 32
 AWW = 400
-CFG = {"REF_DVE": ((3, 4), (4, 2)), "MPRE": (1, 2), "PROBE_ACT": (8, 8), "CREP": "act", "WIN": 100.0, "QACT": (0, 0), "LACT": (1, 0),
-       "PRE": (1, 1), "SPLIT": (1, 0), "BIAS": 2000.0, "TAIL": 1000.0, "PAIR": (1, 1), "NPAR": (1, 1), "NPE": False, "WAW": True}
-ORDER = {_p.split(":")[0]: int(_p.split(":")[1]) for _p in (
-    "u.272a:-20 u.128a:10 mk.128b:-23 si.0a:10 G.2048a:-2 z.184a:-15 Dd.3072a:-5 gt.128b:-15 Dd.3328a:-20 gr.128a:20 u.208a:-20 "
-    "PE1.144a:-10 su.16a:10 sm.8a:-20 Rf.144a:15 SR.144a:-5 K1.2a:-10 sm.16a:-10 sm.0a:-5").split()}
+CFG = {"REF": (((0, 4, "a"), (4, 9, "d"), (9, 12, "a"), (12, 16, "d")), ((0, 5, "a"), (5, 9, "d"), (9, 16, "a"))),
+       "PROBE": ("aa dd d a d d", "dd aa d d aa"), "H16": True, "WIN": 100.0, "QA": (0, 0), "LA": (1, 2),
+       "BIAS": 2000.0, "TAIL": 1500.0, "PAIR": (1, 1), "CSCAN": (0, 1), "MPRE": (0, 1), "GTQ": (0, 0),
+       "PMACT": (0, 1), "RFA": (0, 0), "LR": 2500.0, "TURNS": 3}
+ORDER = {}
 
 SCRATCH = {}
+_r = "bfloat16" if CFG["H16"] else "float32"
 for _n, _w, _d in (
         ("X", WX, "bfloat16"), ("IOTA", WX, "float32"), ("G", W, "bfloat16"), ("Dd", W, "bfloat16"), ("AB", W, "bfloat16"),
-        ("L", 256, "int32"), ("L1", 256, "float32"), ("L2", 256, "float32"), ("L3", 288, "float32"), ("L4", 288, "float32"),
-        ("L5", 288, "float32"), ("L6", 288, "float32"), ("ng", 16, "float32"),
-        ("wti", 8, "int32"), ("wtf", 8, "float32"), ("sgi", 256, "int32"), ("sgb", 256, "bfloat16"),
-        ("COL", 144, "float32"), ("COLX", 256, "float32"), ("COLG", 128, "float32"), ("PAR", 144, "bfloat16"),
-        ("pi", 8, "int32"), ("pv", 16, "int32"), ("pf", 16, "float32"), ("ci", 128, "int32"), ("cj", 128, "int32"),
-        ("cb", 8, "bfloat16"), ("cu", 160, "uint16"),
+        ("L", 256, "int32"), ("L1", 256, "float32"), ("L2", 256, "float32"), ("ng", 32, "float32"), ("ngb", 256, "float32"),
+        ("wti", 8, "int32"), ("sgi", 256, "int32"), ("sgb", 256, "bfloat16"),
+        ("COL", 144, "float32"), ("COLX", 128, "float32"), ("COLG", 128, "float32"),
+        ("pi", 8, "int32"), ("pv", 16, "int32"), ("pf", 24, "float32"), ("ci", 128, "int32"),
+        ("cb", 8, "bfloat16"), ("cu", 128, "uint16"), ("M4", 16, "bfloat16"), ("CZ", 128, "bfloat16"), ("CP", 256, "bfloat16"),
         ("I", 128, "bfloat16"), ("NI", 128, "bfloat16"), ("IA", 128, "bfloat16"), ("NIA", 128, "bfloat16"), ("IB", 128, "bfloat16"),
-        ("IC", 128, "bfloat16"), ("If", 128, "float32"), ("NIf", 128, "float32"), ("I4", 128, "float32"),
-        ("BW8", 144, "bfloat16"), ("dm2", 8, "float32"), ("I8", 128, "bfloat16"), ("NI8", 128, "bfloat16"), ("ONE", 128, "bfloat16"), ("BW", 144, "bfloat16"), ("NBW", 144, "bfloat16"), ("WU", 144, "bfloat16"),
-        ("WE", 144, "bfloat16"), ("SX", 128, "bfloat16"), ("BO", 128, "bfloat16"), ("DG", 256, "bfloat16"), ("TRI", 2048, "bfloat16"),
-        ("trs", 16, "float32"),
-        ("Rf", 288, "float32"), ("wr", 256, "bfloat16"), ("si", 256, "int32"), ("u", 288, "int32"), ("pr", 256, "int32"),
-        ("p16", 256, "int32"), ("tt", 256, "int32"), ("h", 256, "int32"), ("dh", 256, "float32"), ("z", 256, "int32"),
-        ("q", 256, "int32"), ("QU", 256, "uint16"), ("vo", 256, "bfloat16"), ("K", 256, "float32"), ("K1", 384, "float32"),
-        ("K2", 192, "float32"), ("K3", 96, "float32"), ("KV", 48, "int32"), ("OF", 64, "int32"), ("oh", 256, "int32"),
-        ("mk", 256, "float32"), ("M1", 256, "float32"), ("ID", 128, "bfloat16"), ("IE", 128, "bfloat16"),
-        ("sm", 256, "float32"), ("su", 96, "uint16"), ("Dq", 256, "bfloat16"), ("gt", 256, "bfloat16"), ("Dl", 256, "bfloat16"),
-        ("ABl", 256, "bfloat16"), ("cl", 256, "bfloat16"), ("tb", 256, "bfloat16"), ("cq", 256, "bfloat16"),
-        ("msk", 288, "float32"), ("md", 288, "float32"), ("crep", 256, "float32"), ("eq", 256, "bfloat16"),
-        ("F0", 288, "float32"), ("F1", 256, "float32"), ("F2", 256, "float32"), ("F3", 256, "float32"), ("F4", 256, "float32"),
-        ("F5", 256, "float32"), ("F6", 256, "float32"), ("cr2", 128, "float32"), ("F8", 256, "float32"),
-        ("r2", 256, "bfloat16"), ("r3", 256, "bfloat16"), ("gr", 256, "bfloat16"), ("fb", 256, "bfloat16"), ("ys2", 256, "float32")):
+        ("NIB", 128, "bfloat16"), ("IC", 128, "bfloat16"), ("If", 128, "float32"), ("IR", 128, _r), ("Id", 128, _r),
+        ("NId", 128, _r), ("Ih", 128, "bfloat16"), ("NIh", 128, "bfloat16"), ("IE", 128, "bfloat16"), ("I8", 128, "bfloat16"),
+        ("ONE", 128, "bfloat16"), ("BW", 144, "bfloat16"), ("WU", 144, "bfloat16"), ("WE", 144, "bfloat16"), ("SX", 128, "bfloat16"),
+        ("BO", 128, "bfloat16"), ("BO8", 128, "bfloat16"), ("DG", 128, "bfloat16"), ("TRI", 128, "bfloat16"), ("PK", 128, "bfloat16"),
+        ("Rf", 256, "float32"), ("Rt", 256, "float32"), ("PP", 768, "float32"), ("Rh", 256, "float16"), ("wr", 256, "bfloat16"),
+        ("si", 288, "int32"), ("u", 256, "int32"), ("pr", 256, "int32"), ("p16", 256, "int32"), ("tt", 256, "int32"),
+        ("h", 256, "int32"), ("dh", 256, "float32"), ("z", 256, "int32"), ("q", 256, "int32"), ("QU", 256, "uint16"),
+        ("vo", 256, "bfloat16"), ("KA", 384, "float32"), ("K1", 384, "float32"), ("K2", 192, "float32"),
+        ("K3", 96, "float32"), ("KV", 48, "int32"), ("OF", 64, "int32"), ("sm", 256, "float32"), ("sb", 32, "bfloat16"),
+        ("src", 32, "float32"), ("su", 128, "uint16"), ("Dq", 256, "bfloat16"), ("gt", 256, "bfloat16"), ("Dp", 512, "bfloat16"),
+        ("Ap", 512, "bfloat16"), ("Dl", 256, "bfloat16"), ("cl", 512, "bfloat16"), ("tb", 256, "bfloat16"), ("cq", 512, "bfloat16"),
+        ("msk", 256, "float32"), ("L3", 256, "float32"), ("md", 256, "float32"), ("crep", 256, "float32"), ("eq", 256, "bfloat16"),
+        ("eq2", 256, "bfloat16"), ("sc", 256, "float32"), ("gr", 256, "bfloat16"),
+        ("RF", 256, "float32"), ("SF", 256, "float32"), ("F0", 256, "float32"), ("F2", 256, "float32"), ("F3", 256, "float32"),
+        ("F4", 256, "float32"), ("F5", 256, "float32"), ("F6", 256, "float32"), ("F8", 256, "float32"), ("fb", 256, "bfloat16"),
+        ("ys2", 256, "float32")):
     SCRATCH[_n] = ("sbuf", [128, _w], _d)
 for _t in range(TS + 1):
-    SCRATCH["RU%d" % _t] = ("sbuf", [128, 288], "uint16")
     SCRATCH["AW%d" % _t] = ("sbuf", [128, 2 * AWW], "bfloat16")
 for _t in range(TS):
-    SCRATCH["SR%d" % _t] = ("sbuf", [128, 288], "uint16")
+    SCRATCH["RU%d" % _t] = ("sbuf", [128, 256], "uint16")
     SCRATCH["SA%d" % _t] = ("sbuf", [128, 288], "bfloat16")
-for _b in ("PS0", "PS1", "PE0", "PE1", "PR0", "PR1", "PV0", "PV1"):
+for _t in range(TS - 1):
+    SCRATCH["SR%d" % _t] = ("sbuf", [128, 256], "uint16")
+for _b in ("PA0", "PA1", "PB0", "PB1", "PC0", "PC1", "PV0", "PV1"):
     SCRATCH[_b] = ("psum", [128, 512], "float32")
 
-SEMAPHORES = (["c_dve", "c_act", "c_pe", "c_pool", "sent", "d_x", "d_l", "d_a", "d_w", "d_s", "o_x", "o_r", "o_r2", "o_a", "o_s"]
+SEMAPHORES = (["c_dve", "c_act", "c_pe", "c_pool", "sent", "d_x", "d_l", "d_l2", "d_a", "d_w", "d_s", "o_x"]
+              + ["o_%s%d" % (k, b) for k in "rtas" for b in range(2)]
               + ["a%s%d_%d" % (k, t, b) for k in "ra" for t in range(TS) for b in range(2)])
 
 CYC, PCYC, GC, SC = 0.86, 0.5, 1.56, 3.8
-LAT_SAME, LAT_X, LAT_R = 180.0, 250.0, 4000.0
+LAT_SAME, LAT_X = 180.0, 250.0
 OVH, MINC, POV = 10.0, 64.0, 8.0
-WOVEN = {"K1": 3, "su": 2, "F2": 2, "F3": 2, "F4": 2, "F5": 2}
+WOVEN = {"KA": 3, "su": 2, "F2": 2, "F3": 2, "F4": 2, "F5": 2}
+BIG = 262144.0
+ODD, EVEN = [(0, 32, 40), (96, 120, 72), (120, 128, 32)], [(32, 64, 0), (64, 96, 96)]
 OP = AluOpType
 AF = ActivationFunctionType
 
 
 def arrange(ops):
     n = len(ops)
-    pri = [o["pri"] + 100.0 * ORDER.get(o.get("key"), 0) for o in ops]
-    left = [len(o["deps"]) for o in ops]
-    rdy = [0.0] * n
-    free = {"arr": 0.0, "dve": 0.0, "act": 0.0, "pe": 0.0, "pool": 0.0, "sp": 0.0}
-    ready = [k for k in range(n) if left[k] == 0]
-    order = []
-    while ready:
-        st = {k: max(rdy[k], free[ops[k]["eng"]]) for k in ready}
-        k0 = min(ready, key=lambda j: (st[j], -pri[j], j))
-        lim = st[k0] + min(CFG["WIN"], 0.6 * ops[k0]["cost"])
-        k = max([j for j in ready if ops[j]["eng"] == ops[k0]["eng"] and st[j] <= lim], key=lambda j: (pri[j], -j))
-        ready.remove(k)
-        o = ops[k]
-        if o["eng"] != "arr":
-            free[o["eng"]] = st[k] + o["cost"]
-        o["t0"] = st[k]
-        order.append(k)
+    pred = [[] for _ in range(n)]
+    for k, o in enumerate(ops):
         for (s, e) in o["succ"]:
-            rdy[s] = max(rdy[s], st[k] + o["cost"] + e)
-            left[s] -= 1
-            if left[s] == 0:
-                ready.append(s)
-    return order
+            pred[s].append((k, e))
+
+    def sweep(pri, nxt, prv, head):
+        left = [len(p) for p in prv]
+        rdy = list(head)
+        free = {"arr": 0.0, "dve": 0.0, "act": 0.0, "pe": 0.0, "pool": 0.0, "sp": 0.0}
+        ready = [k for k in range(n) if left[k] == 0]
+        order, t0 = [], [0.0] * n
+        while ready:
+            st = {k: max(rdy[k], free[ops[k]["eng"]]) for k in ready}
+            k0 = min(ready, key=lambda j: (st[j], -pri[j], j))
+            lim = st[k0] + min(CFG["WIN"], 0.6 * ops[k0]["cost"])
+            k = max([j for j in ready if ops[j]["eng"] == ops[k0]["eng"] and st[j] <= lim], key=lambda j: (pri[j], -j))
+            ready.remove(k)
+            o = ops[k]
+            if o["eng"] != "arr":
+                free[o["eng"]] = st[k] + o["cost"]
+            t0[k] = st[k]
+            order.append(k)
+            for (s, e) in nxt[k]:
+                rdy[s] = max(rdy[s], st[k] + o["cost"] + e)
+                left[s] -= 1
+                if left[s] == 0:
+                    ready.append(s)
+        return order, t0
+    succ = [o["succ"] for o in ops]
+    bias = [100.0 * ORDER.get(o.get("key"), 0) for o in ops]
+    pri = [o["pri"] + bias[k] for k, o in enumerate(ops)]
+    best = None
+    for _ in range(CFG["TURNS"] + 1):
+        order, t0 = sweep(pri, succ, pred, [0.0] * n)
+        end = max(t0[k] + o["cost"] + o["lat"] for k, o in enumerate(ops))
+        if best is None or end < best[0]:
+            best = (end, order, t0)
+        if CFG["TURNS"]:
+            _, tb = sweep([t0[k] + o["cost"] for k, o in enumerate(ops)], pred, succ, [o["lat"] if not succ[k] else 0.0 for k, o in enumerate(ops)])
+            pri = [tb[k] + o["cost"] + o["first"] + bias[k] for k, o in enumerate(ops)]
+    for k, o in enumerate(ops):
+        o["t0"] = best[2][k]
+    return best[1]
 
 
 def rank_program(g, core, T, topo):
@@ -108,31 +133,25 @@ def rank_program(g, core, T, topo):
     def add(eng, fn, reads, writes, cost, sem=None, cnt=0, lat=0.0, after=()):
         k = len(ops)
         deps = set(after)
-        soft = set()
         for regs, isw in ((reads, False), (writes, True)):
             for (nm, a, b) in regs:
                 ps = SCRATCH[nm][0] == "psum"
                 for (j, e2, a2, b2, w2) in hist.setdefault(nm, []):
                     if ps and (e2 != eng or eng == "pe"):
                         deps.add(j)
-                    elif isw and w2 and nm in WOVEN and e2 == eng and j >= k - 4 and (a - a2) % WOVEN[nm] and abs(a - a2) < WOVEN[nm]:
+                    elif isw and w2 and e2 == eng and j >= k - 4 and (a - a2) % WOVEN.get(nm, 3 if ps else 1) and abs(a - a2) < WOVEN.get(nm, 3):
                         continue
                     elif (isw or w2) and a < b2 and a2 < b:
-                        if isw and e2 == eng and ops[j]["sem"] is None and sem is None and not CFG["WAW"]:
-                            soft.add(j)
-                        else:
-                            deps.add(j)
+                        deps.add(j)
         for regs, isw in ((reads, False), (writes, True)):
             for (nm, a, b) in regs:
                 hist[nm].append((k, eng, a, b, isw))
         deps.discard(k)
-        soft -= deps
-        deps |= soft
-        ops.append({"soft": soft, "w": writes[0] if writes else ("-", 0, 0), "eng": eng, "fn": fn, "deps": deps, "cost": cost, "sem": sem, "cnt": cnt, "lat": lat})
+        ops.append({"w": writes[0] if writes else ("-", 0, 0), "eng": eng, "fn": fn, "deps": deps, "cost": cost, "sem": sem, "cnt": cnt, "lat": lat})
         return k
 
     def two(*vs):
-        return all(v[3] in ("bfloat16", "uint16") for v in vs)
+        return all(v[3] in ("bfloat16", "uint16", "float16") for v in vs)
 
     def vcost(n, f):
         if f in (GC, SC):
@@ -163,6 +182,13 @@ def rank_program(g, core, T, topo):
             return add("dve", lambda: g.vector.tensor_scalar(o[0], a[0], x1, None, op0), rd, o[1], vcost(o[2], f))
         return add("dve", lambda: g.vector.tensor_scalar(o[0], a[0], x1, x2, op0, op1), rd, o[1], vcost(o[2], f))
 
+    def pick(o, i):
+        pk = V("PK")
+        return add("dve", lambda: g.vector.tensor_tensor_scan(o[0], pk[0], i[0], 0.0, OP.add, OP.max), i[1] + pk[1], o[1], vcost(o[2], 1.0))
+
+    def turn(o, i):
+        return add("dve", lambda: g.vector.transpose(o[0], i[0]), i[1], o[1], vcost(o[2], 1.0))
+
     def ms(o, val):
         return add("dve", lambda: g.vector.memset(o[0], val), [], o[1], vcost(o[2], 1.0))
 
@@ -186,382 +212,412 @@ def rank_program(g, core, T, topo):
             return last
         return add("pe", fn, rd, wr, cost)
 
+    def group(its, start=True, stop=True):
+        for i, (o, l, r) in enumerate(its):
+            mm([(o, l, r, start and i == 0, stop and i == len(its) - 1)])
+
     def fold(o, wname, src, a, n, first, last):
-        its = []
-        for x in range(16):
-            l = V("TRI", 128 * x, 128 * x + 128) if wname == "TRI" else V(wname, 15 - x, 143 - x)
-            its.append((o, l, V(src, a + x, a + 16 * n, 16), first and x == 0, last and x == 15))
-        return mm(its)
+        return mm([(o, V(wname, 15 - x, 143 - x), V(src, a + x, a + 16 * n, 16), first and x == 0, last and x == 15) for x in range(16)])
 
     def iota(o, pat, base, cm, after=()):
         if o[3] == "int32":
             return add("pool", lambda: g.iota(o[0], pat, base, cm), [], o[1], 130.0 + 2 * o[2] * CYC, after=after)
         return add("pool", lambda: g.iota(o[0], pat, base, cm, allow_small_or_imprecise_dtypes=True), [], o[1], 130.0 + 2 * o[2] * CYC, after=after)
 
-    def dma(eng, pairs, reads, writes, sem, lat):
+    def dma(eng, pairs, reads, writes, sem, lat, after=()):
         def fn():
             for (o, i) in pairs:
                 Q[eng].dma_start(o, i).then_inc(T.sem[sem], 16)
             return None
-        return add(eng, fn, reads, writes, 60.0 * len(pairs), sem, 16 * len(pairs), lat)
+        return add(eng, fn, reads, writes, 60.0 * len(pairs), sem, 16 * len(pairs), lat, after)
 
-    dma("sp", [(T.X[:, 0:W], T.xt[:])], [], [("X", 0, W)], "d_x", 6500.0)
     pieces = [(gh, b, gl) for gh in range(4) for b in range(2) for gl in range(2)]
-    dma("act", [(T.L[32 * gh + 16 * b:32 * gh + 16 * b + 16, 128 * gl:128 * gl + 128],
-                 T.rl[32 * gh + 16 * gl:32 * gh + 16 * gl + 16, 128 * b:128 * b + 128]) for (gh, b, gl) in pieces],
-        [], [("L", 0, 256)], "d_l", 2500.0)
+    lp = [(T.L[32 * gh + 16 * b:32 * gh + 16 * b + 16, 128 * gl:128 * gl + 128],
+           T.rl[32 * gh + 16 * gl:32 * gh + 16 * gl + 16, 128 * b:128 * b + 128]) for (gh, b, gl) in pieces]
+    k1 = dma("act", lp[:10], [], [], "d_l", 2500.0)
+    k2 = dma("sp", lp[10:], [], [], "d_l2", 2500.0)
+    dma("sp", [(T.X[:, 0:W], T.xt[:])], [], [("X", 0, W)], "d_x", 5000.0)
     ms(V("sgi"), 0)
-    dma("sp", [(T.sgi[0:128:16, :], T.sg[:])], [], [("sgi", 0, 256)], "d_s", 2500.0)
-    dma("sp", [(T.wti[:, 0:1], T.wt[:])], [], [("wti", 0, 8)], "d_w", 2500.0)
-    dma("sp", [(T.AW0[:, AWW * b + 16:AWW * b + 144], T.av[:, 128 * b:128 * b + 128]) for b in range(2)], [],
+    dma("act", [(T.wti[:, 0:1], T.wt[:])], [], [("wti", 0, 8)], "d_w", 2500.0)
+    dma("act", [(T.AW0[:, AWW * b + 16:AWW * b + 144], T.av[:, 128 * b:128 * b + 128]) for b in range(2)], [],
         [("AW0", 16, 144), ("AW0", AWW + 16, AWW + 144)], "d_a", 2500.0)
+    dma("sp", [(T.sgi[0:128:16, :], T.sg[:])], [], [("sgi", 0, 256)], "d_s", 2500.0)
+    hist["L"] = [(k1, "act", 0, 256, True), (k2, "sp", 0, 256, True)]
 
     io = [iota(V("pi", 0, 1), [[0, 1]], 0, 1),
-          iota(V("COL"), [[1, 144]], 0, 0),
           iota(V("ci", 0, 16), [[16, 8], [128, 2]], 0, 0),
-          iota(V("ci", 16, 34), [[0, 2], [2, 9]], 0, 0),
-          iota(V("ci", 40, 58), [[16, 2], [0, 9]], 0, 0),
-          iota(V("COLX"), [[0, 16], [1, 16]], 0, 0),
-          iota(V("ci", 64, 80), [[8, 16]], 0, 0),
-          iota(V("ci", 80, 96), [[16, 2], [32, 8]], 0, 0),
-          iota(V("COLG"), [[16, 8], [0, 16]], 0, 0),
-          iota(V("PAR"), [[0, 9], [1, 2], [0, 8]], 0, 0),
-          iota(V("ci", 112, 128), [[16, 8], [128, 2]], 0, 0)]
+          iota(V("ci", 16, 24), [[16, 2], [-1, 2], [4, 2]], 1, 0),
+          iota(V("ci", 24, 32), [[16, 2], [1, 2], [4, 2]], 8, 0),
+          iota(V("COL"), [[1, 144]], 0, 0),
+          iota(V("ci", 32, 40), [[1, 8]], 0, 0),
+          iota(V("ci", 40, 48), [[2, 4], [0, 2]], 0, 0),
+          iota(V("ci", 48, 56), [[16, 4], [64, 2]], 0, 0),
+          iota(V("ci", 56, 64), [[16, 2], [32, 4]], 0, 0),
+          iota(V("COLX"), [[0, 8], [1, 16]], 0, 0),
+          iota(V("COLG"), [[16, 8], [0, 16]], 0, 0)]
     iota(V("IOTA"), [[1, WX]], 0, 0, after=io)
-    ms(V("X", W, WX), 0.0)
-    ms(V("ONE"), 1.0)
     P = V("pi", 0, 1)
     ts(V("pv", 0, 1), P, 15, OP.bitwise_and)
     ts(V("pv", 1, 2), P, 112, OP.bitwise_and)
     ts(V("pv", 2, 3), P, 7, OP.bitwise_and)
-    ts(V("pv", 3, 4), P, 3, OP.logical_shift_right, 1, OP.bitwise_and)
-    ts(V("pv", 4, 5), P, 1, OP.bitwise_and)
-    ts(V("pv", 5, 6), P, 1, OP.logical_shift_right, 7, OP.bitwise_and)
-    cp(V("pf", 0, 6), V("pv", 0, 6))
+    ts(V("pv", 3, 4), P, 2, OP.logical_shift_right, 2, OP.bitwise_and)
+    cp(V("pf", 0, 4), V("pv", 0, 4))
     cp(V("pf", 6, 7), P)
-    xf, g16, y3, k0, pff = V("pf", 0, 1), V("pf", 1, 2), V("pf", 2, 3), V("pf", 3, 4), V("pf", 6, 7)
+    xf, g16, y3, k2f, pff = V("pf", 0, 1), V("pf", 1, 2), V("pf", 2, 3), V("pf", 3, 4), V("pf", 6, 7)
+    ts(V("cu", 0, 16), V("ci", 0, 16), xf, OP.add)
+    ts(V("pf", 4, 5), y3, 32.0, OP.mult, k2f, OP.add)
+    for b in (1, 0):
+        for a in range(2):
+            ts(V("cu", 16 + 8 * b + 4 * a, 20 + 8 * b + 4 * a), V("ci", 16 + 8 * a + 4 * b, 20 + 8 * a + 4 * b), V("pf", 4, 5), OP.add)
+    ts(V("cu", 32, 40), V("ci", 32, 40), 0.0, OP.mult, y3, OP.add)
+    cp(V("cu", 40, 48), V("ci", 32, 40))
+    cp(V("cu", 48, 56), V("ci", 40, 48))
+    ms(V("cu", 48, 56, 2), 8)
+    ts(V("cu", 56, 64), V("ci", 48, 56), xf, OP.add)
+    ts(V("cu", 64, 72), V("ci", 56, 64), xf, OP.add)
+    P1, BX, BY, BE, P3, P4 = V("cu", 0, 16), V("cu", 32, 40), V("cu", 40, 48), V("cu", 48, 56), V("cu", 56, 64), V("cu", 64, 72)
     ts(V("pf", 7, 8), g16, 15.0, OP.add)
     ts(V("pf", 8, 9), xf, float(W), OP.add)
-    ts(V("pf", 9, 10), xf, -1.0, OP.mult, -float(W), OP.add)
-    DUM, NDUM = V("pf", 8, 9), V("pf", 9, 10)
-    ts(V("pf", 10, 11), y3, 32.0, OP.mult)
-    ms(V("pf", 12, 13), 4088.0)
-    B4088 = V("pf", 12, 13)
-    ms(V("pf", 14, 15), -0.5)
-    ms(V("pf", 15, 16), -2.0)
-    ms(V("wtf", 4, 5), -8.0)
-    CMH, CM2, CM8 = V("pf", 14, 15), V("pf", 15, 16), V("wtf", 4, 5)
-    ts(V("cu", 0, 16), V("ci", 0, 16), xf, OP.add)
-    for j, one in ((0, 0.0), (1, 1.0)):
-        a = 24 * j
-        ts(V("cj", a, a + 18), V("ci", 16, 34), k0, OP.add, one, OP.add)
-        ts(V("cj", 48 + a, 66 + a), V("cj", a, a + 18), 15, OP.bitwise_and)
-        tt(V("cj", a, a + 18), V("cj", 48 + a, 66 + a), V("ci", 40, 58), OP.add)
-        ts(V("cu", 16 + 18 * j, 34 + 18 * j), V("cj", a, a + 18), V("pf", 10, 11), OP.add)
-    ts(V("cu", 52, 70), V("ci", 40, 58), 0.5, OP.mult, y3, OP.add)
-    ts(V("cu", 70, 86), V("ci", 112, 128), xf, OP.add)
-    ts(V("cu", 86, 102), V("ci", 80, 96), xf, OP.add)
-    ts(V("cu", 102, 118), V("ci", 64, 80), 0.125, OP.mult)
-    ts(V("cu", 118, 128), V("ci", 64, 74), 0.0, OP.mult, y3, OP.add)
-    ts(V("cu", 128, 136), V("ci", 64, 72), 0.125, OP.mult)
-    P1, P2, P2b, BN, P3, P4, P5 = (V("cu", 0, 16), V("cu", 16, 34), V("cu", 34, 52), V("cu", 52, 70), V("cu", 70, 86),
-                                   V("cu", 86, 102), V("cu", 102, 118))
-    BX, BX9, BY = V("cu", 118, 126), V("cu", 118, 127), V("cu", 128, 136)
+    ts(V("pf", 9, 10), xf, float(W + 16), OP.add)
+    ts(V("pf", 10, 11), xf, 14.5, OP.is_lt, BIG, OP.mult)
+    ts(V("pf", 11, 12), V("pf", 10, 11), 7.5, OP.add)
     ts(V("pf", 13, 14), xf, 16.0, OP.add)
-    ts(V("cb"), V("ci", 64, 72), 2.0, OP.mult, V("pf", 13, 14), OP.add)
+    ts(V("pf", 14, 15), xf, 1.0, OP.add)
+    DUM, DUM2, HELD, HELD8 = V("pf", 8, 9), V("pf", 9, 10), V("pf", 10, 11), V("pf", 11, 12)
+    for j, val in enumerate((0.998, -1.0, -2.0, -8.0, -32.0, 255.0 / 512)):
+        ms(V("pf", 16 + j, 17 + j), val)
+    CVO, CM1, CM2, CM8, CM32, CZP = (V("pf", 16 + j, 17 + j) for j in range(6))
+    ms(V("X", W, WX), 0.0)
+    ms(V("ONE"), 1.0)
+    ms(V("M4"), -4096.0)
+    ms(V("CZ"), -255.0 / 512)
+    ms(V("src"), -1.0)
+    ts(V("cb"), V("ci", 32, 40), 16.0, OP.mult, V("pf", 13, 14), OP.add)
     C128 = V("COL", 0, 128)
     ts(V("BW"), V("COL"), V("pf", 7, 8), OP.is_equal)
-    cp(V("wtf", 0, 1), V("wti", 0, 1))
-    ts(V("WU"), V("BW"), V("wtf", 0, 1), OP.mult, 16.0, OP.mult)
-    for nm, f in (("If", 1.0), ("NIf", -1.0), ("I4", 4096.0), ("I", 1.0), ("NI", -1.0), ("IA", 2048.0), ("NIA", -2048.0),
-                  ("IB", 16777216.0), ("IC", 256.0), ("ID", 2040.0), ("IE", 16711680.0), ("I8", 8192.0), ("NI8", -8192.0)):
-        ts(V(nm), C128, pff, OP.is_equal, f, OP.mult)
+    cp(V("pf", 23, 24), V("wti", 0, 1))
+    ts(V("WU"), V("BW"), V("pf", 23, 24), OP.mult, 32.0, OP.mult)
+    ds = 1.0 / 256
+    h16 = CFG["H16"]
+    RH = "Rh" if h16 else "Rf"
+    ts(V("I"), C128, pff, OP.is_equal)
+    for nm, f in (("If", 1.0), ("Id", ds), ("NId", -ds), ("IR", 1.0), ("NI", -1.0), ("IA", 2048.0), ("NIA", -2048.0), ("IB", 33554432.0),
+                  ("NIB", -33554432.0), ("IC", 256.0), ("IE", 16711680.0), ("I8", 8192.0), ("Ih", 8.0), ("NIh", -8.0)):
+        ts(V(nm), V("I"), f, OP.mult)
+    ms(V("CP"), 2048.0 * h16)
+    for a, e in ((0, 32), (96, 128), (160, 224)):
+        ms(V("CP", a, e), 2048.0 * h16 + 2048.0)
     ts(V("WE"), V("BW"), -8192.0, OP.mult)
-    ts(V("NBW"), V("BW"), -1.0, OP.mult)
-    ts(V("BW8"), V("BW"), 8192.0, OP.mult)
-    ts(V("cu", 136, 140), V("ci", 64, 68), 0.25, OP.mult)
-    BE = V("cu", 136, 140)
-    ts(V("dm2", 0, 1), DUM, 16.0, OP.add)
-    ts(V("SX"), V("COLX", 0, 128), xf, OP.is_equal, 16.0, OP.mult)
-    ts(V("trs"), V("COL", 0, 16), xf, OP.is_gt, 8192.0, OP.mult)
-    for x in range(16):
-        ts(V("TRI", 128 * x, 128 * x + 128), V("BW", 15 - x, 143 - x), V("trs", x, x + 1), OP.mult)
+    ts(V("SX"), V("COLX"), xf, OP.is_equal, 32.0, OP.mult)
     ts(V("BO"), V("COLG"), g16, OP.is_equal)
+    ts(V("BO8"), V("BO"), 8192.0, OP.mult)
     ts(V("DG"), V("COLX"), xf, OP.is_equal)
-    ts(V("PAR"), V("PAR"), 0.25, OP.mult)
+    t1, t2 = V("F2", 0, 128), V("F3", 0, 128)
+    ts(t1, V("COLX"), xf, OP.is_gt)
+    tt(t2, t1, V("DG"), OP.subtract)
+    tt(V("TRI"), t2, V("BO8"), OP.mult)
+    ts(t2, V("COLX"), V("pf", 14, 15), OP.is_equal, BIG, OP.mult)
+    ts(t1, t1, 2 * BIG, OP.mult, -2 * BIG, OP.add)
+    tt(V("PK"), t1, t2, OP.add)
     for b in range(2):
         ms(V("AW0", AWW * b, AWW * b + 16), 0.0)
         for t in range(TS):
             ms(V("SA%d" % t, 144 * b + 8, 144 * b + 16), 0.0)
 
     cp(V("L1"), IND(V("L"), P1))
-    add("dve", lambda: g.vector.transpose(T.L2[:], T.L1[:]), [("L1", 0, 256)], [("L2", 0, 256)], vcost(256, 1.0))
+    turn(V("L2"), V("L1"))
+    for b in (1, 0):
+        cp(V("RU0", 128 * b, 128 * b + 128), IND(V("L2"), V("cu", 16 + 8 * b, 24 + 8 * b)))
     ts(V("sgb"), V("sgi"), 0.0, OP.is_lt)
-    fold(V("PE0", 0, 16), "BW", "sgb", 0, 16, True, True)
-    cp(V("ng"), V("PE0", 0, 16))
-    cp(V("msk"), IND(V("ng"), BN))
-    ts(V("md"), V("msk"), -1.0, OP.mult, 1.0, OP.add)
-    tt(V("L4"), IND(V("L2"), P2b), V("msk"), OP.mult)
-    tt(V("L5"), IND(V("L2"), P2), V("md"), OP.mult)
-    for c in (144, 0):
-        tt(V("L6", c, c + 144), V("L5", c, c + 144), V("L4", c, c + 144), OP.add)
-        cp(V("RU0", c, c + 144), V("L6", c, c + 144))
+    fold(V("PV0", 0, 16), "BW", "sgb", 0, 16, True, True)
+    cp(V("ng", 0, 16), V("PV0", 0, 16))
+    ts(V("ng", 16, 32), V("ng", 0, 16), 1.0 / ds, OP.mult)
 
     XW = V("X")
     nv = [0]
     lead = []
     steps = []
     for t in range(TS):
-        RU, AW, SR, SA = "RU%d" % t, "AW%d" % t, "SR%d" % t, "SA%d" % t
+        RU, AW, SA = "RU%d" % t, "AW%d" % t, "SA%d" % t
+        SR, RN = ("SR%d" % t, "RU%d" % (t + 1)) if t < TS - 1 else ("SF", "RF")
         sends = []
         step0 = len(ops)
         for hi, b in enumerate((1, 0)):
-            def H(nm, a=0, e=128, s=1, other=None, b=b):
-                nm = other or nm
+            def H(nm, a=0, e=128, s=1, b=b):
                 w = SCRATCH[nm][1][1] // 2
                 return V(nm, w * b + a, w * b + e, s)
 
             def S(j, b=b):
                 return V("sm", 128 * b + 8 * j, 128 * b + 8 * j + 8)
+
+            def own(c, l, spans):
+                return [(V(PB, c + a, c + e), V(l), H(RH, a, e)) for (a, e) in spans]
+
+            def ahead(c, l, spans):
+                return [(V(PB, c + a, c + e), V(l), H(RH, f, f + e - a)) for (a, e, f) in spans]
             first = len(ops)
-            PS, PE, PR = "PS%d" % b, "PE%d" % b, "PR%d" % b
+            PA, PB, PC = "PA%d" % b, "PB%d" % b, "PC%d" % b
             A, A2 = H(AW, 16, 144), H(AW, 16, 272)
-            PD = V(PR, 144, 272)
-            cp(H("Rf", 0, 144), H(RU, 0, 144))
+            PD, PZ = V(PB, 0, 128), V(PB, 128, 256)
+            rfa = CFG["RFA"][hi] and t > 0
+            RM = H("PP", 0, 128) if rfa else H("Rf")
+            if t == 0:
+                act(H("Rf"), IND(V("L2"), V("cu", 16 + 8 * b, 24 + 8 * b)), AF.Copy)
+            elif not rfa:
+                cp(H("Rf"), H(RU))
+            if h16:
+                ts(H("Rh"), H(RU), -2048.0, OP.add)
             act(H(AW, 144, 272), A, AF.Copy)
-            mm([(V(PR, 272, 400), V("If"), H("Rf", 8, 136), True, False), (V(PR, 272, 400), V("NIf"), H("Rf"), False, True)])
-            act(H("wr"), V(PR, 272, 400), AF.Sign)
-            mm([(PD, V("If"), H("Rf", 8, 136), True, False), (PD, V("NIf"), H("Rf"), False, False),
-                (PD, V("NIA"), H("wr"), False, False), (PD, V("IA"), V("ONE"), False, True),
-                (V(PR, 0, 136), V("I4"), H("Rf", 0, 136), True, True)])
-            rd = CFG["REF_DVE"][hi]
-            for a0, r in zip((0, 8), rd):
-                cuts = sorted(set([a0, a0 + 8 - r, a0 + 8] + ([a0 + 4] if r in (0, 8) else [])))
-                for a, e in zip(cuts[:-1], cuts[1:]):
-                    src = IND(XW, H(RU, 8 * a, 8 * e))
-                    if a >= a0 + 8 - r:
-                        cp(H("G", 128 * a, 128 * e), src)
-                    else:
-                        act(H("G", 128 * a, 128 * e), src, AF.Copy)
-            if t > 0:
-                act(H("gr"), IND(H(AW, 0, 16), BX), AF.Copy)
-                mm([(V(PE, 256, 384), V("SX"), H("gr"), True, True)])
-            fold(V(PS, 0, 64), "WU", "G", 2048 * b, 64, True, True)
-            if CFG["SPLIT"][hi]:
-                fold(V("PV1", 0, 72), "WU", "G", 2048 * b + 896, 72, True, True)
-                parts = ((0, 64, 0, 56, PS, 0), (64, 128, 56, 128, "PV1", -56))
-            else:
-                fold(V(PS, 64, 128), "WU", "G", 2048 * b + 1024, 64, True, True)
-                parts = ((0, 128, 0, 128, PS, 0),)
-            for (s0, s1, a, e, bank, sh) in parts:
-                cp(H("si", s0, s1), V(bank, s0 + sh, s1 + sh))
-                ts(H("u", s0, s1), H("si", s0, s1), 4, OP.logical_shift_right, 4095, OP.bitwise_and)
-                if s0 == 0:
-                    ts(H("u", 128, 136), H("si", 0, 8), 4, OP.logical_shift_right, 4095, OP.bitwise_and)
-                tt(H("pr", a, e), H("u", a, e), H("u", a + 8, e + 8), OP.mult)
-                ts(H("p16", a, e), H("pr", a, e), 1, OP.logical_shift_right, 4080, OP.bitwise_and)
-                npar = t > 0 and CFG["NPAR"][hi]
-                SN = V(bank, a + sh, e + sh)
-                if npar:
-                    tt(H("z", a, e), H("si", a, e), V(PE, 256 + a, 256 + e), OP.add)
-                    SN = H("z", a, e)
-                tt(H("tt", a, e), H("p16", a, e), SN, OP.add)
-                if t > 0 and not npar:
-                    tt(H("pr", a, e), H("tt", a, e), V(PE, 256 + a, 256 + e), OP.add)
-                    ts(H("h", a, e), H("pr", a, e), 4080, OP.bitwise_and)
+            group(own(256, "NId", [(0, 128)]) + ahead(256, "Id", ODD + EVEN))
+            act(H("wr"), V(PB, 256, 384), AF.Sign)
+            if t == 0:
+                act(H("ngb"), IND(V("ng", 16 + 8 * b, 24 + 8 * b), BX), AF.Copy)
+                tt(H("L3"), H("ngb"), V(PB, 256, 384), OP.mult)
+                tt(H("Rt"), H("L3"), H("Rf"), OP.add)
+                RM = H("Rt")
+            group(own(128, "IR", [(0, 128)]) + ([(PZ, V("IA"), V("ONE"))] if h16 else []) + [(PZ, V("I"), V("CZ"))])
+            group(own(0, "NId", [(0, 128)]) + ahead(0, "Id", ODD + EVEN)
+                  + [(PD, V("Ih"), V("ONE")), (PD, V("NIh"), H("wr"))])
+            group([(V(PB, 256, 512), V("I"), V("CP"))]
+                  + own(256, "IR", [(32, 96)]) + ahead(256, "IR", ODD) + own(384, "IR", [(0, 32), (96, 128)]) + ahead(384, "IR", EVEN)
+                  + [(V(PB, 256 + a, 256 + e), V("NIA"), H("wr", a % 128, (e - 1) % 128 + 1)) for a, e in ((0, 32), (96, 128), (160, 224))])
+            act(H("PP", 128, 384), V(PB, 256, 512), AF.Copy)
+            if rfa:
+                act(H("PP", 0, 128), PZ, AF.Identity, CZP)
+            for (a, e, eng) in CFG["REF"][hi]:
+                src = IND(XW, H(RU, 8 * a, 8 * e))
+                if eng == "d":
+                    cp(H("G", 128 * a, 128 * e), src)
                 else:
-                    ts(H("h", a, e), H("tt", a, e), 4080, OP.bitwise_and)
-                tt(H("dh", a, e), H("h", a, e), V(PR, 144 + a, 144 + e), OP.mult)
-                tt(H("z", a, e), H("dh", a, e), V(PR, a, e), OP.add)
-                ts(H("q", a, e), H("z", a, e), 12, OP.logical_shift_right, 4095, OP.bitwise_and)
+                    act(H("G", 128 * a, 128 * e), src, AF.Copy)
+            if t > 0:
+                act(H("gr", 0, 64), IND(H(AW, 0, 16), V("cu", 32, 36)), AF.Identity, CM32)
+                mm([(V(PB, 256, 320), V("SX"), H("gr", 0, 64), True, True)])
+            EP = (V(PA, 128, 192), V(PC, 128, 192))
+            for part, (bank, wide) in enumerate(((PA, 72), (PC, 64))):
+                a, e = 64 * part, 64 * part + 64
+                fold(V(bank, 0, wide), "WU", "G", 2048 * b + 1024 * part, wide, True, True)
+                cp(H("si", 72 * part, 72 * part + wide), V(bank, 0, wide))
+                if part == 0:
+                    ts(H("u", 0, 72), H("si", 0, 72), 5, OP.logical_shift_right, 4095, OP.bitwise_and)
+                else:
+                    ts(H("u", 72, 128), H("si", 80, 136), 5, OP.logical_shift_right, 4095, OP.bitwise_and)
+                low = H("p16", a, e)
+                ts(low, H("si", 72 * part, 72 * part + 64), 8191, OP.bitwise_and)
+                if t > 0:
+                    low = H("pr", a, e)
+                    tt(low, H("p16", a, e), V(PB, 256, 320), OP.add)
+                for (c0, c1, f) in ODD + EVEN:
+                    if a <= c0 < e:
+                        tt(V(bank, c0 - a, c1 - a), H("u", c0, c1), H("u", f, f + c1 - c0), OP.mult)
+                tt(H("tt", a, e), low, V(bank, 0, 64), OP.add)
+                ts(H("h", a, e), H("tt", a, e), 5, OP.arith_shift_right, 255, OP.bitwise_and)
+                tt(H("dh", a, e), H("h", a, e), V(PB, a, e), OP.mult)
+                tt(H("z", a, e), H("dh", a, e), V(PB, 128 + a, 128 + e), OP.add)
+                ts(H("q", a, e), H("z", a, e), 4095, OP.bitwise_and)
                 cp(H("QU", a, e), H("q", a, e))
-            act(H("vo"), H("dh"), AF.Sign, B4088, -1.0)
-            ts(H("oh"), H("z"), 12, OP.logical_shift_right)
-            mm([(V(PE, 0, 128), V("IB"), H("vo"), True, False), (V(PE, 0, 128), V("IB"), V("ONE"), False, False),
-                (V(PE, 0, 128), V("IE"), V("ONE"), False, False)])
-            pa = CFG["PROBE_ACT"][hi]
-            for a in range(0, 16, 4):
-                c0, c1 = 128 * a, 128 * a + 512
-                if a < pa:
+            act(H("vo"), H("dh"), AF.Sign, CVO, -1.0)
+            for part in range(2):
+                mm([(EP[part], V("IB"), H("vo", 64 * part, 64 * part + 64), True, False), (EP[part], V("IB"), V("ONE", 0, 64), False, False),
+                    (EP[part], V("IE"), V("ONE", 0, 64), False, False)])
+            m = 0
+            for kind in CFG["PROBE"][hi].split():
+                c0, c1 = 128 * m, 128 * m + 256 * len(kind)
+                if kind[0] == "a":
                     pv = "PV%d" % (nv[0] % 2)
                     nv[0] += 1
-                    act(H("Dd", c0, c1), IND(XW, H("QU", 8 * a, 8 * a + 32)), AF.Copy)
-                    mm([(V(pv), V("I"), H("Dd", c0, c1), True, False), (V(pv, 0, 256), V("NI"), A2, False, False),
-                        (V(pv, 256, 512), V("NI"), A2, False, True)])
-                    act(H("AB", c0, c1), V(pv), AF.Abs)
+                    act(H("Dd", c0, c1), IND(XW, H("QU", 8 * m, 8 * m + 16 * len(kind))), AF.Copy)
+                    mm([(V(pv, 0, c1 - c0), V("I"), H("Dd", c0, c1), True, False)]
+                       + [(V(pv, 256 * j, 256 * j + 256), V("NI"), A2, False, j == len(kind) - 1) for j in range(len(kind))])
+                    act(H("AB", c0, c1), V(pv, 0, c1 - c0), AF.Abs)
                 else:
-                    for m in (a, a + 2):
-                        tt(H("Dd", 128 * m, 128 * m + 256), IND(XW, H("QU", 8 * m, 8 * m + 16)), A2, OP.subtract)
-                        if a == 12:
-                            act(H("AB", 128 * m, 128 * m + 256), H("Dd", 128 * m, 128 * m + 256), AF.Abs)
-                    if a < 12:
-                        act(H("AB", c0, c1), H("Dd", c0, c1), AF.Abs)
-                if a % 8 == 4:
-                    fold(V(PE, 8 * (a - 4), 8 * (a + 4)), "WE", "AB", 2048 * b + 128 * (a - 4), 64, False, a == 12)
+                    for j in range(m, m + 2 * len(kind), 2):
+                        tt(H("Dd", 128 * j, 128 * j + 256), IND(XW, H("QU", 8 * j, 8 * j + 16)), A2, OP.subtract)
+                    act(H("AB", c0, c1), H("Dd", c0, c1), AF.Abs)
+                m += 2 * len(kind)
+                if m % 8 == 0:
+                    fold(EP[m // 8 - 1], "WE", "AB", 2048 * b + 128 * (m - 8), 64, False, True)
             tail = len(ops)
-            tt(H("mk"), H("oh"), V(PE, 0, 128), OP.add)
-            tt(H("K"), H("Rf"), V(PE, 0, 128), OP.add)
-            tt(H("K1", 0, 192, 3), H("mk", 0, 64), H("mk", 64, 128), OP.min)
-            tt(H("M1"), H("K"), PD, OP.add)
-            tt(H("K1", 1, 192, 3), H("K", 0, 64), H("K", 64, 128), OP.min)
-            tt(H("K1", 2, 192, 3), H("M1", 0, 64), H("M1", 64, 128), OP.min)
+            for j, (nm, c0) in enumerate((("z", 0), ("PP", 128), ("PP", 256))):
+                tt(H("KA", j, 192, 3), H(nm, c0, c0 + 64), EP[0], OP.add)
+            for j, (nm, c0) in enumerate((("z", 64), ("PP", 192), ("PP", 320))):
+                tt(V(PC, 192 + j, 384, 3), H(nm, c0, c0 + 64), EP[1], OP.add)
+            tt(H("K1", 0, 192), H("KA", 0, 192), V(PC, 192, 384), OP.min)
             tt(H("K2", 0, 96), H("K1", 0, 96), H("K1", 96, 192), OP.min)
             tt(H("K3", 0, 48), H("K2", 0, 48), H("K2", 48, 96), OP.min)
             tt(H("KV", 0, 24), H("K3", 0, 24), H("K3", 24, 48), OP.min)
             ts(H("OF", 0, 24), H("KV", 0, 24), 4095, OP.bitwise_and)
-            cp(H("su", 0, 8), H("OF", 0, 24, 3))
-            ts(H("OF", 24, 32), H("KV", 0, 24, 3), 13, OP.arith_shift_right)
-            negE, Rr, Rl, qs = H("OF", 24, 32), H("OF", 2, 24, 3), H("OF", 1, 24, 3), H("OF", 0, 24, 3)
-            qa, la = CFG["QACT"][hi], CFG["LACT"][hi]
-            DQ, DL = H("Dq"), H("Dl")
-            if qa == 3:
-                DQ = V(PS, 128, 256)
-                act(H("Dq"), IND(XW, H("su", 0, 8)), AF.Copy)
-                mm([(DQ, V("I"), H("Dq"), True, False), (DQ, V("NI"), A, False, True)])
-                act(H("gt"), DQ, AF.Sign, CMH)
+            for j in range(3):
+                cp(H("su", 8 * j, 8 * j + 8), H("OF", j, 24, 3))
+            ts(H("OF", 24, 32), H("KV", 0, 24, 3), -8192, OP.bitwise_and)
+            negE, qs, Rp, Rm = H("OF", 24, 32), H("OF", 0, 24, 3), H("OF", 1, 24, 3), H("OF", 2, 24, 3)
+            qa, la = CFG["QA"][hi], CFG["LA"][hi]
+            gtq = CFG["GTQ"][hi] and qa < 2
+            if gtq:
+                tt(H("Dq"), IND(XW, H("su", 0, 8)), A, OP.subtract)
+                ts(H("gt"), H("Dq"), 0.0, OP.is_gt)
             else:
                 tt(H("gt"), IND(XW, H("su", 0, 8)), A, OP.is_gt)
-                tt(H("Dq"), IND(XW, H("su", 0, 8)), A, OP.subtract)
-            fold(V(PE, 128, 136), "BW", "gt", 128 * b, 8, True, True)
-            tt(S(0), H("K3", 0, 24, 3), H("K3", 24, 48, 3), OP.is_lt)
-            tt(S(1), Rl, Rr, OP.subtract)
-            ts(S(2), V(PE, 128, 136), -0.5 if qa == 3 else 7.5, OP.is_ge)
-            if CFG["PRE"][hi]:
-                tt(S(11), S(0), S(1), OP.mult)
-                ts(S(12), S(0), 2.0, OP.mult, -1.0, OP.add)
-                tt(S(13), Rl, S(11), OP.subtract)
-                tt(S(3), S(12), S(1), OP.mult)
-                tt(S(4), S(2), S(3), OP.mult)
-                tt(S(5), S(4), S(13), OP.add)
+            if CFG["PMACT"][hi]:
+                act(H("Dp", 0, 256), IND(XW, H("su", 8, 24)), AF.Copy)
+                mm([(V(PB, 256, 512), V("I"), H("Dp", 0, 256), True, False), (V(PB, 256, 512), V("NI"), A2, False, True)])
+                act(H("Ap", 0, 256), V(PB, 256, 512), AF.Abs)
             else:
-                tt(S(3), S(2), S(0), OP.is_equal)
-                tt(S(4), S(3), S(1), OP.mult)
-                tt(S(5), S(4), Rr, OP.add)
-            cp(H("su", 8, 16), S(5))
-            if la == 3:
-                DL = V(PS, 264, 392)
-                act(H("Dl"), IND(XW, H("su", 8, 16)), AF.Copy)
-                mm([(DL, V("I"), H("Dl"), True, False), (DL, V("NI"), A, False, True)])
+                tt(H("Dp", 0, 256), IND(XW, H("su", 8, 24)), A2, OP.subtract)
+                act(H("Ap", 0, 256), H("Dp", 0, 256), AF.Abs)
+            sg = H("sb", 0, 8)
+            SG = sg
+            if t == 0:
+                SG = H("sb", 8, 16)
+            if CFG["CSCAN"][hi]:
+                mm([(V(PA, 192, 320), V("BO"), H("gt"), True, True)])
+                pick(H("sc"), V(PA, 192, 320))
+                ts(SG, H("sc", 15, 128, 16), HELD8, OP.is_ge)
             else:
-                tt(H("Dl"), IND(XW, H("su", 8, 16)), A, OP.subtract)
-            act(H("ABl"), DL, AF.Abs)
-            mm([(V(PE, 136, 144), V("ID"), V("ONE", 0, 8), True, False)])
-            fold(V(PE, 136, 144), "NBW", "ABl", 128 * b, 8, False, True)
-            tt(S(6), qs, S(5), OP.subtract)
-            if qa >= 2:
-                act(H("cq"), DQ, AF.Relu, CM2, -1.0)
-                act(H("r2"), DQ, AF.Relu, CM2)
-                mm([(V(PS, 0, 128), V("I"), H("Dq"), True, False)] + ([(V(PS, 0, 128), V("I"), A, False, False)] if qa == 2 else [])
-                   + [(V(PS, 0, 128), V("I"), H("cq"), False, False), (V(PS, 0, 128), V("NI"), H("r2"), False, True)])
-                act(H(AW, 272, 400), V(PS, 0, 128), AF.Copy)
-            elif qa == 1:
-                ts(H("cq"), H("Dq"), -2.0, OP.max, 2.0, OP.min)
-                mm([(V(PS, 0, 128), V("I"), A, True, False), (V(PS, 0, 128), V("I"), H("cq"), False, True)])
-                act(H(AW, 272, 400), V(PS, 0, 128), AF.Copy)
-            else:
-                ts(H("cq"), H("Dq"), -2.0, OP.max, 2.0, OP.min)
-                tt(H(AW, 272, 400), A, H("cq"), OP.add)
+                fold(V(PA, 192, 200), "BW", "gt", 128 * b, 8, True, True)
+                ts(SG, V(PA, 192, 200), 7.5, OP.is_ge)
+            if t == 0:
+                tt(sg, SG, V("ng", 8 * b, 8 * b + 8), OP.not_equal)
+            tt(S(0), Rp, Rm, OP.subtract)
+            tt(S(1), sg, S(0), OP.mult)
+            tt(S(2), S(1), Rm, OP.add)
+            col = S(2)
+            cp(H("su", 24, 32), col)
+            PM = V(PC, 384, 400)
+            mm([(PM, V("IE"), V("ONE", 0, 16), True, False), (PM, V("I"), V("M4"), False, False),
+                (V(PC, 384, 392), V("NIB"), V("ONE", 0, 8), False, False)])
+            fold(PM, "WE", "Ap", 256 * b, 16, False, False)
+            mm([(V(PC, 384, 392), V("IB"), sg, False, False), (V(PC, 392, 400), V("NIB"), sg, False, True)])
+            tt(S(3), V(PC, 384, 392), negE, OP.subtract)
+            tt(S(4), V(PC, 392, 400), negE, OP.subtract)
+            tt(S(5), S(3), S(4), OP.max)
+            src = H("src", 0, 8)
+            tt(src, S(5), col, OP.min)
             go = H(SA, 0, 8)
-            tt(go, V(PE, 136, 144), negE, OP.is_gt)
-            tt(H("msk", 0, 144), IND(S(5), BX9), H("Rf", 0, 144), OP.is_equal)
-            if CFG["MPRE"][hi] == 2:
-                tt(H("L3", 0, 144), IND(S(6), BX9), H("msk", 0, 144), OP.mult)
-                tt(H("md", 0, 144), IND(H(SA, 0, 16), BX9), H("L3", 0, 144), OP.mult)
+            ts(go, S(5), 0.0, OP.is_gt)
+            tt(S(6), qs, col, OP.subtract)
+            PQ = V(PA, 384, 512)
+            if qa >= 2:
+                act(H("Dq"), IND(XW, H("su", 0, 8)), AF.Copy)
+                mm([(PQ, V("I"), H("Dq"), True, False), (PQ, V("NI"), A, False, True)])
+            elif not gtq:
+                tt(H("Dq"), IND(XW, H("su", 0, 8)), A, OP.subtract)
+            if qa == 3:
+                act(H("cq"), PQ, AF.Relu, CM2, -1.0)
+                act(H("cq", 128, 256), PQ, AF.Relu, CM2)
+                mm([(PQ, V("I"), H("Dq"), True, False), (PQ, V("I"), H("cq"), False, False), (PQ, V("NI"), H("cq", 128, 256), False, True)])
             else:
-                tt(S(10), go, S(6), OP.mult)
-                tt(H("md", 0, 144), IND(S(10), BX9), H("msk", 0, 144), OP.mult)
-            mm([(V(PR, 272, 416), V("If"), H("Rf", 0, 144), True, False)]
-               + ([(V(PR, 272, 416), V("I"), V("PAR"), False, False)] if t == TS - 1 else []))
-            mm([(V(PR, 272, 416), V("If"), H("md", 0, 144), False, True)])
+                ts(H("cq"), PQ if qa == 2 else H("Dq"), -2.0, OP.max, 2.0, OP.min)
+                if qa:
+                    mm([(PQ, V("I"), A, True, False), (PQ, V("I"), H("cq"), False, True)])
+            if qa:
+                act(H(AW, 272, 400), PQ, AF.Copy)
+            else:
+                tt(H(AW, 272, 400), A, H("cq"), OP.add)
+            if CFG["MPRE"][hi]:
+                tt(H("msk"), IND(col, BX), RM, OP.is_equal)
+                tt(H("L3"), IND(S(6), BX), H("msk"), OP.mult)
+                tt(H("md"), IND(H(SA, 0, 16), BX), H("L3"), OP.mult)
+            else:
+                tt(H("msk"), IND(src, BX), RM, OP.is_equal)
+                tt(H("md"), IND(S(6), BX), H("msk"), OP.mult)
+            if h16 and t > 0:
+                mm([(V(PB, 0, 128), V("IR"), H("Rh"), True, False), (V(PB, 0, 128), V("IA"), V("ONE"), False, False)])
+            else:
+                mm([(V(PB, 0, 128), V("If"), RM, True, False)])
+            mm([(V(PB, 0, 128), V("If"), H("md"), False, True)])
             if t == TS - 1:
-                ts(H(SR, 0, 144), V(PR, 272, 416), 4.0, OP.mult)
+                act(H(SR), V(PB, 0, 128), AF.Copy)
             else:
-                cp(H(SR, 0, 144), V(PR, 272, 416))
-            mm([(V(PS, 256, 264), V("I"), V("cb"), True, False), (V(PS, 256, 264), V("IC"), go, False, True)])
-            cp(H("su", 16, 24), V(PS, 256, 264))
-            act(H(SA, 16, 144), IND(H(AW, 0, AWW), H("su", 16, 24)), AF.Copy)
+                cp(H(SR), V(PB, 0, 128))
+            act(H("crep"), IND(V("IOTA"), H("su", 24, 32)), AF.Copy)
+            PL = V(PC, 0, 128)
+            if la >= 2:
+                act(H("Dl"), IND(XW, H("su", 24, 32)), AF.Copy)
+                mm([(PL, V("I"), H("Dl"), True, False), (PL, V("NI"), A, False, True)])
+            else:
+                tt(H("Dl"), IND(XW, H("su", 24, 32)), A, OP.subtract)
+            if la == 3:
+                act(H("cl"), PL, AF.Relu, CM8)
+                act(H("cl", 128, 256), PL, AF.Relu, CM8, -1.0)
+                mm([(PL, V("I"), H("cl"), True, False), (PL, V("NI"), H("cl", 128, 256), False, True)])
+            else:
+                ts(H("cl"), PL if la == 2 else H("Dl"), -8.0, OP.max, 8.0, OP.min)
+                if la == 2:
+                    mm([(PL, V("I"), H("Dl"), True, False), (PL, V("NI"), A, False, False), (PL, V("NI"), H("cl"), False, True)])
+                elif la:
+                    mm([(PL, V("I"), H("Dl"), True, False), (PL, V("NI"), H("cl"), False, True)])
+            if la:
+                act(H("tb"), PL, AF.Copy)
+            else:
+                tt(H("tb"), H("Dl"), H("cl"), OP.subtract)
+            PDD = V(PA, 256, 384)
+            mm([(PDD, V("If"), H("crep"), True, False), (PDD, V("I8"), V("ONE"), False, False)])
+            tt(H("eq"), IND(H("src", 0, 16), BY), H("crep"), OP.is_equal)
+            if CFG["PAIR"][hi]:
+                tt(H("eq2"), IND(H("src", 0, 16), BE), H("crep"), OP.is_equal)
+                mm([(PDD, V("TRI"), H("eq"), False, False), (PDD, V("BO8"), H("eq2"), False, True)])
+                pick(H("sc"), PDD)
+                ts(H("su", 32, 40, 2), H("sc", 15, 128, 32), HELD, OP.subtract, DUM, OP.min)
+                ts(H("su", 33, 40, 2), H("sc", 31, 128, 32), HELD, OP.subtract, DUM2, OP.min)
+            else:
+                mm([(PDD, V("TRI"), H("eq"), False, True)])
+                pick(H("sc"), PDD)
+                ts(H("su", 32, 48, 2), H("sc", 15, 128, 16), HELD, OP.subtract, DUM, OP.min)
+            mm([(V(PC, 400, 408), V("I"), V("cb"), True, False), (V(PC, 400, 408), V("IC"), go, False, True)])
+            cp(H("su", 48, 56), V(PC, 400, 408))
+            act(H(SA, 16, 144), IND(H(AW, 0, AWW), H("su", 48, 56)), AF.Copy)
 
-            def send_r(t=t, b=b, SR=SR):
-                return g.remote_dma(T["RU%d" % (t + 1)][:, 144 * b:144 * b + 144], T[SR][:, 144 * b:144 * b + 144],
+            def send_r(b=b, SR=SR, RN=RN, t=t):
+                return g.remote_dma(T[RN][:, 128 * b:128 * b + 128], T[SR][:, 128 * b:128 * b + 128],
                                     T.sem["ar%d_%d" % (t, b)], T.sem.sent, pid, rid, emask)
 
             def send_a(t=t, b=b, SA=SA):
                 return g.remote_dma(T["AW%d" % (t + 1)][:, AWW * b:AWW * b + 144], T[SA][:, 144 * b:144 * b + 144],
                                     T.sem["aa%d_%d" % (t, b)], T.sem.sent, pid, rid, emask)
-            k1 = add("pool", send_r, H(SR, 0, 144)[1], [], 800.0, "remote")
+            k1 = add("pool", send_r, H(SR)[1], [], 800.0, "remote")
             sends.append((k1, add("pool", send_a, H(SA, 0, 144)[1], [], 800.0, "remote", after=[k1])))
-            if CFG["CREP"] == "act":
-                act(H("crep"), IND(V("IOTA"), H("su", 8, 16)), AF.Copy)
-            else:
-                cp(H("crep"), IND(V("IOTA"), H("su", 8, 16)))
-            tt(H("mk"), IND(S(5), BY), H("crep"), OP.is_equal)
-            mm([(V(PE, 144, 152), V("If"), S(5), True, False), (V(PE, 144, 152), V("I8"), V("ONE", 0, 8), False, False),
-                (V(PE, 144, 152), V("NI8"), go, False, False)])
-            if CFG["PAIR"][hi]:
-                cp(H("su", 24, 28), V("sm", 128 * b + 41, 128 * b + 48, 2))
-                act(H("cr2", 0, 64), IND(V("IOTA"), H("su", 24, 28)), AF.Copy)
-                tt(H("M1", 0, 64), IND(S(5), BE), H("cr2", 0, 64), OP.is_equal)
-                tt(H("gt", 0, 64), IND(H(SA, 0, 16), BE), H("M1", 0, 64), OP.mult)
-                fold(V(PE, 145, 152, 2), "BW8", "gt", 128 * b, 4, False, False)
-            tt(H("eq"), IND(H(SA, 0, 16), BY), H("mk"), OP.mult)
-            fold(V(PE, 144, 152), "TRI", "eq", 128 * b, 8, False, True)
-            if la >= 2:
-                act(H("cl"), DL, AF.Relu, CM8)
-                act(H("r3"), DL, AF.Relu, CM8, -1.0)
-                mm([(V(PS, 128, 256), V("I"), H("cl"), True, False), (V(PS, 128, 256), V("NI"), H("r3"), False, True)])
-                act(H("tb"), V(PS, 128, 256), AF.Copy)
-            elif la == 1:
-                ts(H("cl"), H("Dl"), -8.0, OP.max, 8.0, OP.min)
-                mm([(V(PS, 384, 512), V("I"), H("Dl"), True, False), (V(PS, 384, 512), V("NI"), H("cl"), False, True)])
-                act(H("tb"), V(PS, 384, 512), AF.Copy)
-            else:
-                ts(H("cl"), H("Dl"), -8.0, OP.max, 8.0, OP.min)
-                tt(H("tb"), H("Dl"), H("cl"), OP.subtract)
-            if CFG["PAIR"][hi]:
-                ts(H("su", 32, 40, 2), V(PE, 144, 152, 2), DUM, OP.min)
-                ts(H("su", 33, 40, 2), V(PE, 145, 152, 2), V("dm2", 0, 1), OP.min)
-            else:
-                ts(H("su", 32, 48, 2), V(PE, 144, 152), DUM, OP.min)
             if hi == 0:
                 lead.append((first, len(ops), CFG["BIAS"]))
                 lead.append((tail, len(ops), CFG["TAIL"]))
         for b in (1, 0):
             if CFG["PAIR"][1 - b]:
                 for y in range(6, -1, -2):
-                    tt(IND(XW, V("su", 48 * b + 32 + y, 48 * b + 34 + y)), V("tb", 128 * b + 16 * y, 128 * b + 16 * y + 32),
+                    tt(IND(XW, V("su", 64 * b + 32 + y, 64 * b + 34 + y)), V("tb", 128 * b + 16 * y, 128 * b + 16 * y + 32),
                        V(AW, AWW * b + 16 + 16 * y, AWW * b + 48 + 16 * y), OP.add)
                 continue
             for y in range(7, -1, -1):
-                tt(IND(XW, V("su", 48 * b + 32 + 2 * y, 48 * b + 33 + 2 * y)), V("tb", 128 * b + 16 * y, 128 * b + 16 * y + 16),
+                tt(IND(XW, V("su", 64 * b + 32 + 2 * y, 64 * b + 33 + 2 * y)), V("tb", 128 * b + 16 * y, 128 * b + 16 * y + 16),
                    V(AW, AWW * b + 16 + 16 * y, AWW * b + 32 + 16 * y), OP.add)
         steps.append((step0, len(ops)))
         for b, k in zip((1, 0), sends):
-            add("arr", None, [], [("RU%d" % (t + 1), 144 * b, 144 * b + 144)], 0.0, "ar%d_%d" % (t, b), nen, LAT_R, after=[k[0]])
-            add("arr", None, [], [("AW%d" % (t + 1), AWW * b, AWW * b + 144)], 0.0, "aa%d_%d" % (t, b), nen, LAT_R, after=[k[1]])
+            add("arr", None, [], [(RN, 128 * b, 128 * b + 128)], 0.0, "ar%d_%d" % (t, b), nen, CFG["LR"], after=[k[0]])
+            add("arr", None, [], [("AW%d" % (t + 1), AWW * b, AWW * b + 144)], 0.0, "aa%d_%d" % (t, b), nen, CFG["LR"], after=[k[1]])
 
-    dma("sp", [(T.yx[:], T.X[:, 0:W])], [("X", 0, W)], [], "o_x", 6000.0)
-    dma("act", [(T.ya[:, 128 * b:128 * b + 128], T["AW%d" % TS][:, AWW * b + 16:AWW * b + 144]) for b in range(2)],
-        [("AW%d" % TS, 0, 2 * AWW)], [], "o_a", 2500.0)
+    dma("sp", [(T.yx[:], T.X[:, 0:W])], [("X", 0, W)], [], "o_x", 5000.0)
     for b in (1, 0):
         c = 128 * b
-        ts(V("F1", c, c + 128), V("RU%d" % TS, 144 * b, 144 * b + 128), 0.25, OP.mult)
-        for j in range(1, 5):
-            i, o = "F%d" % j, "F%d" % (j + 1)
-            tt(V(o, c, c + 128, 2), V(i, c, c + 64), V(i, c + 64, c + 128), OP.min)
-            tt(V(o, c + 1, c + 128, 2), V(i, c, c + 64), V(i, c + 64, c + 128), OP.max)
-    cp(V("F0", 0, 256), IND(V("F5"), P3))
-    add("dve", lambda: g.vector.transpose(T.F6[:], T.F0[:, 0:256]), [("F0", 0, 256)], [("F6", 0, 256)], vcost(256, 1.0))
-    ts(V("F8"), IND(V("F6"), P4), 12582912.0, OP.add, -12582912.0, OP.add)
-    for eng, sem, part in (("act", "o_r", pieces[:8]), ("sp", "o_r2", pieces[8:])):
-        dma(eng, [(T.yr[32 * gh + 16 * gl:32 * gh + 16 * gl + 16, 128 * b:128 * b + 128],
-                   T.F8[32 * gh + 16 * b:32 * gh + 16 * b + 16, 128 * gl:128 * gl + 128]) for (gh, b, gl) in part],
-            [("F8", 0, 256)], [], sem, 2500.0)
-    cp(V("KV", 0, 16), V("F5", 0, 256, 16))
-    tt(V("ng"), V("F5", 0, 256, 16), V("KV", 0, 16), OP.subtract)
-    tt(V("fb"), IND(V("ng"), P5), V("DG"), OP.mult)
-    mm([(V("PE0", 0, 256), V("BO"), V("fb"), True, True)])
-    ts(V("ys2"), V("PE0", 0, 256), -8.0, OP.mult, 1.0, OP.add)
-    dma("sp", [(T.ys[:], T.ys2[0:128:16, :])], [("ys2", 0, 256)], [], "o_s", 2500.0)
+        dma("act", [(T.ya[:, c:c + 128], T["AW%d" % TS][:, AWW * b + 16:AWW * b + 144])], [("AW%d" % TS, AWW * b, AWW * b + 144)], [],
+            "o_a%d" % b, 2500.0)
+        for i, o in (("RF", "F2"), ("F2", "F3"), ("F3", "F4")):
+            for p in (c, c + 64):
+                l, r = (p, p + 32) if i != "RF" else ((c, c + 96) if p == c else (c + 32, c + 64))
+                tt(V(o, p, p + 64, 2), V(i, l, l + 32), V(i, r, r + 32), OP.min)
+                tt(V(o, p + 1, p + 64, 2), V(i, l, l + 32), V(i, r, r + 32), OP.max)
+        tt(V("F5", c, c + 128, 2), V("F4", c, c + 64), V("F4", c + 64, c + 128), OP.min)
+        tt(V("F5", c + 1, c + 128, 2), V("F4", c, c + 64), V("F4", c + 64, c + 128), OP.max)
+        tt(V("ng", 8 * b, 8 * b + 8), V("F4", c + 64, c + 128, 8), V("F4", c, c + 64, 8), OP.is_lt)
+        cp(V("F0", c, c + 128), IND(V("F5", c, c + 128), P3))
+        turn(V("F6", c, c + 128), V("F0", c, c + 128))
+        cp(V("F8", c, c + 128), IND(V("F6", c, c + 128), P4))
+        for eng, sem, part in (("act", "o_r%d" % b, pieces[:8]), ("sp", "o_t%d" % b, pieces[8:])):
+            dma(eng, [(T.yr[32 * gh + 16 * gl:32 * gh + 16 * gl + 16, c + 64 * y2:c + 64 * y2 + 64],
+                       T.F8[32 * gh + 16 * y2:32 * gh + 16 * y2 + 16, c + 64 * gl:c + 64 * gl + 64]) for (gh, y2, gl) in part],
+                [("F8", c, c + 128)], [], sem, 2500.0)
+        tt(V("fb", c, c + 128), IND(V("ng", 8 * b, 8 * b + 8), BY), V("DG"), OP.mult)
+        mm([(V("PV%d" % b, 0, 128), V("BO"), V("fb", c, c + 128), True, True)])
+        act(V("ys2", c, c + 128), V("PV%d" % b, 0, 128), AF.Identity, CM1, 2.0)
+        dma("sp", [(T.ys[:, c:c + 128], T.ys2[0:128:16, c:c + 128])], [("ys2", c, c + 128)], [], "o_s%d" % b, 2500.0)
 
     n = len(ops)
     succ = [[] for _ in range(n)]
@@ -571,7 +627,7 @@ def rank_program(g, core, T, topo):
 
     def edge(j, k):
         a, b = ops[j]["eng"], ops[k]["eng"]
-        if a == b and (a in ("pe", "pool") or j in ops[k]["soft"]):
+        if a == b and a in ("pe", "pool"):
             return 0.0
         return ops[j]["lat"] + (LAT_SAME if a == b else LAT_X)
     pri = [0.0] * n
@@ -580,15 +636,18 @@ def rank_program(g, core, T, topo):
     for (a, e, f) in lead:
         for k in range(a, e):
             pri[k] += f
+    for k in range(3):
+        pri[k] += 1e6 - k
     for (a, e) in steps:
         names = {}
         for k in range(a, e):
             nm, c0 = ops[k]["w"][0], ops[k]["w"][1]
-            nm = "%s.%d" % (nm[:2] if nm[:2] in ("AW", "SR", "SA") else nm, c0)
+            nm = "%s.%d" % ({"SF": "SR"}.get(nm, nm[:2] if nm[:2] in ("AW", "SR", "SA") else nm), c0)
             names[nm] = names.get(nm, 0) + 1
             ops[k]["key"] = nm + "abcdefghijklmnop"[names[nm] - 1]
     for k, o in enumerate(ops):
         o["pri"] = pri[k]
+        o["first"] = 1e6 - k if k < 3 else 0.0
         o["succ"] = [(s, edge(k, s)) for s in succ[k]]
     order = arrange(ops)
 
@@ -603,7 +662,7 @@ def rank_program(g, core, T, topo):
             best = {}
             for j in ops[k]["deps"]:
                 o = ops[j]
-                if o["sem"] == "remote" or (o["eng"] == e and e in ("pe", "pool")) or j in ops[k]["soft"]:
+                if o["sem"] == "remote" or (o["eng"] == e and e in ("pe", "pool")):
                     continue
                 if o["sem"] is not None:
                     if (e, j) not in seen:

from concourse.mybir import AluOpType, ActivationFunctionType

N, W, C, TS = 4, 4096, 256, 4
WX = W + 32
AWW = 400
CFG = {"REF": (((0, 4, "a"), (4, 9, "d"), (9, 12, "a"), (12, 16, "d")), ((0, 5, "a"), (5, 9, "d"), (9, 16, "a"))),
       "PROBE": ("aa dd d a d d", "dd aa d d aa"), "H16": True, "WIN": 100.0, "QA": (0, 0), "LA": (1, 2),
       "BIAS": 2000.0, "TAIL": 1500.0, "PAIR": (1, 1), "CSCAN": (0, 1), "MPRE": (0, 1), "GTQ": (0, 0),
       "PMACT": (0, 1), "RFA": (0, 0), "LR": 2500.0, "TURNS": 3}
ORDER = {}

SCRATCH = {}
_r = "bfloat16" if CFG["H16"] else "float32"
for _n, _w, _d in (
        ("X", WX, "bfloat16"), ("IOTA", WX, "float32"), ("G", W, "bfloat16"), ("Dd", W, "bfloat16"), ("AB", W, "bfloat16"),
        ("L", 256, "int32"), ("L1", 256, "float32"), ("L2", 256, "float32"), ("ng", 32, "float32"), ("ngb", 256, "float32"),
        ("wti", 8, "int32"), ("sgi", 256, "int32"), ("sgb", 256, "bfloat16"),
        ("COL", 144, "float32"), ("COLX", 128, "float32"), ("COLG", 128, "float32"),
        ("pi", 8, "int32"), ("pv", 16, "int32"), ("pf", 24, "float32"), ("ci", 128, "int32"),
        ("cb", 8, "bfloat16"), ("cu", 128, "uint16"), ("M4", 16, "bfloat16"), ("CZ", 128, "bfloat16"), ("CP", 256, "bfloat16"),
        ("I", 128, "bfloat16"), ("NI", 128, "bfloat16"), ("IA", 128, "bfloat16"), ("NIA", 128, "bfloat16"), ("IB", 128, "bfloat16"),
        ("NIB", 128, "bfloat16"), ("IC", 128, "bfloat16"), ("If", 128, "float32"), ("IR", 128, _r), ("Id", 128, _r),
        ("NId", 128, _r), ("Ih", 128, "bfloat16"), ("NIh", 128, "bfloat16"), ("IE", 128, "bfloat16"), ("I8", 128, "bfloat16"),
        ("ONE", 128, "bfloat16"), ("BW", 144, "bfloat16"), ("WU", 144, "bfloat16"), ("WE", 144, "bfloat16"), ("SX", 128, "bfloat16"),
        ("BO", 128, "bfloat16"), ("BO8", 128, "bfloat16"), ("DG", 128, "bfloat16"), ("TRI", 128, "bfloat16"), ("PK", 128, "bfloat16"),
        ("Rf", 256, "float32"), ("Rt", 256, "float32"), ("PP", 768, "float32"), ("Rh", 256, "float16"), ("wr", 256, "bfloat16"),
        ("si", 288, "int32"), ("u", 256, "int32"), ("pr", 256, "int32"), ("p16", 256, "int32"), ("tt", 256, "int32"),
        ("h", 256, "int32"), ("dh", 256, "float32"), ("z", 256, "int32"), ("q", 256, "int32"), ("QU", 256, "uint16"),
        ("vo", 256, "bfloat16"), ("KA", 384, "float32"), ("K1", 384, "float32"), ("K2", 192, "float32"),
        ("K3", 96, "float32"), ("KV", 48, "int32"), ("OF", 64, "int32"), ("sm", 256, "float32"), ("sb", 32, "bfloat16"),
        ("src", 32, "float32"), ("su", 128, "uint16"), ("Dq", 256, "bfloat16"), ("gt", 256, "bfloat16"), ("Dp", 512, "bfloat16"),
        ("Ap", 512, "bfloat16"), ("Dl", 256, "bfloat16"), ("cl", 512, "bfloat16"), ("tb", 256, "bfloat16"), ("cq", 512, "bfloat16"),
        ("msk", 256, "float32"), ("L3", 256, "float32"), ("md", 256, "float32"), ("crep", 256, "float32"), ("eq", 256, "bfloat16"),
        ("eq2", 256, "bfloat16"), ("sc", 256, "float32"), ("gr", 256, "bfloat16"),
        ("RF", 256, "float32"), ("SF", 256, "float32"), ("F0", 256, "float32"), ("F2", 256, "float32"), ("F3", 256, "float32"),
        ("F4", 256, "float32"), ("F5", 256, "float32"), ("F6", 256, "float32"), ("F8", 256, "float32"), ("fb", 256, "bfloat16"),
        ("ys2", 256, "float32")):
    SCRATCH[_n] = ("sbuf", [128, _w], _d)
for _t in range(TS + 1):
    SCRATCH["AW%d" % _t] = ("sbuf", [128, 2 * AWW], "bfloat16")
for _t in range(TS):
    SCRATCH["RU%d" % _t] = ("sbuf", [128, 256], "uint16")
    SCRATCH["SA%d" % _t] = ("sbuf", [128, 288], "bfloat16")
for _t in range(TS - 1):
    SCRATCH["SR%d" % _t] = ("sbuf", [128, 256], "uint16")
for _b in ("PA0", "PA1", "PB0", "PB1", "PC0", "PC1", "PV0", "PV1"):
    SCRATCH[_b] = ("psum", [128, 512], "float32")

SEMAPHORES = (["c_dve", "c_act", "c_pe", "c_pool", "sent", "d_x", "d_l", "d_l2", "d_a", "d_w", "d_s", "o_x"]
              + ["o_%s%d" % (k, b) for k in "rtas" for b in range(2)]
              + ["a%s%d_%d" % (k, t, b) for k in "ra" for t in range(TS) for b in range(2)])

CYC, PCYC, GC, SC = 0.86, 0.5, 1.56, 3.8
LAT_SAME, LAT_X = 180.0, 250.0
OVH, MINC, POV = 10.0, 64.0, 8.0
WOVEN = {"KA": 3, "su": 2, "F2": 2, "F3": 2, "F4": 2, "F5": 2}
BIG = 262144.0
ODD, EVEN = [(0, 32, 40), (96, 120, 72), (120, 128, 32)], [(32, 64, 0), (64, 96, 96)]
OP = AluOpType
AF = ActivationFunctionType


def arrange(ops):
    n = len(ops)
    pred = [[] for _ in range(n)]
    for k, o in enumerate(ops):
        for (s, e) in o["succ"]:
            pred[s].append((k, e))

    def sweep(pri, nxt, prv, head):
        left = [len(p) for p in prv]
        rdy = list(head)
        free = {"arr": 0.0, "dve": 0.0, "act": 0.0, "pe": 0.0, "pool": 0.0, "sp": 0.0}
        ready = [k for k in range(n) if left[k] == 0]
        order, t0 = [], [0.0] * n
        while ready:
            st = {k: max(rdy[k], free[ops[k]["eng"]]) for k in ready}
            k0 = min(ready, key=lambda j: (st[j], -pri[j], j))
            lim = st[k0] + min(CFG["WIN"], 0.6 * ops[k0]["cost"])
            k = max([j for j in ready if ops[j]["eng"] == ops[k0]["eng"] and st[j] <= lim], key=lambda j: (pri[j], -j))
            ready.remove(k)
            o = ops[k]
            if o["eng"] != "arr":
                free[o["eng"]] = st[k] + o["cost"]
            t0[k] = st[k]
            order.append(k)
            for (s, e) in nxt[k]:
                rdy[s] = max(rdy[s], st[k] + o["cost"] + e)
                left[s] -= 1
                if left[s] == 0:
                    ready.append(s)
        return order, t0
    succ = [o["succ"] for o in ops]
    bias = [100.0 * ORDER.get(o.get("key"), 0) for o in ops]
    pri = [o["pri"] + bias[k] for k, o in enumerate(ops)]
    best = None
    for _ in range(CFG["TURNS"] + 1):
        order, t0 = sweep(pri, succ, pred, [0.0] * n)
        end = max(t0[k] + o["cost"] + o["lat"] for k, o in enumerate(ops))
        if best is None or end < best[0]:
            best = (end, order, t0)
        if CFG["TURNS"]:
            _, tb = sweep([t0[k] + o["cost"] for k, o in enumerate(ops)], pred, succ, [o["lat"] if not succ[k] else 0.0 for k, o in enumerate(ops)])
            pri = [tb[k] + o["cost"] + o["first"] + bias[k] for k, o in enumerate(ops)]
    for k, o in enumerate(ops):
        o["t0"] = best[2][k]
    return best[1]


def rank_program(g, core, T, topo):
    rank = T.rank_of(core)
    if rank is None:
        return
    nxt = T.cores[(rank + 1) % N]
    rid, pid, _ = topo.addr(nxt)
    engs = topo.engines(core, nxt)
    nen = len(engs)
    emask = topo.mask(core, nxt)
    ops = []
    hist = {}
    Q = {"dve": g.vector, "act": g.scalar, "pe": g.tensor, "pool": g, "sp": g.sync}

    def V(name, a=None, b=None, s=1):
        w = SCRATCH[name][1][1]
        a = 0 if a is None else a
        b = w if b is None else b
        ap = T[name][:, a:b] if s == 1 else T[name][:, a:b:s]
        return (ap, [(name, a, b)], len(range(a, b, s)), SCRATCH[name][2], SCRATCH[name][0])

    def IND(win, off):
        return (win[0].indirect(off[0]), win[1] + off[1], 16 * off[2], win[3], "ind")

    def add(eng, fn, reads, writes, cost, sem=None, cnt=0, lat=0.0, after=()):
        k = len(ops)
        deps = set(after)
        for regs, isw in ((reads, False), (writes, True)):
            for (nm, a, b) in regs:
                ps = SCRATCH[nm][0] == "psum"
                for (j, e2, a2, b2, w2) in hist.setdefault(nm, []):
                    if ps and (e2 != eng or eng == "pe"):
                        deps.add(j)
                    elif isw and w2 and e2 == eng and j >= k - 4 and (a - a2) % WOVEN.get(nm, 3 if ps else 1) and abs(a - a2) < WOVEN.get(nm, 3):
                        continue
                    elif (isw or w2) and a < b2 and a2 < b:
                        deps.add(j)
        for regs, isw in ((reads, False), (writes, True)):
            for (nm, a, b) in regs:
                hist[nm].append((k, eng, a, b, isw))
        deps.discard(k)
        ops.append({"w": writes[0] if writes else ("-", 0, 0), "eng": eng, "fn": fn, "deps": deps, "cost": cost, "sem": sem, "cnt": cnt, "lat": lat})
        return k

    def two(*vs):
        return all(v[3] in ("bfloat16", "uint16", "float16") for v in vs)

    def vcost(n, f):
        if f in (GC, SC):
            return 50.0 + n * f * CYC
        return OVH + max(MINC, n * f) * CYC

    def cp(o, i):
        f = GC if i[4] == "ind" else (0.5 if two(o, i) else 1.0)
        return add("dve", lambda: g.vector.tensor_copy(o[0], i[0]), i[1], o[1], vcost(o[2], f))

    def tt(o, a, b, op):
        if o[4] == "ind":
            return add("dve", lambda: g.vector.tensor_tensor(o[0], a[0], b[0], op), a[1] + b[1] + o[1][1:], o[1][:1], vcost(o[2], SC))
        f = GC if a[4] == "ind" else (1.0 if "psum" in (a[4], b[4]) else 2.0)
        return add("dve", lambda: g.vector.tensor_tensor(o[0], a[0], b[0], op), a[1] + b[1], o[1], vcost(o[2], f))

    def ts(o, a, s1, op0, s2=None, op1=None):
        rd = list(a[1])
        x1, x2 = s1, s2
        if isinstance(s1, tuple):
            rd += s1[1]
            x1 = s1[0]
        if isinstance(s2, tuple):
            rd += s2[1]
            x2 = s2[0]
        f = GC if a[4] == "ind" else (0.5 if two(o, a) else 1.0)
        if op1 is None:
            return add("dve", lambda: g.vector.tensor_scalar(o[0], a[0], x1, None, op0), rd, o[1], vcost(o[2], f))
        return add("dve", lambda: g.vector.tensor_scalar(o[0], a[0], x1, x2, op0, op1), rd, o[1], vcost(o[2], f))

    def pick(o, i):
        pk = V("PK")
        return add("dve", lambda: g.vector.tensor_tensor_scan(o[0], pk[0], i[0], 0.0, OP.add, OP.max), i[1] + pk[1], o[1], vcost(o[2], 1.0))

    def turn(o, i):
        return add("dve", lambda: g.vector.transpose(o[0], i[0]), i[1], o[1], vcost(o[2], 1.0))

    def ms(o, val):
        return add("dve", lambda: g.vector.memset(o[0], val), [], o[1], vcost(o[2], 1.0))

    def act(o, i, fn, bias=None, scale=1.0):
        f = GC if i[4] == "ind" else 1.0
        if bias is None:
            return add("act", lambda: g.scalar.activation(o[0], i[0], fn), i[1], o[1], 65.0 + o[2] * f * CYC)
        return add("act", lambda: g.scalar.activation(o[0], i[0], fn, bias=bias[0], scale=scale), i[1] + bias[1], o[1], 65.0 + o[2] * f * CYC)

    def mm(items):
        rd, wr, cost = [], [], 0.0
        for (o, l, r, st, sp) in items:
            rd += l[1] + r[1]
            wr += o[1]
            cost += POV + max(64, r[2]) * PCYC * (4 if r[3] == "float32" else 1)

        def fn():
            last = None
            for (o, l, r, st, sp) in items:
                last = g.tensor.matmul(o[0], l[0], r[0], st, sp)
            return last
        return add("pe", fn, rd, wr, cost)

    def group(its, start=True, stop=True):
        for i, (o, l, r) in enumerate(its):
            mm([(o, l, r, start and i == 0, stop and i == len(its) - 1)])

    def fold(o, wname, src, a, n, first, last):
        return mm([(o, V(wname, 15 - x, 143 - x), V(src, a + x, a + 16 * n, 16), first and x == 0, last and x == 15) for x in range(16)])

    def iota(o, pat, base, cm, after=()):
        if o[3] == "int32":
            return add("pool", lambda: g.iota(o[0], pat, base, cm), [], o[1], 130.0 + 2 * o[2] * CYC, after=after)
        return add("pool", lambda: g.iota(o[0], pat, base, cm, allow_small_or_imprecise_dtypes=True), [], o[1], 130.0 + 2 * o[2] * CYC, after=after)

    def dma(eng, pairs, reads, writes, sem, lat, after=()):
        def fn():
            for (o, i) in pairs:
                Q[eng].dma_start(o, i).then_inc(T.sem[sem], 16)
            return None
        return add(eng, fn, reads, writes, 60.0 * len(pairs), sem, 16 * len(pairs), lat, after)

    pieces = [(gh, b, gl) for gh in range(4) for b in range(2) for gl in range(2)]
    lp = [(T.L[32 * gh + 16 * b:32 * gh + 16 * b + 16, 128 * gl:128 * gl + 128],
           T.rl[32 * gh + 16 * gl:32 * gh + 16 * gl + 16, 128 * b:128 * b + 128]) for (gh, b, gl) in pieces]
    k1 = dma("act", lp[:10], [], [], "d_l", 2500.0)
    k2 = dma("sp", lp[10:], [], [], "d_l2", 2500.0)
    dma("sp", [(T.X[:, 0:W], T.xt[:])], [], [("X", 0, W)], "d_x", 5000.0)
    ms(V("sgi"), 0)
    dma("act", [(T.wti[:, 0:1], T.wt[:])], [], [("wti", 0, 8)], "d_w", 2500.0)
    dma("act", [(T.AW0[:, AWW * b + 16:AWW * b + 144], T.av[:, 128 * b:128 * b + 128]) for b in range(2)], [],
        [("AW0", 16, 144), ("AW0", AWW + 16, AWW + 144)], "d_a", 2500.0)
    dma("sp", [(T.sgi[0:128:16, :], T.sg[:])], [], [("sgi", 0, 256)], "d_s", 2500.0)
    hist["L"] = [(k1, "act", 0, 256, True), (k2, "sp", 0, 256, True)]

    io = [iota(V("pi", 0, 1), [[0, 1]], 0, 1),
          iota(V("ci", 0, 16), [[16, 8], [128, 2]], 0, 0),
          iota(V("ci", 16, 24), [[16, 2], [-1, 2], [4, 2]], 1, 0),
          iota(V("ci", 24, 32), [[16, 2], [1, 2], [4, 2]], 8, 0),
          iota(V("COL"), [[1, 144]], 0, 0),
          iota(V("ci", 32, 40), [[1, 8]], 0, 0),
          iota(V("ci", 40, 48), [[2, 4], [0, 2]], 0, 0),
          iota(V("ci", 48, 56), [[16, 4], [64, 2]], 0, 0),
          iota(V("ci", 56, 64), [[16, 2], [32, 4]], 0, 0),
          iota(V("COLX"), [[0, 8], [1, 16]], 0, 0),
          iota(V("COLG"), [[16, 8], [0, 16]], 0, 0)]
    iota(V("IOTA"), [[1, WX]], 0, 0, after=io)
    P = V("pi", 0, 1)
    ts(V("pv", 0, 1), P, 15, OP.bitwise_and)
    ts(V("pv", 1, 2), P, 112, OP.bitwise_and)
    ts(V("pv", 2, 3), P, 7, OP.bitwise_and)
    ts(V("pv", 3, 4), P, 2, OP.logical_shift_right, 2, OP.bitwise_and)
    cp(V("pf", 0, 4), V("pv", 0, 4))
    cp(V("pf", 6, 7), P)
    xf, g16, y3, k2f, pff = V("pf", 0, 1), V("pf", 1, 2), V("pf", 2, 3), V("pf", 3, 4), V("pf", 6, 7)
    ts(V("cu", 0, 16), V("ci", 0, 16), xf, OP.add)
    ts(V("pf", 4, 5), y3, 32.0, OP.mult, k2f, OP.add)
    for b in (1, 0):
        for a in range(2):
            ts(V("cu", 16 + 8 * b + 4 * a, 20 + 8 * b + 4 * a), V("ci", 16 + 8 * a + 4 * b, 20 + 8 * a + 4 * b), V("pf", 4, 5), OP.add)
    ts(V("cu", 32, 40), V("ci", 32, 40), 0.0, OP.mult, y3, OP.add)
    cp(V("cu", 40, 48), V("ci", 32, 40))
    cp(V("cu", 48, 56), V("ci", 40, 48))
    ms(V("cu", 48, 56, 2), 8)
    ts(V("cu", 56, 64), V("ci", 48, 56), xf, OP.add)
    ts(V("cu", 64, 72), V("ci", 56, 64), xf, OP.add)
    P1, BX, BY, BE, P3, P4 = V("cu", 0, 16), V("cu", 32, 40), V("cu", 40, 48), V("cu", 48, 56), V("cu", 56, 64), V("cu", 64, 72)
    ts(V("pf", 7, 8), g16, 15.0, OP.add)
    ts(V("pf", 8, 9), xf, float(W), OP.add)
    ts(V("pf", 9, 10), xf, float(W + 16), OP.add)
    ts(V("pf", 10, 11), xf, 14.5, OP.is_lt, BIG, OP.mult)
    ts(V("pf", 11, 12), V("pf", 10, 11), 7.5, OP.add)
    ts(V("pf", 13, 14), xf, 16.0, OP.add)
    ts(V("pf", 14, 15), xf, 1.0, OP.add)
    DUM, DUM2, HELD, HELD8 = V("pf", 8, 9), V("pf", 9, 10), V("pf", 10, 11), V("pf", 11, 12)
    for j, val in enumerate((0.998, -1.0, -2.0, -8.0, -32.0, 255.0 / 512)):
        ms(V("pf", 16 + j, 17 + j), val)
    CVO, CM1, CM2, CM8, CM32, CZP = (V("pf", 16 + j, 17 + j) for j in range(6))
    ms(V("X", W, WX), 0.0)
    ms(V("ONE"), 1.0)
    ms(V("M4"), -4096.0)
    ms(V("CZ"), -255.0 / 512)
    ms(V("src"), -1.0)
    ts(V("cb"), V("ci", 32, 40), 16.0, OP.mult, V("pf", 13, 14), OP.add)
    C128 = V("COL", 0, 128)
    ts(V("BW"), V("COL"), V("pf", 7, 8), OP.is_equal)
    cp(V("pf", 23, 24), V("wti", 0, 1))
    ts(V("WU"), V("BW"), V("pf", 23, 24), OP.mult, 32.0, OP.mult)
    ds = 1.0 / 256
    h16 = CFG["H16"]
    RH = "Rh" if h16 else "Rf"
    ts(V("I"), C128, pff, OP.is_equal)
    for nm, f in (("If", 1.0), ("Id", ds), ("NId", -ds), ("IR", 1.0), ("NI", -1.0), ("IA", 2048.0), ("NIA", -2048.0), ("IB", 33554432.0),
                  ("NIB", -33554432.0), ("IC", 256.0), ("IE", 16711680.0), ("I8", 8192.0), ("Ih", 8.0), ("NIh", -8.0)):
        ts(V(nm), V("I"), f, OP.mult)
    ms(V("CP"), 2048.0 * h16)
    for a, e in ((0, 32), (96, 128), (160, 224)):
        ms(V("CP", a, e), 2048.0 * h16 + 2048.0)
    ts(V("WE"), V("BW"), -8192.0, OP.mult)
    ts(V("SX"), V("COLX"), xf, OP.is_equal, 32.0, OP.mult)
    ts(V("BO"), V("COLG"), g16, OP.is_equal)
    ts(V("BO8"), V("BO"), 8192.0, OP.mult)
    ts(V("DG"), V("COLX"), xf, OP.is_equal)
    t1, t2 = V("F2", 0, 128), V("F3", 0, 128)
    ts(t1, V("COLX"), xf, OP.is_gt)
    tt(t2, t1, V("DG"), OP.subtract)
    tt(V("TRI"), t2, V("BO8"), OP.mult)
    ts(t2, V("COLX"), V("pf", 14, 15), OP.is_equal, BIG, OP.mult)
    ts(t1, t1, 2 * BIG, OP.mult, -2 * BIG, OP.add)
    tt(V("PK"), t1, t2, OP.add)
    for b in range(2):
        ms(V("AW0", AWW * b, AWW * b + 16), 0.0)
        for t in range(TS):
            ms(V("SA%d" % t, 144 * b + 8, 144 * b + 16), 0.0)

    cp(V("L1"), IND(V("L"), P1))
    turn(V("L2"), V("L1"))
    for b in (1, 0):
        cp(V("RU0", 128 * b, 128 * b + 128), IND(V("L2"), V("cu", 16 + 8 * b, 24 + 8 * b)))
    ts(V("sgb"), V("sgi"), 0.0, OP.is_lt)
    fold(V("PV0", 0, 16), "BW", "sgb", 0, 16, True, True)
    cp(V("ng", 0, 16), V("PV0", 0, 16))
    ts(V("ng", 16, 32), V("ng", 0, 16), 1.0 / ds, OP.mult)

    XW = V("X")
    nv = [0]
    lead = []
    steps = []
    for t in range(TS):
        RU, AW, SA = "RU%d" % t, "AW%d" % t, "SA%d" % t
        SR, RN = ("SR%d" % t, "RU%d" % (t + 1)) if t < TS - 1 else ("SF", "RF")
        sends = []
        step0 = len(ops)
        for hi, b in enumerate((1, 0)):
            def H(nm, a=0, e=128, s=1, b=b):
                w = SCRATCH[nm][1][1] // 2
                return V(nm, w * b + a, w * b + e, s)

            def S(j, b=b):
                return V("sm", 128 * b + 8 * j, 128 * b + 8 * j + 8)

            def own(c, l, spans):
                return [(V(PB, c + a, c + e), V(l), H(RH, a, e)) for (a, e) in spans]

            def ahead(c, l, spans):
                return [(V(PB, c + a, c + e), V(l), H(RH, f, f + e - a)) for (a, e, f) in spans]
            first = len(ops)
            PA, PB, PC = "PA%d" % b, "PB%d" % b, "PC%d" % b
            A, A2 = H(AW, 16, 144), H(AW, 16, 272)
            PD, PZ = V(PB, 0, 128), V(PB, 128, 256)
            rfa = CFG["RFA"][hi] and t > 0
            RM = H("PP", 0, 128) if rfa else H("Rf")
            if t == 0:
                act(H("Rf"), IND(V("L2"), V("cu", 16 + 8 * b, 24 + 8 * b)), AF.Copy)
            elif not rfa:
                cp(H("Rf"), H(RU))
            if h16:
                ts(H("Rh"), H(RU), -2048.0, OP.add)
            act(H(AW, 144, 272), A, AF.Copy)
            group(own(256, "NId", [(0, 128)]) + ahead(256, "Id", ODD + EVEN))
            act(H("wr"), V(PB, 256, 384), AF.Sign)
            if t == 0:
                act(H("ngb"), IND(V("ng", 16 + 8 * b, 24 + 8 * b), BX), AF.Copy)
                tt(H("L3"), H("ngb"), V(PB, 256, 384), OP.mult)
                tt(H("Rt"), H("L3"), H("Rf"), OP.add)
                RM = H("Rt")
            group(own(128, "IR", [(0, 128)]) + ([(PZ, V("IA"), V("ONE"))] if h16 else []) + [(PZ, V("I"), V("CZ"))])
            group(own(0, "NId", [(0, 128)]) + ahead(0, "Id", ODD + EVEN)
                  + [(PD, V("Ih"), V("ONE")), (PD, V("NIh"), H("wr"))])
            group([(V(PB, 256, 512), V("I"), V("CP"))]
                  + own(256, "IR", [(32, 96)]) + ahead(256, "IR", ODD) + own(384, "IR", [(0, 32), (96, 128)]) + ahead(384, "IR", EVEN)
                  + [(V(PB, 256 + a, 256 + e), V("NIA"), H("wr", a % 128, (e - 1) % 128 + 1)) for a, e in ((0, 32), (96, 128), (160, 224))])
            act(H("PP", 128, 384), V(PB, 256, 512), AF.Copy)
            if rfa:
                act(H("PP", 0, 128), PZ, AF.Identity, CZP)
            for (a, e, eng) in CFG["REF"][hi]:
                src = IND(XW, H(RU, 8 * a, 8 * e))
                if eng == "d":
                    cp(H("G", 128 * a, 128 * e), src)
                else:
                    act(H("G", 128 * a, 128 * e), src, AF.Copy)
            if t > 0:
                act(H("gr", 0, 64), IND(H(AW, 0, 16), V("cu", 32, 36)), AF.Identity, CM32)
                mm([(V(PB, 256, 320), V("SX"), H("gr", 0, 64), True, True)])
            EP = (V(PA, 128, 192), V(PC, 128, 192))
            for part, (bank, wide) in enumerate(((PA, 72), (PC, 64))):
                a, e = 64 * part, 64 * part + 64
                fold(V(bank, 0, wide), "WU", "G", 2048 * b + 1024 * part, wide, True, True)
                cp(H("si", 72 * part, 72 * part + wide), V(bank, 0, wide))
                if part == 0:
                    ts(H("u", 0, 72), H("si", 0, 72), 5, OP.logical_shift_right, 4095, OP.bitwise_and)
                else:
                    ts(H("u", 72, 128), H("si", 80, 136), 5, OP.logical_shift_right, 4095, OP.bitwise_and)
                low = H("p16", a, e)
                ts(low, H("si", 72 * part, 72 * part + 64), 8191, OP.bitwise_and)
                if t > 0:
                    low = H("pr", a, e)
                    tt(low, H("p16", a, e), V(PB, 256, 320), OP.add)
                for (c0, c1, f) in ODD + EVEN:
                    if a <= c0 < e:
                        tt(V(bank, c0 - a, c1 - a), H("u", c0, c1), H("u", f, f + c1 - c0), OP.mult)
                tt(H("tt", a, e), low, V(bank, 0, 64), OP.add)
                ts(H("h", a, e), H("tt", a, e), 5, OP.arith_shift_right, 255, OP.bitwise_and)
                tt(H("dh", a, e), H("h", a, e), V(PB, a, e), OP.mult)
                tt(H("z", a, e), H("dh", a, e), V(PB, 128 + a, 128 + e), OP.add)
                ts(H("q", a, e), H("z", a, e), 4095, OP.bitwise_and)
                cp(H("QU", a, e), H("q", a, e))
            act(H("vo"), H("dh"), AF.Sign, CVO, -1.0)
            for part in range(2):
                mm([(EP[part], V("IB"), H("vo", 64 * part, 64 * part + 64), True, False), (EP[part], V("IB"), V("ONE", 0, 64), False, False),
                    (EP[part], V("IE"), V("ONE", 0, 64), False, False)])
            m = 0
            for kind in CFG["PROBE"][hi].split():
                c0, c1 = 128 * m, 128 * m + 256 * len(kind)
                if kind[0] == "a":
                    pv = "PV%d" % (nv[0] % 2)
                    nv[0] += 1
                    act(H("Dd", c0, c1), IND(XW, H("QU", 8 * m, 8 * m + 16 * len(kind))), AF.Copy)
                    mm([(V(pv, 0, c1 - c0), V("I"), H("Dd", c0, c1), True, False)]
                       + [(V(pv, 256 * j, 256 * j + 256), V("NI"), A2, False, j == len(kind) - 1) for j in range(len(kind))])
                    act(H("AB", c0, c1), V(pv, 0, c1 - c0), AF.Abs)
                else:
                    for j in range(m, m + 2 * len(kind), 2):
                        tt(H("Dd", 128 * j, 128 * j + 256), IND(XW, H("QU", 8 * j, 8 * j + 16)), A2, OP.subtract)
                    act(H("AB", c0, c1), H("Dd", c0, c1), AF.Abs)
                m += 2 * len(kind)
                if m % 8 == 0:
                    fold(EP[m // 8 - 1], "WE", "AB", 2048 * b + 128 * (m - 8), 64, False, True)
            tail = len(ops)
            for j, (nm, c0) in enumerate((("z", 0), ("PP", 128), ("PP", 256))):
                tt(H("KA", j, 192, 3), H(nm, c0, c0 + 64), EP[0], OP.add)
            for j, (nm, c0) in enumerate((("z", 64), ("PP", 192), ("PP", 320))):
                tt(V(PC, 192 + j, 384, 3), H(nm, c0, c0 + 64), EP[1], OP.add)
            tt(H("K1", 0, 192), H("KA", 0, 192), V(PC, 192, 384), OP.min)
            tt(H("K2", 0, 96), H("K1", 0, 96), H("K1", 96, 192), OP.min)
            tt(H("K3", 0, 48), H("K2", 0, 48), H("K2", 48, 96), OP.min)
            tt(H("KV", 0, 24), H("K3", 0, 24), H("K3", 24, 48), OP.min)
            ts(H("OF", 0, 24), H("KV", 0, 24), 4095, OP.bitwise_and)
            for j in range(3):
                cp(H("su", 8 * j, 8 * j + 8), H("OF", j, 24, 3))
            ts(H("OF", 24, 32), H("KV", 0, 24, 3), -8192, OP.bitwise_and)
            negE, qs, Rp, Rm = H("OF", 24, 32), H("OF", 0, 24, 3), H("OF", 1, 24, 3), H("OF", 2, 24, 3)
            qa, la = CFG["QA"][hi], CFG["LA"][hi]
            gtq = CFG["GTQ"][hi] and qa < 2
            if gtq:
                tt(H("Dq"), IND(XW, H("su", 0, 8)), A, OP.subtract)
                ts(H("gt"), H("Dq"), 0.0, OP.is_gt)
            else:
                tt(H("gt"), IND(XW, H("su", 0, 8)), A, OP.is_gt)
            if CFG["PMACT"][hi]:
                act(H("Dp", 0, 256), IND(XW, H("su", 8, 24)), AF.Copy)
                mm([(V(PB, 256, 512), V("I"), H("Dp", 0, 256), True, False), (V(PB, 256, 512), V("NI"), A2, False, True)])
                act(H("Ap", 0, 256), V(PB, 256, 512), AF.Abs)
            else:
                tt(H("Dp", 0, 256), IND(XW, H("su", 8, 24)), A2, OP.subtract)
                act(H("Ap", 0, 256), H("Dp", 0, 256), AF.Abs)
            sg = H("sb", 0, 8)
            SG = sg
            if t == 0:
                SG = H("sb", 8, 16)
            if CFG["CSCAN"][hi]:
                mm([(V(PA, 192, 320), V("BO"), H("gt"), True, True)])
                pick(H("sc"), V(PA, 192, 320))
                ts(SG, H("sc", 15, 128, 16), HELD8, OP.is_ge)
            else:
                fold(V(PA, 192, 200), "BW", "gt", 128 * b, 8, True, True)
                ts(SG, V(PA, 192, 200), 7.5, OP.is_ge)
            if t == 0:
                tt(sg, SG, V("ng", 8 * b, 8 * b + 8), OP.not_equal)
            tt(S(0), Rp, Rm, OP.subtract)
            tt(S(1), sg, S(0), OP.mult)
            tt(S(2), S(1), Rm, OP.add)
            col = S(2)
            cp(H("su", 24, 32), col)
            PM = V(PC, 384, 400)
            mm([(PM, V("IE"), V("ONE", 0, 16), True, False), (PM, V("I"), V("M4"), False, False),
                (V(PC, 384, 392), V("NIB"), V("ONE", 0, 8), False, False)])
            fold(PM, "WE", "Ap", 256 * b, 16, False, False)
            mm([(V(PC, 384, 392), V("IB"), sg, False, False), (V(PC, 392, 400), V("NIB"), sg, False, True)])
            tt(S(3), V(PC, 384, 392), negE, OP.subtract)
            tt(S(4), V(PC, 392, 400), negE, OP.subtract)
            tt(S(5), S(3), S(4), OP.max)
            src = H("src", 0, 8)
            tt(src, S(5), col, OP.min)
            go = H(SA, 0, 8)
            ts(go, S(5), 0.0, OP.is_gt)
            tt(S(6), qs, col, OP.subtract)
            PQ = V(PA, 384, 512)
            if qa >= 2:
                act(H("Dq"), IND(XW, H("su", 0, 8)), AF.Copy)
                mm([(PQ, V("I"), H("Dq"), True, False), (PQ, V("NI"), A, False, True)])
            elif not gtq:
                tt(H("Dq"), IND(XW, H("su", 0, 8)), A, OP.subtract)
            if qa == 3:
                act(H("cq"), PQ, AF.Relu, CM2, -1.0)
                act(H("cq", 128, 256), PQ, AF.Relu, CM2)
                mm([(PQ, V("I"), H("Dq"), True, False), (PQ, V("I"), H("cq"), False, False), (PQ, V("NI"), H("cq", 128, 256), False, True)])
            else:
                ts(H("cq"), PQ if qa == 2 else H("Dq"), -2.0, OP.max, 2.0, OP.min)
                if qa:
                    mm([(PQ, V("I"), A, True, False), (PQ, V("I"), H("cq"), False, True)])
            if qa:
                act(H(AW, 272, 400), PQ, AF.Copy)
            else:
                tt(H(AW, 272, 400), A, H("cq"), OP.add)
            if CFG["MPRE"][hi]:
                tt(H("msk"), IND(col, BX), RM, OP.is_equal)
                tt(H("L3"), IND(S(6), BX), H("msk"), OP.mult)
                tt(H("md"), IND(H(SA, 0, 16), BX), H("L3"), OP.mult)
            else:
                tt(H("msk"), IND(src, BX), RM, OP.is_equal)
                tt(H("md"), IND(S(6), BX), H("msk"), OP.mult)
            if h16 and t > 0:
                mm([(V(PB, 0, 128), V("IR"), H("Rh"), True, False), (V(PB, 0, 128), V("IA"), V("ONE"), False, False)])
            else:
                mm([(V(PB, 0, 128), V("If"), RM, True, False)])
            mm([(V(PB, 0, 128), V("If"), H("md"), False, True)])
            if t == TS - 1:
                act(H(SR), V(PB, 0, 128), AF.Copy)
            else:
                cp(H(SR), V(PB, 0, 128))
            act(H("crep"), IND(V("IOTA"), H("su", 24, 32)), AF.Copy)
            PL = V(PC, 0, 128)
            if la >= 2:
                act(H("Dl"), IND(XW, H("su", 24, 32)), AF.Copy)
                mm([(PL, V("I"), H("Dl"), True, False), (PL, V("NI"), A, False, True)])
            else:
                tt(H("Dl"), IND(XW, H("su", 24, 32)), A, OP.subtract)
            if la == 3:
                act(H("cl"), PL, AF.Relu, CM8)
                act(H("cl", 128, 256), PL, AF.Relu, CM8, -1.0)
                mm([(PL, V("I"), H("cl"), True, False), (PL, V("NI"), H("cl", 128, 256), False, True)])
            else:
                ts(H("cl"), PL if la == 2 else H("Dl"), -8.0, OP.max, 8.0, OP.min)
                if la == 2:
                    mm([(PL, V("I"), H("Dl"), True, False), (PL, V("NI"), A, False, False), (PL, V("NI"), H("cl"), False, True)])
                elif la:
                    mm([(PL, V("I"), H("Dl"), True, False), (PL, V("NI"), H("cl"), False, True)])
            if la:
                act(H("tb"), PL, AF.Copy)
            else:
                tt(H("tb"), H("Dl"), H("cl"), OP.subtract)
            PDD = V(PA, 256, 384)
            mm([(PDD, V("If"), H("crep"), True, False), (PDD, V("I8"), V("ONE"), False, False)])
            tt(H("eq"), IND(H("src", 0, 16), BY), H("crep"), OP.is_equal)
            if CFG["PAIR"][hi]:
                tt(H("eq2"), IND(H("src", 0, 16), BE), H("crep"), OP.is_equal)
                mm([(PDD, V("TRI"), H("eq"), False, False), (PDD, V("BO8"), H("eq2"), False, True)])
                pick(H("sc"), PDD)
                ts(H("su", 32, 40, 2), H("sc", 15, 128, 32), HELD, OP.subtract, DUM, OP.min)
                ts(H("su", 33, 40, 2), H("sc", 31, 128, 32), HELD, OP.subtract, DUM2, OP.min)
            else:
                mm([(PDD, V("TRI"), H("eq"), False, True)])
                pick(H("sc"), PDD)
                ts(H("su", 32, 48, 2), H("sc", 15, 128, 16), HELD, OP.subtract, DUM, OP.min)
            mm([(V(PC, 400, 408), V("I"), V("cb"), True, False), (V(PC, 400, 408), V("IC"), go, False, True)])
            cp(H("su", 48, 56), V(PC, 400, 408))
            act(H(SA, 16, 144), IND(H(AW, 0, AWW), H("su", 48, 56)), AF.Copy)

            def send_r(b=b, SR=SR, RN=RN, t=t):
                return g.remote_dma(T[RN][:, 128 * b:128 * b + 128], T[SR][:, 128 * b:128 * b + 128],
                                    T.sem["ar%d_%d" % (t, b)], T.sem.sent, pid, rid, emask)

            def send_a(t=t, b=b, SA=SA):
                return g.remote_dma(T["AW%d" % (t + 1)][:, AWW * b:AWW * b + 144], T[SA][:, 144 * b:144 * b + 144],
                                    T.sem["aa%d_%d" % (t, b)], T.sem.sent, pid, rid, emask)
            k1 = add("pool", send_r, H(SR)[1], [], 800.0, "remote")
            sends.append((k1, add("pool", send_a, H(SA, 0, 144)[1], [], 800.0, "remote", after=[k1])))
            if hi == 0:
                lead.append((first, len(ops), CFG["BIAS"]))
                lead.append((tail, len(ops), CFG["TAIL"]))
        for b in (1, 0):
            if CFG["PAIR"][1 - b]:
                for y in range(6, -1, -2):
                    tt(IND(XW, V("su", 64 * b + 32 + y, 64 * b + 34 + y)), V("tb", 128 * b + 16 * y, 128 * b + 16 * y + 32),
                       V(AW, AWW * b + 16 + 16 * y, AWW * b + 48 + 16 * y), OP.add)
                continue
            for y in range(7, -1, -1):
                tt(IND(XW, V("su", 64 * b + 32 + 2 * y, 64 * b + 33 + 2 * y)), V("tb", 128 * b + 16 * y, 128 * b + 16 * y + 16),
                   V(AW, AWW * b + 16 + 16 * y, AWW * b + 32 + 16 * y), OP.add)
        steps.append((step0, len(ops)))
        for b, k in zip((1, 0), sends):
            add("arr", None, [], [(RN, 128 * b, 128 * b + 128)], 0.0, "ar%d_%d" % (t, b), nen, CFG["LR"], after=[k[0]])
            add("arr", None, [], [("AW%d" % (t + 1), AWW * b, AWW * b + 144)], 0.0, "aa%d_%d" % (t, b), nen, CFG["LR"], after=[k[1]])

    dma("sp", [(T.yx[:], T.X[:, 0:W])], [("X", 0, W)], [], "o_x", 5000.0)
    for b in (1, 0):
        c = 128 * b
        dma("act", [(T.ya[:, c:c + 128], T["AW%d" % TS][:, AWW * b + 16:AWW * b + 144])], [("AW%d" % TS, AWW * b, AWW * b + 144)], [],
            "o_a%d" % b, 2500.0)
        for i, o in (("RF", "F2"), ("F2", "F3"), ("F3", "F4")):
            for p in (c, c + 64):
                l, r = (p, p + 32) if i != "RF" else ((c, c + 96) if p == c else (c + 32, c + 64))
                tt(V(o, p, p + 64, 2), V(i, l, l + 32), V(i, r, r + 32), OP.min)
                tt(V(o, p + 1, p + 64, 2), V(i, l, l + 32), V(i, r, r + 32), OP.max)
        tt(V("F5", c, c + 128, 2), V("F4", c, c + 64), V("F4", c + 64, c + 128), OP.min)
        tt(V("F5", c + 1, c + 128, 2), V("F4", c, c + 64), V("F4", c + 64, c + 128), OP.max)
        tt(V("ng", 8 * b, 8 * b + 8), V("F4", c + 64, c + 128, 8), V("F4", c, c + 64, 8), OP.is_lt)
        cp(V("F0", c, c + 128), IND(V("F5", c, c + 128), P3))
        turn(V("F6", c, c + 128), V("F0", c, c + 128))
        cp(V("F8", c, c + 128), IND(V("F6", c, c + 128), P4))
        for eng, sem, part in (("act", "o_r%d" % b, pieces[:8]), ("sp", "o_t%d" % b, pieces[8:])):
            dma(eng, [(T.yr[32 * gh + 16 * gl:32 * gh + 16 * gl + 16, c + 64 * y2:c + 64 * y2 + 64],
                       T.F8[32 * gh + 16 * y2:32 * gh + 16 * y2 + 16, c + 64 * gl:c + 64 * gl + 64]) for (gh, y2, gl) in part],
                [("F8", c, c + 128)], [], sem, 2500.0)
        tt(V("fb", c, c + 128), IND(V("ng", 8 * b, 8 * b + 8), BY), V("DG"), OP.mult)
        mm([(V("PV%d" % b, 0, 128), V("BO"), V("fb", c, c + 128), True, True)])
        act(V("ys2", c, c + 128), V("PV%d" % b, 0, 128), AF.Identity, CM1, 2.0)
        dma("sp", [(T.ys[:, c:c + 128], T.ys2[0:128:16, c:c + 128])], [("ys2", c, c + 128)], [], "o_s%d" % b, 2500.0)

    n = len(ops)
    succ = [[] for _ in range(n)]
    for k, o in enumerate(ops):
        for j in o["deps"]:
            succ[j].append(k)

    def edge(j, k):
        a, b = ops[j]["eng"], ops[k]["eng"]
        if a == b and a in ("pe", "pool"):
            return 0.0
        return ops[j]["lat"] + (LAT_SAME if a == b else LAT_X)
    pri = [0.0] * n
    for k in range(n - 1, -1, -1):
        pri[k] = ops[k]["cost"] + max([edge(k, s) + pri[s] for s in succ[k]] + [ops[k]["lat"]])
    for (a, e, f) in lead:
        for k in range(a, e):
            pri[k] += f
    for k in range(3):
        pri[k] += 1e6 - k
    for (a, e) in steps:
        names = {}
        for k in range(a, e):
            nm, c0 = ops[k]["w"][0], ops[k]["w"][1]
            nm = "%s.%d" % ({"SF": "SR"}.get(nm, nm[:2] if nm[:2] in ("AW", "SR", "SA") else nm), c0)
            names[nm] = names.get(nm, 0) + 1
            ops[k]["key"] = nm + "abcdefghijklmnop"[names[nm] - 1]
    for k, o in enumerate(ops):
        o["pri"] = pri[k]
        o["first"] = 1e6 - k if k < 3 else 0.0
        o["succ"] = [(s, edge(k, s)) for s in succ[k]]
    order = arrange(ops)

    pos = {k: i for i, k in enumerate(order)}
    need = set()
    seen = {}
    waits = {}
    for k in order:
        e = ops[k]["eng"]
        w = []
        if e != "arr":
            best = {}
            for j in ops[k]["deps"]:
                o = ops[j]
                if o["sem"] == "remote" or (o["eng"] == e and e in ("pe", "pool")):
                    continue
                if o["sem"] is not None:
                    if (e, j) not in seen:
                        seen[(e, j)] = 1
                        w.append(j)
                elif pos[j] > seen.get((e, o["eng"]), -1) and pos[j] > best.get(o["eng"], (-1, 0))[0]:
                    best[o["eng"]] = (pos[j], j)
            for f, (p, j) in best.items():
                seen[(e, f)] = p
                need.add(j)
                w.append(j)
        waits[k] = w
    count = {}
    val = {}
    for k in order:
        if k in need:
            count[ops[k]["eng"]] = count.get(ops[k]["eng"], 0) + 1
            val[k] = count[ops[k]["eng"]]
    for k in order:
        o = ops[k]
        if o["eng"] == "arr":
            continue
        for j in waits[k]:
            if ops[j]["sem"] is not None:
                Q[o["eng"]].wait_ge(T.sem[ops[j]["sem"]], ops[j]["cnt"])
            else:
                Q[o["eng"]].wait_ge(T.sem["c_" + ops[j]["eng"]], val[j])
        ins = o["fn"]()
        if k in need:
            ins.then_inc(T.sem["c_" + o["eng"]], 1)
    g.wait_ge(T.sem.sent, 4 * TS * nen)
    for o in ops:
        if o["sem"] is not None and o["sem"].startswith("o_"):
            g.wait_ge(T.sem[o["sem"]], o["cnt"])
    return ops, order
